import numpy as np
import ml_dtypes


def mxq(x, axis, fmt="e4m3"):
    dtype, down = {"e4m3": (ml_dtypes.float8_e4m3fn, 7), "e5m2": (ml_dtypes.float8_e5m2, 14)}[fmt]
    v = np.moveaxis(np.asarray(x, np.float32).astype(ml_dtypes.bfloat16).astype(np.float64), axis, -1)
    blocks = v.reshape(v.shape[:-1] + (-1, 32))
    amax = np.abs(blocks).max(-1, keepdims=True)
    byte = np.maximum(np.where(amax > 0, np.frexp(amax)[1] - 1 + 127, 0) - down, 1)
    scale = np.exp2(byte - 127.0)
    codes = (blocks / scale).astype(np.float32).astype(dtype).astype(np.float64)
    return np.moveaxis((codes * scale).reshape(v.shape), -1, axis)


WIDE = False


def mx_kscale(k):
    if not WIDE:
        return np.ones(k)
    levels = np.array([10, -10, 5, -5, 0])
    if k % 512:
        return np.exp2(np.random.permutation(np.resize(levels, k // 32))).repeat(32)
    a = np.empty((k // 512, 16))
    for p in range(k // 512):
        a[p, :8] = np.random.permutation(np.resize(levels, 8))
        for g in range(8):
            far = levels[np.abs(levels - a[p, g]) >= 10]
            a[p, g + 8] = far[np.random.randint(len(far))]
    return np.exp2(a.ravel()).repeat(32)


BF16 = ml_dtypes.bfloat16


def bf(x):
    return np.asarray(x, np.float32).astype(BF16)


def f64(x):
    return np.asarray(x).astype(np.float64)


E2M1 = np.array([0.0, 0.5, 1.0, 1.5, 2.0, 3.0, 4.0, 6.0, -0.0, -0.5, -1.0, -1.5, -2.0, -3.0, -4.0, -6.0])


def pack_weight(w, fmt):
    k, n = w.shape
    w = f64(bf(w)).reshape(k // 32, 32, n)
    amax = np.abs(w).max(1)
    if fmt == "e4m3":
        byte = np.frexp(amax)[1] - 1 + 127 - 7
    else:
        mant, ex = np.frexp(amax / 6.0)
        byte = np.where(mant > 0.5, ex, ex - 1) + 127
    byte = np.clip(np.where(amax > 0, byte, 1), 1, 254)
    scaled = (w * np.exp2(127.0 - byte)[:, None, :]).reshape(k, n).astype(np.float32)
    by_word = np.ascontiguousarray(scaled.reshape(k // 512, 128, 4, n).transpose(0, 1, 3, 2))
    if fmt == "e4m3":
        words = by_word.astype(ml_dtypes.float8_e4m3fn).view(np.uint8)
    else:
        c = by_word.astype(ml_dtypes.float4_e2m1fn).view(np.uint8) & 0xF
        words = c[..., 0::2] | (c[..., 1::2] << 4)
    return np.ascontiguousarray(words), np.ascontiguousarray(byte.astype(np.uint8).reshape(k // 512, 16, n))


def unpack_weight(words, scales, fmt):
    g, p, n, _ = words.shape
    if fmt == "e4m3":
        vals = np.ascontiguousarray(words).view(ml_dtypes.float8_e4m3fn).astype(np.float64)
    else:
        nib = np.empty((g, p, n, 4), np.uint8)
        nib[..., 0::2] = words & 0xF
        nib[..., 1::2] = words >> 4
        vals = E2M1[nib]
    vals = vals * np.repeat(np.exp2(scales.astype(np.float64) - 127.0), 8, axis=1)[..., None]
    return vals.transpose(0, 1, 3, 2).reshape(g * 512, n)
def pack4(w):
    words, scales = pack_weight(w, "e2m1")
    return words.reshape(words.shape[0], 128, -1), scales


def unpack4(words, scales):
    return unpack_weight(words.reshape(words.shape[0], 128, -1, 2), scales, "e2m1")


M, K, R, N = 1024, 1024, 512, 1024


def setup_inputs():
    s = mx_kscale(K)
    t = mx_kscale(R)
    sym = np.random.randint(0, 4, (K, M)) - 1.5
    dig = np.random.standard_normal((K, 2 * R)) / np.sqrt(K)
    theta = np.random.uniform(-np.pi, np.pi, (R, N))
    gain = 1 + 0.1 * np.random.standard_normal(2 * R)
    sym_words, sym_scales = pack4(sym * s[:, None])
    dig_words, dig_scales = pack4(dig / s[:, None])
    return {"sym_words": sym_words, "sym_scales": sym_scales,
            "dig_words": dig_words, "dig_scales": dig_scales,
            "gain": bf(gain * np.concatenate([t, t])),
            "cosw": bf(np.cos(theta) / np.sqrt(R) / t[:, None]),
            "sinw": bf(np.sin(theta) / np.sqrt(R) / t[:, None])}


def reference(sym_words, sym_scales, dig_words, dig_scales, gain, cosw, sinw):
    x = unpack4(sym_words, sym_scales)
    d = unpack4(dig_words, dig_scales)
    h = x.T @ d
    h = np.tanh(h) * f64(gain)
    u = mxq(h[:, :R], 1, "e4m3")
    v = mxq(h[:, R:], 1, "e4m3")
    c = mxq(f64(cosw), 0, "e4m3")
    b = mxq(f64(sinw), 0, "e4m3")
    y_re = (u @ c) - (v @ b)
    y_im = (u @ b) + (v @ c)
    return y_re, y_im

@@ -1,0 +1,277 @@
+from contextlib import ExitStack
+
+import concourse.mybir as mybir
+from concourse.masks import make_identity
+
+SAMPLES, STREAMS, CHAINS, ANTENNAS = 1024, 1024, 512, 1024
+FLOPS = 2 * SAMPLES * STREAMS * 2 * CHAINS + 4 * 2 * SAMPLES * CHAINS * ANTENNAS
+
+F32 = mybir.dt.float32
+BF16 = mybir.dt.bfloat16
+I32 = mybir.dt.int32
+U32 = mybir.dt.uint32
+U8 = mybir.dt.uint8
+FP4X4 = mybir.dt.float4_e2m1fn_x4
+FP8X4 = mybir.dt.float8_e4m3fn_x4
+TANH = mybir.ActivationFunctionType.Tanh
+MULT = mybir.AluOpType.mult
+
+P = 128
+SLOTS = 4
+GROUPS = STREAMS // 512
+HALF = 512
+PHASES = 2
+U, V = 0, 1
+RE, IM = 0, 1
+BLOCKS = SAMPLES // P
+WARM_UP = 10
+
+
+def tile_hybrid_beamforming_precoder_s4_kernel(
+    tc, sym_words, sym_scales, dig_words, dig_scales, gain, cosw, sinw, out_0, out_1
+):
+    nc = tc.nc
+    with ExitStack() as ctx:
+        keep = ctx.enter_context(tc.tile_pool(name="keep", bufs=1))
+        rows_pool = ctx.enter_context(tc.tile_pool(name="rows", bufs=PHASES * BLOCKS))
+        psum = ctx.enter_context(tc.psum_pool(name="psum", bufs=8))
+
+        def tile(shape, dtype, name):
+            return keep.tile(shape, dtype, name=name, align_bytes=64)
+
+        x_codes = {h: tile([P, GROUPS, 2 * HALF], U8, "x_codes%d" % h) for h in range(2)}
+        x_scales = tile([P, GROUPS, SAMPLES], U8, "x_scales")
+        d_raw = tile([P, GROUPS, 2 * PHASES * CHAINS], U8, "d_raw")
+        d_scales_raw = tile([P, GROUPS, PHASES * CHAINS], U8, "d_scales_raw")
+        d_codes = {s: tile([P, GROUPS, SLOTS, 2 * P], U8, "d_codes%d" % s) for s in (U, V)}
+        d_scales = tile([P, SLOTS, GROUPS, PHASES, P], U8, "d_scales")
+        gain_rows = tile([P, PHASES, P], BF16, "gain_rows")
+        identity = tile([P, P], BF16, "identity")
+        gain_cols = tile([P, PHASES * SLOTS], F32, "gain_cols")
+        dummy = tile([P, 1], F32, "dummy")
+
+        w_raw = {(k, nh): tile([P, SLOTS, HALF], BF16, "raw_%s%d" % (k, nh)) for k in ("c", "b") for nh in range(2)}
+        w_packed = {k: tile([P, SLOTS * ANTENNAS], BF16, "packed_" + k) for k in ("c", "b", "nb")}
+        w_codes = {k: tile([P, ANTENNAS], U32, "codes_" + k) for k in ("c", "b", "nb")}
+        w_scales = {k: tile([P, ANTENNAS], U8, "scales_" + k) for k in ("c", "b", "nb")}
+
+        tanh_h = {(s, h): tile([P, SLOTS, HALF], F32, "tanh_%d%d" % (s, h)) for s in (U, V) for h in range(2)}
+        rounded = {(s, q): tile([P, SLOTS, 256], BF16, "rounded_%d%d" % (s, q)) for s in (U, V) for q in range(4)}
+        uv_packed = {(s, m): tile([P, SLOTS * P], BF16, "uv_packed_%d%d" % (s, m)) for s in (U, V) for m in range(BLOCKS)}
+        uv_codes = {(s, m): tile([P, P], U32, "uv_codes_%d%d" % (s, m)) for s in (U, V) for m in range(BLOCKS)}
+        uv_scales = {(s, m): tile([P, P], U8, "uv_scales_%d%d" % (s, m)) for s in (U, V) for m in range(BLOCKS)}
+
+        ctx.enter_context(tc.manual_schedule())
+
+        def words(t, pattern):
+            return t[:].rearrange(pattern).bitcast(I32)
+
+        nc.vector.memset(words(d_scales_raw, "p g n -> p (g n)"), 0)
+        nc.vector.memset(words(x_scales, "p g n -> p (g n)"), 0)
+        nc.vector.memset(gain_rows[:], 0.0)
+        nc.vector.memset(w_scales["c"][:].bitcast(I32), 0)
+        nc.vector.memset(x_codes[1][:, 0, :].bitcast(I32), 0)
+        nc.vector.memset(dummy[:], 0.0)
+
+        warm_bank = psum.tile([P, HALF], F32, name="bank")
+        for unused in range(WARM_UP):
+            nc.tensor.matmul_mx(
+                out=warm_bank[:],
+                lhsT=x_codes[1][:, 0, 0 : 2 * P].bitcast(FP4X4),
+                lhsT_scale=w_scales["c"][:, 0:P],
+                rhs=x_codes[1][:, 0, :].bitcast(FP4X4),
+                rhs_scale=w_scales["c"][:, HALF : 2 * HALF],
+                start=True,
+                stop=True,
+            )
+
+        def load_x(engine, h):
+            by_partition = sym_words.rearrange("g p x -> p g x")
+            engine.dma_start(
+                out=x_codes[h][:].bitcast(I32),
+                in_=by_partition[:, :, 2 * HALF * h : 2 * HALF * (h + 1)].bitcast(I32),
+            )
+
+        def load_scales(engine, dst, src):
+            for j in range(4):
+                engine.dma_start(
+                    out=dst[32 * j : 32 * j + 4, :, :].bitcast(I32),
+                    in_=src[:, 4 * j : 4 * j + 4, :].rearrange("g r n -> r g n").bitcast(I32),
+                )
+
+        def load_w(engine, k, nh):
+            w = (cosw if k == "c" else sinw).rearrange("(b t i) n -> t b i n", t=SLOTS, i=4)
+            for t in range(SLOTS):
+                engine.dma_start(out=w_raw[k, nh][:, t, :], in_=w[t][:, :, HALF * nh : HALF * (nh + 1)])
+
+        nc.gpsimd.dma_start(out=d_raw[:].bitcast(I32), in_=dig_words.rearrange("g p x -> p g x").bitcast(I32))
+        load_x(nc.gpsimd, 0)
+        load_scales(nc.scalar, d_scales_raw, dig_scales)
+        load_scales(nc.sync, x_scales, sym_scales)
+        nc.gpsimd.dma_start(
+            out=gain_rows[0:SLOTS, :, :].rearrange("t s (b i) -> t (s b) i", i=4),
+            in_=gain.rearrange("(c t i) -> t c i", t=SLOTS, i=4),
+        )
+        make_identity(nc, identity[:])
+        nc.scalar.activation(out=dummy[:], in_=dummy[:], func=TANH)
+        load_w(nc.sync, "c", 0)
+        load_w(nc.sync, "b", 0)
+        load_x(nc.sync, 1)
+        load_w(nc.sync, "c", 1)
+        load_w(nc.sync, "b", 1)
+
+        nc.vector.tensor_copy(
+            out=words(d_scales, "p t g s n -> p (t g s n)").rearrange("p (t c) -> p t c", t=SLOTS),
+            in_=words(d_scales_raw, "p g n -> p (g n)").rearrange("p (c t) -> p t c", t=SLOTS),
+        )
+        d_src = words(d_raw, "p g x -> p (g x)").rearrange("p (g s c t w) -> p g s t c w", g=GROUPS, s=PHASES, t=SLOTS, w=2)
+        for s in (U, V):
+            d_dst = words(d_codes[s], "p g t n -> p (g t n)").rearrange("p (g t c w) -> p g t c w", g=GROUPS, t=SLOTS, w=2)
+            for g in range(GROUPS):
+                nc.vector.tensor_copy(out=d_dst[:, g], in_=d_src[:, g, s])
+
+        def chains(s, t, h):
+            bank = psum.tile([P, HALF], F32, name="bank")
+            for g in range(GROUPS):
+                nc.tensor.matmul_mx(
+                    out=bank[:],
+                    lhsT=d_codes[s][:, g, t, :].bitcast(FP4X4),
+                    lhsT_scale=d_scales[:, t, g, s, :],
+                    rhs=x_codes[h][:, g, :].bitcast(FP4X4),
+                    rhs_scale=x_scales[:, g, HALF * h : HALF * (h + 1)],
+                    start=(g == 0),
+                    stop=(g == GROUPS - 1),
+                )
+            nc.scalar.activation(out=tanh_h[s, h][:, t, :], in_=bank[:], func=TANH)
+
+        def packed_half(k, nh):
+            return w_packed[k][:, SLOTS * HALF * nh : SLOTS * HALF * (nh + 1)]
+
+        def pack_w(copy, k, nh):
+            copy(
+                out=packed_half(k, nh).rearrange("p (n t) -> p n t", t=SLOTS),
+                in_=w_raw[k, nh][:].rearrange("p t n -> p n t"),
+            )
+
+        def negate_b(nh):
+            nc.vector.tensor_scalar(out=packed_half("nb", nh), in0=packed_half("b", nh), scalar1=-1.0, scalar2=None, op0=MULT)
+
+        def quantise_w(k, nh):
+            n = slice(HALF * nh, HALF * (nh + 1))
+            nc.vector.quantize_mx(out=w_codes[k][:, n].bitcast(FP8X4), scales=w_scales[k][:, n], in_=packed_half(k, nh))
+
+        def times_gain(s, q):
+            n = 256 * (q % 2)
+            for t in range(SLOTS):
+                nc.vector.tensor_scalar(
+                    out=rounded[s, q][:, t, :],
+                    in0=tanh_h[s, q // 2][:, t, n : n + 256],
+                    scalar1=gain_cols[:, SLOTS * s + t : SLOTS * s + t + 1],
+                    scalar2=None,
+                    op0=MULT,
+                )
+
+        def pack_uv(s, m):
+            n = P * (m % 2)
+            nc.vector.tensor_copy(
+                out=uv_packed[s, m][:].rearrange("p (n t) -> p n t", t=SLOTS),
+                in_=rounded[s, m // 2][:, :, n : n + P].rearrange("p t n -> p n t"),
+            )
+
+        def quantise_uv(s, m):
+            nc.vector.quantize_mx(out=uv_codes[s, m][:].bitcast(FP8X4), scales=uv_scales[s, m][:], in_=uv_packed[s, m][:])
+
+        def block(m):
+            if m % 2 == 0:
+                times_gain(U, m // 2)
+                times_gain(V, m // 2)
+            pack_uv(U, m)
+            pack_uv(V, m)
+            quantise_uv(U, m)
+            quantise_uv(V, m)
+
+        row_tiles = {}
+
+        def product(m, part, nh, copy):
+            bank = psum.tile([P, HALF], F32, name="bank")
+            n = slice(HALF * nh, HALF * (nh + 1))
+            for s in (U, V):
+                k = (("c", "nb"), ("b", "c"))[part][s]
+                nc.tensor.matmul_mx(
+                    out=bank[:],
+                    lhsT=uv_codes[s, m][:].bitcast(FP8X4),
+                    lhsT_scale=uv_scales[s, m][:],
+                    rhs=w_codes[k][:, n].bitcast(FP8X4),
+                    rhs_scale=w_scales[k][:, n],
+                    start=(s == U),
+                    stop=(s == V),
+                )
+            if nh == 0:
+                row_tiles[m, part] = rows_pool.tile([P, ANTENNAS], F32, name="row")
+            copy(out=row_tiles[m, part][:, n], in_=bank[:])
+
+        def store(m, part, first, last):
+            out = (out_0, out_1)[part]
+            nc.sync.dma_start(out=out[P * m : P * (m + 1), first:last], in_=row_tiles[m, part][:, first:last])
+
+        def half_rows(m, part, nh, copy=nc.scalar.copy):
+            product(m, part, nh, copy)
+            store(m, part, HALF * nh, HALF * (nh + 1))
+
+        for s in (U, V):
+            for t in range(SLOTS):
+                chains(s, t, 0)
+        gain_bank = psum.tile([P, PHASES, P], BF16, name="bank")
+        for s in (U, V):
+            nc.tensor.transpose(gain_bank[:, s, :], gain_rows[:, s, :], identity[:])
+        pack_w(nc.scalar.copy, "c", 1)
+        for t in range(SLOTS):
+            chains(U, t, 1)
+
+        pack_w(nc.vector.tensor_copy, "c", 0)
+        pack_w(nc.vector.tensor_copy, "b", 0)
+        quantise_w("c", 0)
+        nc.vector.tensor_copy(out=gain_cols[:].rearrange("p (s t) -> p s t", s=PHASES), in_=gain_bank[:, :, 0:SLOTS])
+        quantise_w("b", 0)
+        block(0)
+        half_rows(0, IM, 0)
+        negate_b(0)
+        pack_uv(U, 1)
+        quantise_w("nb", 0)
+        half_rows(0, RE, 0)
+        pack_uv(V, 1)
+        quantise_uv(U, 1)
+        quantise_uv(V, 1)
+        half_rows(1, IM, 0)
+        half_rows(1, RE, 0)
+        for t in range(SLOTS):
+            chains(V, t, 1)
+
+        pack_w(nc.vector.tensor_copy, "b", 1)
+        quantise_w("c", 1)
+        quantise_w("b", 1)
+        for m in (0, 1):
+            half_rows(m, IM, 1)
+        negate_b(1)
+        times_gain(U, 1)
+        quantise_w("nb", 1)
+        for m in (0, 1):
+            half_rows(m, RE, 1)
+        times_gain(V, 1)
+        pack_uv(U, 2)
+        pack_uv(V, 2)
+        quantise_uv(U, 2)
+        quantise_uv(V, 2)
+        for m in range(3, BLOCKS):
+            block(m)
+
+        for m in range(2, BLOCKS):
+            first_copy = nc.scalar.copy if m < 6 else nc.vector.tensor_copy
+            for part in (IM, RE):
+                if (m, part) == (BLOCKS - 1, RE):
+                    half_rows(m, part, 0, first_copy)
+                    half_rows(m, part, 1)
+                else:
+                    product(m, part, 0, first_copy)
+                    product(m, part, 1, nc.scalar.copy)
+                    store(m, part, 0, ANTENNAS)

@@ -1,7 +1,6 @@
 from contextlib import ExitStack
 
 import concourse.mybir as mybir
-from concourse.masks import make_identity
 
 SAMPLES, STREAMS, CHAINS, ANTENNAS = 1024, 1024, 512, 1024
 FLOPS = 2 * SAMPLES * STREAMS * 2 * CHAINS + 4 * 2 * SAMPLES * CHAINS * ANTENNAS
@@ -18,13 +17,14 @@ MULT = mybir.AluOpType.mult
 
 P = 128
 SLOTS = 4
+RUN = 8
 GROUPS = STREAMS // 512
 HALF = 512
+QUARTER = 256
 PHASES = 2
 U, V = 0, 1
 RE, IM = 0, 1
 BLOCKS = SAMPLES // P
-WARM_UP = 10
 
 
 def tile_hybrid_beamforming_precoder_s4_kernel(
@@ -33,33 +33,33 @@ def tile_hybrid_beamforming_precoder_s4_kernel(
     nc = tc.nc
     with ExitStack() as ctx:
         keep = ctx.enter_context(tc.tile_pool(name="keep", bufs=1))
-        rows_pool = ctx.enter_context(tc.tile_pool(name="rows", bufs=PHASES * BLOCKS))
         psum = ctx.enter_context(tc.psum_pool(name="psum", bufs=8))
 
         def tile(shape, dtype, name):
-            return keep.tile(shape, dtype, name=name, align_bytes=64)
+            return keep.tile(shape, dtype, name=name, align_bytes=256)
 
         x_codes = {h: tile([P, GROUPS, 2 * HALF], U8, "x_codes%d" % h) for h in range(2)}
         x_scales = tile([P, GROUPS, SAMPLES], U8, "x_scales")
-        d_raw = tile([P, GROUPS, 2 * PHASES * CHAINS], U8, "d_raw")
+        d_raw = {s: tile([P, GROUPS, 2 * CHAINS], U8, "d_raw%d" % s) for s in (U, V)}
         d_scales_raw = tile([P, GROUPS, PHASES * CHAINS], U8, "d_scales_raw")
         d_codes = {s: tile([P, GROUPS, SLOTS, 2 * P], U8, "d_codes%d" % s) for s in (U, V)}
-        d_scales = tile([P, SLOTS, GROUPS, PHASES, P], U8, "d_scales")
-        gain_rows = tile([P, PHASES, P], BF16, "gain_rows")
-        identity = tile([P, P], BF16, "identity")
-        gain_cols = tile([P, PHASES * SLOTS], F32, "gain_cols")
-        dummy = tile([P, 1], F32, "dummy")
+        d_scales = {s: tile([P, GROUPS, SLOTS, P], U8, "d_scales%d" % s) for s in (U, V)}
+        gain_rows = tile([P, PHASES * P], BF16, "gain_rows")
+        gain_sorted = tile([P, PHASES * P], BF16, "gain_sorted")
+        gain_turned = tile([P, PHASES * P], BF16, "gain_turned")
+        gain_cols = tile([P, PHASES, SLOTS], F32, "gain_cols")
 
-        w_raw = {(k, nh): tile([P, SLOTS, HALF], BF16, "raw_%s%d" % (k, nh)) for k in ("c", "b") for nh in range(2)}
-        w_packed = {k: tile([P, SLOTS * ANTENNAS], BF16, "packed_" + k) for k in ("c", "b", "nb")}
-        w_codes = {k: tile([P, ANTENNAS], U32, "codes_" + k) for k in ("c", "b", "nb")}
-        w_scales = {k: tile([P, ANTENNAS], U8, "scales_" + k) for k in ("c", "b", "nb")}
+        halves = [(k, nh) for k in ("c", "b", "nb") for nh in range(2)]
+        w_raw = {(k, nh): tile([P, SLOTS, HALF], BF16, "raw_%s%d" % (k, nh)) for k, nh in halves if k != "nb"}
+        w_packed = {(k, nh): tile([P, SLOTS * HALF], BF16, "packed_%s%d" % (k, nh)) for k, nh in halves}
+        w_codes = {(k, nh): tile([P, HALF], U32, "codes_%s%d" % (k, nh)) for k, nh in halves}
+        w_scales = {(k, nh): tile([P, HALF], U8, "scales_%s%d" % (k, nh)) for k, nh in halves}
 
-        tanh_h = {(s, h): tile([P, SLOTS, HALF], F32, "tanh_%d%d" % (s, h)) for s in (U, V) for h in range(2)}
-        rounded = {(s, q): tile([P, SLOTS, 256], BF16, "rounded_%d%d" % (s, q)) for s in (U, V) for q in range(4)}
-        uv_packed = {(s, m): tile([P, SLOTS * P], BF16, "uv_packed_%d%d" % (s, m)) for s in (U, V) for m in range(BLOCKS)}
-        uv_codes = {(s, m): tile([P, P], U32, "uv_codes_%d%d" % (s, m)) for s in (U, V) for m in range(BLOCKS)}
-        uv_scales = {(s, m): tile([P, P], U8, "uv_scales_%d%d" % (s, m)) for s in (U, V) for m in range(BLOCKS)}
+        tanh_h = {(s, q): tile([P, 2, 2 * QUARTER], F32, "tanh_%d%d" % (s, q)) for s in (U, V) for q in range(4)}
+        uv_packed = {m: tile([P, PHASES, SLOTS * P], BF16, "uv_packed%d" % m) for m in range(BLOCKS)}
+        uv_codes = {m: tile([P, PHASES, P], U32, "uv_codes%d" % m) for m in range(BLOCKS)}
+        uv_scales = {m: tile([P, PHASES, P], U8, "uv_scales%d" % m) for m in range(BLOCKS)}
+        rows = {(m, part): tile([P, ANTENNAS], F32, "rows%d%d" % (m, part)) for m in range(BLOCKS) for part in (RE, IM)}
 
         ctx.enter_context(tc.manual_schedule())
 
@@ -69,204 +69,191 @@ def tile_hybrid_beamforming_precoder_s4_kernel(
         nc.vector.memset(words(d_scales_raw, "p g n -> p (g n)"), 0)
         nc.vector.memset(words(x_scales, "p g n -> p (g n)"), 0)
         nc.vector.memset(gain_rows[:], 0.0)
-        nc.vector.memset(w_scales["c"][:].bitcast(I32), 0)
-        nc.vector.memset(x_codes[1][:, 0, :].bitcast(I32), 0)
-        nc.vector.memset(dummy[:], 0.0)
 
-        warm_bank = psum.tile([P, HALF], F32, name="bank")
-        for unused in range(WARM_UP):
-            nc.tensor.matmul_mx(
-                out=warm_bank[:],
-                lhsT=x_codes[1][:, 0, 0 : 2 * P].bitcast(FP4X4),
-                lhsT_scale=w_scales["c"][:, 0:P],
-                rhs=x_codes[1][:, 0, :].bitcast(FP4X4),
-                rhs_scale=w_scales["c"][:, HALF : 2 * HALF],
-                start=True,
-                stop=True,
-            )
-
-        def load_x(engine, h):
-            by_partition = sym_words.rearrange("g p x -> p g x")
+        def load_codes(engine, dst, src, h):
+            by_partition = src.rearrange("g p x -> p g x")
             engine.dma_start(
-                out=x_codes[h][:].bitcast(I32),
+                out=dst[h][:].bitcast(I32),
                 in_=by_partition[:, :, 2 * HALF * h : 2 * HALF * (h + 1)].bitcast(I32),
             )
 
-        def load_scales(engine, dst, src):
-            for j in range(4):
-                engine.dma_start(
-                    out=dst[32 * j : 32 * j + 4, :, :].bitcast(I32),
-                    in_=src[:, 4 * j : 4 * j + 4, :].rearrange("g r n -> r g n").bitcast(I32),
-                )
+        def load_scales(engine, dst, src, j):
+            engine.dma_start(
+                out=dst[32 * j : 32 * j + 4, :, :].bitcast(I32),
+                in_=src[:, 4 * j : 4 * j + 4, :].rearrange("g r n -> r g n").bitcast(I32),
+            )
 
-        def load_w(engine, k, nh):
-            w = (cosw if k == "c" else sinw).rearrange("(b t i) n -> t b i n", t=SLOTS, i=4)
+        def load_w(k, nh):
+            w = (cosw if k == "c" else sinw).rearrange("(q t r) n -> t q r n", t=SLOTS, r=RUN)
             for t in range(SLOTS):
-                engine.dma_start(out=w_raw[k, nh][:, t, :], in_=w[t][:, :, HALF * nh : HALF * (nh + 1)])
+                nc.sync.dma_start(out=w_raw[k, nh][:, t, :], in_=w[t][:, :, HALF * nh : HALF * (nh + 1)])
 
-        nc.gpsimd.dma_start(out=d_raw[:].bitcast(I32), in_=dig_words.rearrange("g p x -> p g x").bitcast(I32))
-        load_x(nc.gpsimd, 0)
-        load_scales(nc.scalar, d_scales_raw, dig_scales)
-        load_scales(nc.sync, x_scales, sym_scales)
+        load_codes(nc.sync, d_raw, dig_words, U)
+        load_codes(nc.gpsimd, x_codes, sym_words, 0)
+        for j in range(4):
+            load_scales(nc.scalar, d_scales_raw, dig_scales, j)
+        for j in range(4):
+            load_scales(nc.sync if j < 3 else nc.gpsimd, x_scales, sym_scales, j)
         nc.gpsimd.dma_start(
-            out=gain_rows[0:SLOTS, :, :].rearrange("t s (b i) -> t (s b) i", i=4),
-            in_=gain.rearrange("(c t i) -> t c i", t=SLOTS, i=4),
+            out=gain_rows[0:P:32, :].rearrange("j (s n) -> j s n", s=PHASES),
+            in_=gain.rearrange("(s j n) -> j s n", s=PHASES, j=4),
         )
-        make_identity(nc, identity[:])
-        nc.scalar.activation(out=dummy[:], in_=dummy[:], func=TANH)
-        load_w(nc.sync, "c", 0)
-        load_w(nc.sync, "b", 0)
-        load_x(nc.sync, 1)
-        load_w(nc.sync, "c", 1)
-        load_w(nc.sync, "b", 1)
+        load_w("c", 0)
+        load_codes(nc.sync, d_raw, dig_words, V)
+        load_w("b", 0)
+        load_codes(nc.sync, x_codes, sym_words, 1)
+        load_w("c", 1)
+        load_w("b", 1)
 
-        nc.vector.tensor_copy(
-            out=words(d_scales, "p t g s n -> p (t g s n)").rearrange("p (t c) -> p t c", t=SLOTS),
-            in_=words(d_scales_raw, "p g n -> p (g n)").rearrange("p (c t) -> p t c", t=SLOTS),
-        )
-        d_src = words(d_raw, "p g x -> p (g x)").rearrange("p (g s c t w) -> p g s t c w", g=GROUPS, s=PHASES, t=SLOTS, w=2)
-        for s in (U, V):
-            d_dst = words(d_codes[s], "p g t n -> p (g t n)").rearrange("p (g t c w) -> p g t c w", g=GROUPS, t=SLOTS, w=2)
-            for g in range(GROUPS):
-                nc.vector.tensor_copy(out=d_dst[:, g], in_=d_src[:, g, s])
+        def sort_d(s):
+            nc.vector.tensor_copy(
+                out=words(d_scales[s], "p g t n -> p (g t n)").rearrange("p (g t q w) -> p g t q w", g=GROUPS, t=SLOTS, w=2),
+                in_=words(d_scales_raw, "p g n -> p (g n)").rearrange(
+                    "p (g s q t w) -> p s g t q w", g=GROUPS, s=PHASES, t=SLOTS, w=2
+                )[:, s],
+            )
+            nc.vector.tensor_copy(
+                out=words(d_codes[s], "p g t n -> p (g t n)").rearrange("p (g t q w) -> p g t q w", g=GROUPS, t=SLOTS, w=4),
+                in_=words(d_raw[s], "p g x -> p (g x)").rearrange("p (g q t w) -> p g t q w", g=GROUPS, t=SLOTS, w=4),
+            )
 
-        def chains(s, t, h):
-            bank = psum.tile([P, HALF], F32, name="bank")
-            for g in range(GROUPS):
-                nc.tensor.matmul_mx(
-                    out=bank[:],
-                    lhsT=d_codes[s][:, g, t, :].bitcast(FP4X4),
-                    lhsT_scale=d_scales[:, t, g, s, :],
-                    rhs=x_codes[h][:, g, :].bitcast(FP4X4),
-                    rhs_scale=x_scales[:, g, HALF * h : HALF * (h + 1)],
-                    start=(g == 0),
-                    stop=(g == GROUPS - 1),
+        def sort_gain():
+            nc.vector.tensor_copy(
+                out=gain_sorted[:].rearrange("p (s t q r) -> p s t q r", s=PHASES, t=SLOTS, r=RUN),
+                in_=gain_rows[:].rearrange("p (s q t r) -> p s t q r", s=PHASES, t=SLOTS, r=RUN),
+            )
+
+        def turn_gain():
+            nc.vector.transpose(out=gain_turned[:], in_=gain_sorted[:])
+
+        def gather_gain():
+            nc.vector.tensor_copy(out=gain_cols[:].rearrange("p s t -> p (s t)"), in_=gain_turned[:, 0 : PHASES * P : 32])
+
+        def chains(s, q):
+            n = QUARTER * (q % 2)
+            for pair in range(2):
+                bank = psum.tile([P, HALF], F32, name="bank")
+                for j in range(2):
+                    for g in range(GROUPS):
+                        nc.tensor.matmul_mx(
+                            out=bank[:, QUARTER * j : QUARTER * (j + 1)],
+                            lhsT=d_codes[s][:, g, 2 * pair + j, :].bitcast(FP4X4),
+                            lhsT_scale=d_scales[s][:, g, 2 * pair + j, :],
+                            rhs=x_codes[q // 2][:, g, 2 * n : 2 * (n + QUARTER)].bitcast(FP4X4),
+                            rhs_scale=x_scales[:, g, QUARTER * q : QUARTER * (q + 1)],
+                            start=(g == 0),
+                            stop=(g == GROUPS - 1),
+                        )
+                nc.scalar.activation(
+                    out=tanh_h[s, q][:, pair, :].rearrange("p (n j) -> p n j", j=2),
+                    in_=bank[:].rearrange("p (j n) -> p n j", j=2),
+                    func=TANH,
                 )
-            nc.scalar.activation(out=tanh_h[s, h][:, t, :], in_=bank[:], func=TANH)
-
-        def packed_half(k, nh):
-            return w_packed[k][:, SLOTS * HALF * nh : SLOTS * HALF * (nh + 1)]
 
         def pack_w(copy, k, nh):
             copy(
-                out=packed_half(k, nh).rearrange("p (n t) -> p n t", t=SLOTS),
-                in_=w_raw[k, nh][:].rearrange("p t n -> p n t"),
+                out=w_packed[k, nh][:].rearrange("p (c i t) -> p c t i", t=SLOTS, i=4),
+                in_=w_raw[k, nh][:].rearrange("p t (c i) -> p c t i", i=4),
             )
 
         def negate_b(nh):
-            nc.vector.tensor_scalar(out=packed_half("nb", nh), in0=packed_half("b", nh), scalar1=-1.0, scalar2=None, op0=MULT)
+            nc.vector.tensor_scalar(out=w_packed["nb", nh][:], in0=w_packed["b", nh][:], scalar1=-1.0, scalar2=None, op0=MULT)
 
         def quantise_w(k, nh):
-            n = slice(HALF * nh, HALF * (nh + 1))
-            nc.vector.quantize_mx(out=w_codes[k][:, n].bitcast(FP8X4), scales=w_scales[k][:, n], in_=packed_half(k, nh))
+            nc.vector.quantize_mx(out=w_codes[k, nh][:].bitcast(FP8X4), scales=w_scales[k, nh][:], in_=w_packed[k, nh][:])
 
-        def times_gain(s, q):
-            n = 256 * (q % 2)
-            for t in range(SLOTS):
-                nc.vector.tensor_scalar(
-                    out=rounded[s, q][:, t, :],
-                    in0=tanh_h[s, q // 2][:, t, n : n + 256],
-                    scalar1=gain_cols[:, SLOTS * s + t : SLOTS * s + t + 1],
-                    scalar2=None,
-                    op0=MULT,
-                )
-
-        def pack_uv(s, m):
+        def times_gain(s, m):
             n = P * (m % 2)
-            nc.vector.tensor_copy(
-                out=uv_packed[s, m][:].rearrange("p (n t) -> p n t", t=SLOTS),
-                in_=rounded[s, m // 2][:, :, n : n + P].rearrange("p t n -> p n t"),
+            nc.vector.tensor_tensor(
+                out=uv_packed[m][:, s, :].rearrange("p (n u j) -> p n u j", u=2, j=2),
+                in0=tanh_h[s, m // 2][:].rearrange("p u (n j) -> p n u j", j=2)[:, n : n + P],
+                in1=gain_cols[:, s, :].rearrange("p (u j) -> p u j", j=2).unsqueeze(1).to_broadcast([P, P, 2, 2]),
+                op=MULT,
             )
 
-        def quantise_uv(s, m):
-            nc.vector.quantize_mx(out=uv_codes[s, m][:].bitcast(FP8X4), scales=uv_scales[s, m][:], in_=uv_packed[s, m][:])
-
-        def block(m):
-            if m % 2 == 0:
-                times_gain(U, m // 2)
-                times_gain(V, m // 2)
-            pack_uv(U, m)
-            pack_uv(V, m)
-            quantise_uv(U, m)
-            quantise_uv(V, m)
-
-        row_tiles = {}
+        def quantise_uv(m):
+            nc.vector.quantize_mx(
+                out=uv_codes[m][:].rearrange("p s n -> p (s n)").bitcast(FP8X4),
+                scales=uv_scales[m][:].rearrange("p s n -> p (s n)"),
+                in_=uv_packed[m][:].rearrange("p s n -> p (s n)"),
+            )
 
         def product(m, part, nh, copy):
             bank = psum.tile([P, HALF], F32, name="bank")
-            n = slice(HALF * nh, HALF * (nh + 1))
             for s in (U, V):
                 k = (("c", "nb"), ("b", "c"))[part][s]
                 nc.tensor.matmul_mx(
                     out=bank[:],
-                    lhsT=uv_codes[s, m][:].bitcast(FP8X4),
-                    lhsT_scale=uv_scales[s, m][:],
-                    rhs=w_codes[k][:, n].bitcast(FP8X4),
-                    rhs_scale=w_scales[k][:, n],
+                    lhsT=uv_codes[m][:, s, :].bitcast(FP8X4),
+                    lhsT_scale=uv_scales[m][:, s, :],
+                    rhs=w_codes[k, nh][:].bitcast(FP8X4),
+                    rhs_scale=w_scales[k, nh][:],
                     start=(s == U),
                     stop=(s == V),
                 )
-            if nh == 0:
-                row_tiles[m, part] = rows_pool.tile([P, ANTENNAS], F32, name="row")
-            copy(out=row_tiles[m, part][:, n], in_=bank[:])
+            copy(out=rows[m, part][:, HALF * nh : HALF * (nh + 1)], in_=bank[:])
 
         def store(m, part, first, last):
             out = (out_0, out_1)[part]
-            nc.sync.dma_start(out=out[P * m : P * (m + 1), first:last], in_=row_tiles[m, part][:, first:last])
+            nc.sync.dma_start(out=out[P * m : P * (m + 1), first:last], in_=rows[m, part][:, first:last])
 
         def half_rows(m, part, nh, copy=nc.scalar.copy):
             product(m, part, nh, copy)
             store(m, part, HALF * nh, HALF * (nh + 1))
 
-        for s in (U, V):
-            for t in range(SLOTS):
-                chains(s, t, 0)
-        gain_bank = psum.tile([P, PHASES, P], BF16, name="bank")
-        for s in (U, V):
-            nc.tensor.transpose(gain_bank[:, s, :], gain_rows[:, s, :], identity[:])
-        pack_w(nc.scalar.copy, "c", 1)
-        for t in range(SLOTS):
-            chains(U, t, 1)
-
+        sort_d(U)
+        chains(U, 0)
+        chains(U, 1)
+        sort_gain()
         pack_w(nc.vector.tensor_copy, "c", 0)
-        pack_w(nc.vector.tensor_copy, "b", 0)
+        sort_d(V)
+        chains(V, 0)
+        chains(V, 1)
+        turn_gain()
         quantise_w("c", 0)
-        nc.vector.tensor_copy(out=gain_cols[:].rearrange("p (s t) -> p s t", s=PHASES), in_=gain_bank[:, :, 0:SLOTS])
+        gather_gain()
+        pack_w(nc.vector.tensor_copy, "b", 0)
+        times_gain(U, 0)
         quantise_w("b", 0)
-        block(0)
-        half_rows(0, IM, 0)
+        times_gain(V, 0)
         negate_b(0)
-        pack_uv(U, 1)
+        quantise_uv(0)
         quantise_w("nb", 0)
+        chains(U, 2)
+        pack_w(nc.scalar.copy, "c", 1)
+        chains(V, 2)
+
+        half_rows(0, IM, 0)
         half_rows(0, RE, 0)
-        pack_uv(V, 1)
-        quantise_uv(U, 1)
-        quantise_uv(V, 1)
+        times_gain(U, 1)
+        times_gain(V, 1)
+        quantise_w("c", 1)
+        quantise_uv(1)
+        chains(U, 3)
         half_rows(1, IM, 0)
         half_rows(1, RE, 0)
-        for t in range(SLOTS):
-            chains(V, t, 1)
+        chains(V, 3)
 
         pack_w(nc.vector.tensor_copy, "b", 1)
-        quantise_w("c", 1)
+        times_gain(U, 2)
         quantise_w("b", 1)
         for m in (0, 1):
             half_rows(m, IM, 1)
         negate_b(1)
-        times_gain(U, 1)
+        times_gain(V, 2)
         quantise_w("nb", 1)
         for m in (0, 1):
             half_rows(m, RE, 1)
-        times_gain(V, 1)
-        pack_uv(U, 2)
-        pack_uv(V, 2)
-        quantise_uv(U, 2)
-        quantise_uv(V, 2)
+        quantise_uv(2)
+        times_gain(U, 3)
         for m in range(3, BLOCKS):
-            block(m)
+            times_gain(V, m)
+            if m + 1 < BLOCKS:
+                times_gain(U, m + 1)
+            quantise_uv(m)
 
         for m in range(2, BLOCKS):
-            first_copy = nc.scalar.copy if m < 6 else nc.vector.tensor_copy
+            first_copy = nc.scalar.copy if m < 5 else nc.vector.tensor_copy
             for part in (IM, RE):
                 if (m, part) == (BLOCKS - 1, RE):
                     half_rows(m, part, 0, first_copy)

@@ -25,6 +25,7 @@ PHASES = 2
 U, V = 0, 1
 RE, IM = 0, 1
 BLOCKS = SAMPLES // P
+EARLY = 4
 
 
 def tile_hybrid_beamforming_precoder_s4_kernel(
@@ -33,6 +34,7 @@ def tile_hybrid_beamforming_precoder_s4_kernel(
     nc = tc.nc
     with ExitStack() as ctx:
         keep = ctx.enter_context(tc.tile_pool(name="keep", bufs=1))
+        results = ctx.enter_context(tc.tile_pool(name="results", bufs=1))
         psum = ctx.enter_context(tc.psum_pool(name="psum", bufs=8))
 
         def tile(shape, dtype, name):
@@ -59,7 +61,6 @@ def tile_hybrid_beamforming_precoder_s4_kernel(
         uv_packed = {m: tile([P, PHASES, SLOTS * P], BF16, "uv_packed%d" % m) for m in range(BLOCKS)}
         uv_codes = {m: tile([P, PHASES, P], U32, "uv_codes%d" % m) for m in range(BLOCKS)}
         uv_scales = {m: tile([P, PHASES, P], U8, "uv_scales%d" % m) for m in range(BLOCKS)}
-        rows = {(m, part): tile([P, ANTENNAS], F32, "rows%d%d" % (m, part)) for m in range(BLOCKS) for part in (RE, IM)}
 
         ctx.enter_context(tc.manual_schedule())
 
@@ -77,29 +78,35 @@ def tile_hybrid_beamforming_precoder_s4_kernel(
                 in_=by_partition[:, :, 2 * HALF * h : 2 * HALF * (h + 1)].bitcast(I32),
             )
 
-        def load_scales(engine, dst, src, j):
+        def load_scales(engine, dst, src, r):
             engine.dma_start(
-                out=dst[32 * j : 32 * j + 4, :, :].bitcast(I32),
-                in_=src[:, 4 * j : 4 * j + 4, :].rearrange("g r n -> r g n").bitcast(I32),
+                out=dst[r:P:32, :, :].bitcast(I32),
+                in_=src[:, r:16:4, :].rearrange("g j n -> j g n").bitcast(I32),
             )
 
-        def load_w(k, nh):
+        def load_gain(engine):
+            engine.dma_start(
+                out=gain_rows[0:P:32, :].rearrange("j (s n) -> j s n", s=PHASES),
+                in_=gain.rearrange("(s j n) -> j s n", s=PHASES, j=4),
+            )
+
+        def load_w(k, nh, engine=nc.sync):
             w = (cosw if k == "c" else sinw).rearrange("(q t r) n -> t q r n", t=SLOTS, r=RUN)
             for t in range(SLOTS):
-                nc.sync.dma_start(out=w_raw[k, nh][:, t, :], in_=w[t][:, :, HALF * nh : HALF * (nh + 1)])
+                engine.dma_start(out=w_raw[k, nh][:, t, :], in_=w[t][:, :, HALF * nh : HALF * (nh + 1)])
 
         load_codes(nc.sync, d_raw, dig_words, U)
         load_codes(nc.gpsimd, x_codes, sym_words, 0)
-        for j in range(4):
-            load_scales(nc.scalar, d_scales_raw, dig_scales, j)
-        for j in range(4):
-            load_scales(nc.sync if j < 3 else nc.gpsimd, x_scales, sym_scales, j)
+        for r in range(4):
+            load_scales(nc.scalar, d_scales_raw, dig_scales, r)
+        for r in range(4):
+            load_scales(nc.sync if r < 3 else nc.gpsimd, x_scales, sym_scales, r)
         nc.gpsimd.dma_start(
             out=gain_rows[0:P:32, :].rearrange("j (s n) -> j s n", s=PHASES),
             in_=gain.rearrange("(s j n) -> j s n", s=PHASES, j=4),
         )
-        load_w("c", 0)
         load_codes(nc.sync, d_raw, dig_words, V)
+        load_w("c", 0)
         load_w("b", 0)
         load_codes(nc.sync, x_codes, sym_words, 1)
         load_w("c", 1)
@@ -150,17 +157,22 @@ def tile_hybrid_beamforming_precoder_s4_kernel(
                     func=TANH,
                 )
 
-        def pack_w(copy, k, nh):
+        def pack_w(copy, k, nh, first=0, last=HALF):
             copy(
-                out=w_packed[k, nh][:].rearrange("p (c i t) -> p c t i", t=SLOTS, i=4),
-                in_=w_raw[k, nh][:].rearrange("p t (c i) -> p c t i", i=4),
+                out=w_packed[k, nh][:, SLOTS * first : SLOTS * last].rearrange("p (c i t) -> p c t i", t=SLOTS, i=4),
+                in_=w_raw[k, nh][:, :, first:last].rearrange("p t (c i) -> p c t i", i=4),
             )
 
-        def negate_b(nh):
-            nc.vector.tensor_scalar(out=w_packed["nb", nh][:], in0=w_packed["b", nh][:], scalar1=-1.0, scalar2=None, op0=MULT)
+        def negate_b(nh, first=0, last=HALF):
+            n = slice(SLOTS * first, SLOTS * last)
+            nc.vector.tensor_scalar(out=w_packed["nb", nh][:, n], in0=w_packed["b", nh][:, n], scalar1=-1.0, scalar2=None, op0=MULT)
 
-        def quantise_w(k, nh):
-            nc.vector.quantize_mx(out=w_codes[k, nh][:].bitcast(FP8X4), scales=w_scales[k, nh][:], in_=w_packed[k, nh][:])
+        def quantise_w(k, nh, first=0, last=HALF):
+            nc.vector.quantize_mx(
+                out=w_codes[k, nh][:, first:last].bitcast(FP8X4),
+                scales=w_scales[k, nh][:, first:last],
+                in_=w_packed[k, nh][:, SLOTS * first : SLOTS * last],
+            )
 
         def times_gain(s, m):
             n = P * (m % 2)
@@ -178,87 +190,115 @@ def tile_hybrid_beamforming_precoder_s4_kernel(
                 in_=uv_packed[m][:].rearrange("p s n -> p (s n)"),
             )
 
-        def product(m, part, nh, copy):
-            bank = psum.tile([P, HALF], F32, name="bank")
+        def passes(out, m, part, nh, first, last):
             for s in (U, V):
                 k = (("c", "nb"), ("b", "c"))[part][s]
                 nc.tensor.matmul_mx(
-                    out=bank[:],
+                    out=out,
                     lhsT=uv_codes[m][:, s, :].bitcast(FP8X4),
                     lhsT_scale=uv_scales[m][:, s, :],
-                    rhs=w_codes[k, nh][:].bitcast(FP8X4),
-                    rhs_scale=w_scales[k, nh][:],
+                    rhs=w_codes[k, nh][:, first:last].bitcast(FP8X4),
+                    rhs_scale=w_scales[k, nh][:, first:last],
                     start=(s == U),
                     stop=(s == V),
                 )
-            copy(out=rows[m, part][:, HALF * nh : HALF * (nh + 1)], in_=bank[:])
 
-        def store(m, part, first, last):
-            out = (out_0, out_1)[part]
-            nc.sync.dma_start(out=out[P * m : P * (m + 1), first:last], in_=rows[m, part][:, first:last])
+        def product(result, m, part, nh, copy):
+            bank = psum.tile([P, HALF], F32, name="bank")
+            passes(bank[:], m, part, nh, 0, HALF)
+            copy(out=result, in_=bank[:])
+
+        def store(result, part, m, blocks, first, last):
+            out = (out_0, out_1)[part][P * m : P * (m + blocks), first:last]
+            nc.sync.dma_start(out=out.rearrange("(j p) n -> p j n", j=blocks), in_=result)
 
         def half_rows(m, part, nh, copy=nc.scalar.copy):
-            product(m, part, nh, copy)
-            store(m, part, HALF * nh, HALF * (nh + 1))
+            result = results.tile([P, 1, HALF], F32, name="half%d%d%d" % (m, part, nh))
+            product(result[:, 0, :], m, part, nh, copy)
+            store(result[:], part, m, 1, HALF * nh, HALF * (nh + 1))
+
+        def full_rows(m, part, first_copy):
+            result = results.tile([P, 1, ANTENNAS], F32, name="full%d%d" % (m, part))
+            product(result[:, 0, 0:HALF], m, part, 0, first_copy)
+            product(result[:, 0, HALF:ANTENNAS], m, part, 1, nc.scalar.copy)
+            store(result[:], part, m, 1, 0, ANTENNAS)
+
+        def quarter_rows(m, part, first):
+            result = results.tile([P, 2, QUARTER], F32, name="quarter%d%d%d" % (m, part, first))
+            bank = psum.tile([P, 2, QUARTER], F32, name="bank")
+            for j in range(2):
+                passes(bank[:, j, :], m + j, part, 1, first, first + QUARTER)
+            nc.scalar.copy(out=result[:], in_=bank[:])
+            store(result[:], part, m, 2, HALF + first, HALF + first + QUARTER)
 
         sort_d(U)
         chains(U, 0)
         chains(U, 1)
         sort_gain()
-        pack_w(nc.vector.tensor_copy, "c", 0)
         sort_d(V)
         chains(V, 0)
         chains(V, 1)
         turn_gain()
-        quantise_w("c", 0)
+        pack_w(nc.vector.tensor_copy, "c", 0)
         gather_gain()
+        quantise_w("c", 0)
         pack_w(nc.vector.tensor_copy, "b", 0)
         times_gain(U, 0)
         quantise_w("b", 0)
         times_gain(V, 0)
         negate_b(0)
         quantise_uv(0)
+        times_gain(U, 1)
         quantise_w("nb", 0)
+        times_gain(V, 1)
         chains(U, 2)
-        pack_w(nc.scalar.copy, "c", 1)
         chains(V, 2)
+        chains(U, 3)
+        chains(V, 3)
 
         half_rows(0, IM, 0)
         half_rows(0, RE, 0)
-        times_gain(U, 1)
-        times_gain(V, 1)
-        quantise_w("c", 1)
-        quantise_uv(1)
-        chains(U, 3)
-        half_rows(1, IM, 0)
-        half_rows(1, RE, 0)
-        chains(V, 3)
-
-        pack_w(nc.vector.tensor_copy, "b", 1)
-        times_gain(U, 2)
-        quantise_w("b", 1)
-        for m in (0, 1):
-            half_rows(m, IM, 1)
-        negate_b(1)
-        times_gain(V, 2)
-        quantise_w("nb", 1)
-        for m in (0, 1):
-            half_rows(m, RE, 1)
-        quantise_uv(2)
-        times_gain(U, 3)
-        for m in range(3, BLOCKS):
-            times_gain(V, m)
-            if m + 1 < BLOCKS:
+        for m in range(1, EARLY):
+            if m + 1 < EARLY:
                 times_gain(U, m + 1)
+            else:
+                pack_w(nc.vector.tensor_copy, "c", 1, 0, QUARTER)
             quantise_uv(m)
+            if m + 1 < EARLY:
+                times_gain(V, m + 1)
+            half_rows(m, IM, 0)
+            half_rows(m, RE, 0)
 
-        for m in range(2, BLOCKS):
-            first_copy = nc.scalar.copy if m < 5 else nc.vector.tensor_copy
+        for first in (0, QUARTER):
+            last = first + QUARTER
+            pack_w(nc.vector.tensor_copy, "b", 1, first, last)
+            quantise_w("c", 1, first, last)
+            quantise_w("b", 1, first, last)
+            for m in range(0, EARLY, 2):
+                quarter_rows(m, IM, first)
+            negate_b(1, first, last)
+            if first == 0:
+                pack_w(nc.vector.tensor_copy, "c", 1, QUARTER, HALF)
+            else:
+                times_gain(U, EARLY)
+            quantise_w("nb", 1, first, last)
+            for m in range(0, EARLY, 2):
+                quarter_rows(m, RE, first)
+        times_gain(V, EARLY)
+        times_gain(U, EARLY + 1)
+        quantise_uv(EARLY)
+
+        for m in range(EARLY, BLOCKS):
+            if m + 1 < BLOCKS:
+                times_gain(V, m + 1)
+            if m + 2 < BLOCKS:
+                times_gain(U, m + 2)
+            if m + 1 < BLOCKS:
+                quantise_uv(m + 1)
             for part in (IM, RE):
+                first_copy = nc.vector.tensor_copy if m >= 6 else nc.scalar.copy
                 if (m, part) == (BLOCKS - 1, RE):
                     half_rows(m, part, 0, first_copy)
                     half_rows(m, part, 1)
                 else:
-                    product(m, part, 0, first_copy)
-                    product(m, part, 1, nc.scalar.copy)
-                    store(m, part, 0, ANTENNAS)
+                    full_rows(m, part, first_copy)

@@ -25,7 +25,7 @@ PHASES = 2
 U, V = 0, 1
 RE, IM = 0, 1
 BLOCKS = SAMPLES // P
-EARLY = 4
+EARLY = 3
 
 
 def tile_hybrid_beamforming_precoder_s4_kernel(
@@ -101,10 +101,7 @@ def tile_hybrid_beamforming_precoder_s4_kernel(
             load_scales(nc.scalar, d_scales_raw, dig_scales, r)
         for r in range(4):
             load_scales(nc.sync if r < 3 else nc.gpsimd, x_scales, sym_scales, r)
-        nc.gpsimd.dma_start(
-            out=gain_rows[0:P:32, :].rearrange("j (s n) -> j s n", s=PHASES),
-            in_=gain.rearrange("(s j n) -> j s n", s=PHASES, j=4),
-        )
+        load_gain(nc.gpsimd)
         load_codes(nc.sync, d_raw, dig_words, V)
         load_w("c", 0)
         load_w("b", 0)
@@ -223,14 +220,6 @@ def tile_hybrid_beamforming_precoder_s4_kernel(
             product(result[:, 0, HALF:ANTENNAS], m, part, 1, nc.scalar.copy)
             store(result[:], part, m, 1, 0, ANTENNAS)
 
-        def quarter_rows(m, part, first):
-            result = results.tile([P, 2, QUARTER], F32, name="quarter%d%d%d" % (m, part, first))
-            bank = psum.tile([P, 2, QUARTER], F32, name="bank")
-            for j in range(2):
-                passes(bank[:, j, :], m + j, part, 1, first, first + QUARTER)
-            nc.scalar.copy(out=result[:], in_=bank[:])
-            store(result[:], part, m, 2, HALF + first, HALF + first + QUARTER)
-
         sort_d(U)
         chains(U, 0)
         chains(U, 1)
@@ -239,9 +228,11 @@ def tile_hybrid_beamforming_precoder_s4_kernel(
         chains(V, 0)
         chains(V, 1)
         turn_gain()
-        pack_w(nc.vector.tensor_copy, "c", 0)
+        pack_w(nc.vector.tensor_copy, "c", 0, 0, QUARTER)
+        pack_w(nc.vector.tensor_copy, "c", 0, QUARTER, HALF)
+        quantise_w("c", 0, 0, QUARTER)
+        quantise_w("c", 0, QUARTER, HALF)
         gather_gain()
-        quantise_w("c", 0)
         pack_w(nc.vector.tensor_copy, "b", 0)
         times_gain(U, 0)
         quantise_w("b", 0)
@@ -258,33 +249,29 @@ def tile_hybrid_beamforming_precoder_s4_kernel(
 
         half_rows(0, IM, 0)
         half_rows(0, RE, 0)
+        pack_w(nc.scalar.copy, "c", 1, 0, QUARTER)
         for m in range(1, EARLY):
             if m + 1 < EARLY:
                 times_gain(U, m + 1)
             else:
-                pack_w(nc.vector.tensor_copy, "c", 1, 0, QUARTER)
+                pack_w(nc.vector.tensor_copy, "b", 1)
             quantise_uv(m)
             if m + 1 < EARLY:
                 times_gain(V, m + 1)
             half_rows(m, IM, 0)
             half_rows(m, RE, 0)
 
-        for first in (0, QUARTER):
-            last = first + QUARTER
-            pack_w(nc.vector.tensor_copy, "b", 1, first, last)
-            quantise_w("c", 1, first, last)
-            quantise_w("b", 1, first, last)
-            for m in range(0, EARLY, 2):
-                quarter_rows(m, IM, first)
-            negate_b(1, first, last)
-            if first == 0:
-                pack_w(nc.vector.tensor_copy, "c", 1, QUARTER, HALF)
-            else:
-                times_gain(U, EARLY)
-            quantise_w("nb", 1, first, last)
-            for m in range(0, EARLY, 2):
-                quarter_rows(m, RE, first)
+        pack_w(nc.vector.tensor_copy, "c", 1, QUARTER, HALF)
+        quantise_w("b", 1)
+        quantise_w("c", 1)
+        for m in range(EARLY):
+            half_rows(m, IM, 1)
+        negate_b(1)
+        times_gain(U, EARLY)
+        quantise_w("nb", 1)
         times_gain(V, EARLY)
+        for m in range(EARLY):
+            half_rows(m, RE, 1)
         times_gain(U, EARLY + 1)
         quantise_uv(EARLY)
 

@@ -22,10 +22,11 @@ GROUPS = STREAMS // 512
 HALF = 512
 QUARTER = 256
 PHASES = 2
-U, V = 0, 1
+U, V, MINUS_V = 0, 1, 2
 RE, IM = 0, 1
+BANKS = 8
 BLOCKS = SAMPLES // P
-EARLY = 3
+EARLY = 2
 
 
 def tile_hybrid_beamforming_precoder_s4_kernel(
@@ -35,7 +36,7 @@ def tile_hybrid_beamforming_precoder_s4_kernel(
     with ExitStack() as ctx:
         keep = ctx.enter_context(tc.tile_pool(name="keep", bufs=1))
         results = ctx.enter_context(tc.tile_pool(name="results", bufs=1))
-        psum = ctx.enter_context(tc.psum_pool(name="psum", bufs=8))
+        psum = ctx.enter_context(tc.psum_pool(name="psum", bufs=1))
 
         def tile(shape, dtype, name):
             return keep.tile(shape, dtype, name=name, align_bytes=256)
@@ -51,18 +52,24 @@ def tile_hybrid_beamforming_precoder_s4_kernel(
         gain_turned = tile([P, PHASES * P], BF16, "gain_turned")
         gain_cols = tile([P, PHASES, SLOTS], F32, "gain_cols")
 
-        halves = [(k, nh) for k in ("c", "b", "nb") for nh in range(2)]
-        w_raw = {(k, nh): tile([P, SLOTS, HALF], BF16, "raw_%s%d" % (k, nh)) for k, nh in halves if k != "nb"}
+        halves = [(k, nh) for k in ("c", "b") for nh in range(2)]
+        w_raw = {(k, nh): tile([P, SLOTS, HALF], BF16, "raw_%s%d" % (k, nh)) for k, nh in halves}
         w_packed = {(k, nh): tile([P, SLOTS * HALF], BF16, "packed_%s%d" % (k, nh)) for k, nh in halves}
         w_codes = {(k, nh): tile([P, HALF], U32, "codes_%s%d" % (k, nh)) for k, nh in halves}
         w_scales = {(k, nh): tile([P, HALF], U8, "scales_%s%d" % (k, nh)) for k, nh in halves}
 
         tanh_h = {(s, q): tile([P, 2, 2 * QUARTER], F32, "tanh_%d%d" % (s, q)) for s in (U, V) for q in range(4)}
-        uv_packed = {m: tile([P, PHASES, SLOTS * P], BF16, "uv_packed%d" % m) for m in range(BLOCKS)}
-        uv_codes = {m: tile([P, PHASES, P], U32, "uv_codes%d" % m) for m in range(BLOCKS)}
-        uv_scales = {m: tile([P, PHASES, P], U8, "uv_scales%d" % m) for m in range(BLOCKS)}
+        uv_packed = {m: tile([P, 3, SLOTS * P], BF16, "uv_packed%d" % m) for m in range(BLOCKS)}
+        uv_codes = {m: tile([P, 3, P], U32, "uv_codes%d" % m) for m in range(BLOCKS)}
+        uv_scales = {m: tile([P, 3, P], U8, "uv_scales%d" % m) for m in range(BLOCKS)}
 
         ctx.enter_context(tc.manual_schedule())
+
+        turns = []
+
+        def next_bank(banks):
+            turns.append(banks)
+            return psum.tile([P, HALF], F32, name="bank%d" % ((len(turns) - 1) % banks))
 
         def words(t, pattern):
             return t[:].rearrange(pattern).bitcast(I32)
@@ -133,14 +140,16 @@ def tile_hybrid_beamforming_precoder_s4_kernel(
         def gather_gain():
             nc.vector.tensor_copy(out=gain_cols[:].rearrange("p s t -> p (s t)"), in_=gain_turned[:, 0 : PHASES * P : 32])
 
-        def chains(s, q):
+        sums = {}
+
+        def first_matmul(s, q):
             n = QUARTER * (q % 2)
             for pair in range(2):
-                bank = psum.tile([P, HALF], F32, name="bank")
+                sums[s, q, pair] = next_bank(BANKS)
                 for j in range(2):
                     for g in range(GROUPS):
                         nc.tensor.matmul_mx(
-                            out=bank[:, QUARTER * j : QUARTER * (j + 1)],
+                            out=sums[s, q, pair][:, QUARTER * j : QUARTER * (j + 1)],
                             lhsT=d_codes[s][:, g, 2 * pair + j, :].bitcast(FP4X4),
                             lhsT_scale=d_scales[s][:, g, 2 * pair + j, :],
                             rhs=x_codes[q // 2][:, g, 2 * n : 2 * (n + QUARTER)].bitcast(FP4X4),
@@ -148,11 +157,18 @@ def tile_hybrid_beamforming_precoder_s4_kernel(
                             start=(g == 0),
                             stop=(g == GROUPS - 1),
                         )
-                nc.scalar.activation(
-                    out=tanh_h[s, q][:, pair, :].rearrange("p (n j) -> p n j", j=2),
-                    in_=bank[:].rearrange("p (j n) -> p n j", j=2),
-                    func=TANH,
-                )
+
+        def soft_limit(s, q, pair):
+            nc.scalar.activation(
+                out=tanh_h[s, q][:, pair, :].rearrange("p (n j) -> p n j", j=2),
+                in_=sums[s, q, pair][:].rearrange("p (j n) -> p n j", j=2),
+                func=TANH,
+            )
+
+        def chains(s, q):
+            first_matmul(s, q)
+            for pair in range(2):
+                soft_limit(s, q, pair)
 
         def pack_w(copy, k, nh, first=0, last=HALF):
             copy(
@@ -160,9 +176,8 @@ def tile_hybrid_beamforming_precoder_s4_kernel(
                 in_=w_raw[k, nh][:, :, first:last].rearrange("p t (c i) -> p c t i", i=4),
             )
 
-        def negate_b(nh, first=0, last=HALF):
-            n = slice(SLOTS * first, SLOTS * last)
-            nc.vector.tensor_scalar(out=w_packed["nb", nh][:, n], in0=w_packed["b", nh][:, n], scalar1=-1.0, scalar2=None, op0=MULT)
+        def negate_v(m):
+            nc.vector.tensor_scalar(out=uv_packed[m][:, MINUS_V, :], in0=uv_packed[m][:, V, :], scalar1=-1.0, scalar2=None, op0=MULT)
 
         def quantise_w(k, nh, first=0, last=HALF):
             nc.vector.quantize_mx(
@@ -180,16 +195,22 @@ def tile_hybrid_beamforming_precoder_s4_kernel(
                 op=MULT,
             )
 
-        def quantise_uv(m):
+        def quantise_uv(m, first, last):
             nc.vector.quantize_mx(
-                out=uv_codes[m][:].rearrange("p s n -> p (s n)").bitcast(FP8X4),
-                scales=uv_scales[m][:].rearrange("p s n -> p (s n)"),
-                in_=uv_packed[m][:].rearrange("p s n -> p (s n)"),
+                out=uv_codes[m][:, first:last, :].rearrange("p s n -> p (s n)").bitcast(FP8X4),
+                scales=uv_scales[m][:, first:last, :].rearrange("p s n -> p (s n)"),
+                in_=uv_packed[m][:, first:last, :].rearrange("p s n -> p (s n)"),
             )
 
+        def block(m):
+            times_gain(V, m)
+            times_gain(U, m)
+            negate_v(m)
+            quantise_uv(m, U, MINUS_V)
+            quantise_uv(m, MINUS_V, MINUS_V + 1)
+
         def passes(out, m, part, nh, first, last):
-            for s in (U, V):
-                k = (("c", "nb"), ("b", "c"))[part][s]
+            for s, k in (((U, "c"), (MINUS_V, "b")), ((U, "b"), (V, "c")))[part]:
                 nc.tensor.matmul_mx(
                     out=out,
                     lhsT=uv_codes[m][:, s, :].bitcast(FP8X4),
@@ -197,11 +218,11 @@ def tile_hybrid_beamforming_precoder_s4_kernel(
                     rhs=w_codes[k, nh][:, first:last].bitcast(FP8X4),
                     rhs_scale=w_scales[k, nh][:, first:last],
                     start=(s == U),
-                    stop=(s == V),
+                    stop=(s != U),
                 )
 
-        def product(result, m, part, nh, copy):
-            bank = psum.tile([P, HALF], F32, name="bank")
+        def product(result, m, part, nh, copy, banks):
+            bank = next_bank(banks)
             passes(bank[:], m, part, nh, 0, HALF)
             copy(out=result, in_=bank[:])
 
@@ -209,15 +230,15 @@ def tile_hybrid_beamforming_precoder_s4_kernel(
             out = (out_0, out_1)[part][P * m : P * (m + blocks), first:last]
             nc.sync.dma_start(out=out.rearrange("(j p) n -> p j n", j=blocks), in_=result)
 
-        def half_rows(m, part, nh, copy=nc.scalar.copy):
+        def half_rows(m, part, nh, copy=nc.scalar.copy, banks=BANKS):
             result = results.tile([P, 1, HALF], F32, name="half%d%d%d" % (m, part, nh))
-            product(result[:, 0, :], m, part, nh, copy)
+            product(result[:, 0, :], m, part, nh, copy, banks)
             store(result[:], part, m, 1, HALF * nh, HALF * (nh + 1))
 
-        def full_rows(m, part, first_copy):
+        def full_rows(m, part, first_copy, banks=BANKS):
             result = results.tile([P, 1, ANTENNAS], F32, name="full%d%d" % (m, part))
-            product(result[:, 0, 0:HALF], m, part, 0, first_copy)
-            product(result[:, 0, HALF:ANTENNAS], m, part, 1, nc.scalar.copy)
+            product(result[:, 0, 0:HALF], m, part, 0, first_copy, banks)
+            product(result[:, 0, HALF:ANTENNAS], m, part, 1, nc.scalar.copy, banks)
             store(result[:], part, m, 1, 0, ANTENNAS)
 
         sort_d(U)
@@ -228,64 +249,42 @@ def tile_hybrid_beamforming_precoder_s4_kernel(
         chains(V, 0)
         chains(V, 1)
         turn_gain()
-        pack_w(nc.vector.tensor_copy, "c", 0, 0, QUARTER)
-        pack_w(nc.vector.tensor_copy, "c", 0, QUARTER, HALF)
-        quantise_w("c", 0, 0, QUARTER)
-        quantise_w("c", 0, QUARTER, HALF)
+        pack_w(nc.vector.tensor_copy, "c", 0)
         gather_gain()
         pack_w(nc.vector.tensor_copy, "b", 0)
-        times_gain(U, 0)
+        quantise_w("c", 0)
         quantise_w("b", 0)
-        times_gain(V, 0)
-        negate_b(0)
-        quantise_uv(0)
-        times_gain(U, 1)
-        quantise_w("nb", 0)
-        times_gain(V, 1)
         chains(U, 2)
+        pack_w(nc.scalar.copy, "c", 1)
         chains(V, 2)
-        chains(U, 3)
-        chains(V, 3)
+        first_matmul(U, 3)
+        first_matmul(V, 3)
 
-        half_rows(0, IM, 0)
-        half_rows(0, RE, 0)
-        pack_w(nc.scalar.copy, "c", 1, 0, QUARTER)
-        for m in range(1, EARLY):
-            if m + 1 < EARLY:
-                times_gain(U, m + 1)
-            else:
-                pack_w(nc.vector.tensor_copy, "b", 1)
-            quantise_uv(m)
-            if m + 1 < EARLY:
-                times_gain(V, m + 1)
-            half_rows(m, IM, 0)
-            half_rows(m, RE, 0)
+        for m in range(EARLY):
+            block(m)
+            half_rows(m, IM, 0, nc.scalar.copy, 4)
+            half_rows(m, RE, 0, nc.scalar.copy, 4)
+        soft_limit(0, 3, 0)
+        soft_limit(0, 3, 1)
 
-        pack_w(nc.vector.tensor_copy, "c", 1, QUARTER, HALF)
-        quantise_w("b", 1)
+        pack_w(nc.vector.tensor_copy, "b", 1)
         quantise_w("c", 1)
+        quantise_w("b", 1)
         for m in range(EARLY):
-            half_rows(m, IM, 1)
-        negate_b(1)
-        times_gain(U, EARLY)
-        quantise_w("nb", 1)
-        times_gain(V, EARLY)
-        for m in range(EARLY):
-            half_rows(m, RE, 1)
-        times_gain(U, EARLY + 1)
-        quantise_uv(EARLY)
+            half_rows(m, IM, 1, nc.scalar.copy, 4)
+            half_rows(m, RE, 1, nc.scalar.copy, 4)
+        block(EARLY)
 
         for m in range(EARLY, BLOCKS):
             if m + 1 < BLOCKS:
-                times_gain(V, m + 1)
-            if m + 2 < BLOCKS:
-                times_gain(U, m + 2)
-            if m + 1 < BLOCKS:
-                quantise_uv(m + 1)
+                block(m + 1)
             for part in (IM, RE):
-                first_copy = nc.vector.tensor_copy if m >= 6 else nc.scalar.copy
+                late = 2 * (m - EARLY) + (part == RE) + 2
+                first_copy = nc.vector.tensor_copy if m >= 6 or late < 4 else nc.scalar.copy
+                if late < 4:
+                    soft_limit(late // 2, 3, late % 2)
                 if (m, part) == (BLOCKS - 1, RE):
                     half_rows(m, part, 0, first_copy)
                     half_rows(m, part, 1)
                 else:
-                    full_rows(m, part, first_copy)
+                    full_rows(m, part, first_copy, 4 if late < 4 else BANKS)

@@ -195,19 +195,15 @@ def tile_hybrid_beamforming_precoder_s4_kernel(
                 op=MULT,
             )
 
-        def quantise_uv(m, first, last):
-            nc.vector.quantize_mx(
-                out=uv_codes[m][:, first:last, :].rearrange("p s n -> p (s n)").bitcast(FP8X4),
-                scales=uv_scales[m][:, first:last, :].rearrange("p s n -> p (s n)"),
-                in_=uv_packed[m][:, first:last, :].rearrange("p s n -> p (s n)"),
-            )
+        def quantise_uv(m, s):
+            nc.vector.quantize_mx(out=uv_codes[m][:, s, :].bitcast(FP8X4), scales=uv_scales[m][:, s, :], in_=uv_packed[m][:, s, :])
 
         def block(m):
             times_gain(V, m)
             times_gain(U, m)
             negate_v(m)
-            quantise_uv(m, U, MINUS_V)
-            quantise_uv(m, MINUS_V, MINUS_V + 1)
+            for s in (V, U, MINUS_V):
+                quantise_uv(m, s)
 
         def passes(out, m, part, nh, first, last):
             for s, k in (((U, "c"), (MINUS_V, "b")), ((U, "b"), (V, "c")))[part]:

@@ -26,7 +26,7 @@ U, V, MINUS_V = 0, 1, 2
 RE, IM = 0, 1
 BANKS = 8
 BLOCKS = SAMPLES // P
-EARLY = 2
+WARM_UP = 7
 
 
 def tile_hybrid_beamforming_precoder_s4_kernel(
@@ -41,7 +41,8 @@ def tile_hybrid_beamforming_precoder_s4_kernel(
         def tile(shape, dtype, name):
             return keep.tile(shape, dtype, name=name, align_bytes=256)
 
-        x_codes = {h: tile([P, GROUPS, 2 * HALF], U8, "x_codes%d" % h) for h in range(2)}
+        x_loads = ((0, QUARTER), (QUARTER, HALF), (HALF, SAMPLES))
+        x_codes = [tile([P, GROUPS, 2 * (last - first)], U8, "x_codes%d" % first) for first, last in x_loads]
         x_scales = tile([P, GROUPS, SAMPLES], U8, "x_scales")
         d_raw = {s: tile([P, GROUPS, 2 * CHAINS], U8, "d_raw%d" % s) for s in (U, V)}
         d_scales_raw = tile([P, GROUPS, PHASES * CHAINS], U8, "d_scales_raw")
@@ -65,11 +66,12 @@ def tile_hybrid_beamforming_precoder_s4_kernel(
 
         ctx.enter_context(tc.manual_schedule())
 
-        turns = []
+        line = list(range(BANKS))
 
-        def next_bank(banks):
-            turns.append(banks)
-            return psum.tile([P, HALF], F32, name="bank%d" % ((len(turns) - 1) % banks))
+        def take_bank():
+            number = line[0]
+            line.remove(number)
+            return number, psum.tile([P, HALF], F32, name="bank%d" % number)
 
         def words(t, pattern):
             return t[:].rearrange(pattern).bitcast(I32)
@@ -78,12 +80,29 @@ def tile_hybrid_beamforming_precoder_s4_kernel(
         nc.vector.memset(words(x_scales, "p g n -> p (g n)"), 0)
         nc.vector.memset(gain_rows[:], 0.0)
 
-        def load_codes(engine, dst, src, h):
-            by_partition = src.rearrange("g p x -> p g x")
-            engine.dma_start(
-                out=dst[h][:].bitcast(I32),
-                in_=by_partition[:, :, 2 * HALF * h : 2 * HALF * (h + 1)].bitcast(I32),
+        nc.vector.memset(x_codes[2][:, 0, :].bitcast(I32), 0)
+        nc.vector.memset(w_scales["b", 1][:].bitcast(I32), 0)
+        warm_bank = psum.tile([P, HALF], F32, name="bank7")
+        for unused in range(WARM_UP):
+            nc.tensor.matmul_mx(
+                out=warm_bank[:],
+                lhsT=x_codes[2][:, 0, 0 : 2 * P].bitcast(FP4X4),
+                lhsT_scale=w_scales["b", 1][:, 0:P],
+                rhs=x_codes[2][:, 0, :].bitcast(FP4X4),
+                rhs_scale=w_scales["b", 1][:],
+                start=True,
+                stop=True,
             )
+
+        def load_codes(engine, dst, src, first, last):
+            by_partition = src.rearrange("g p x -> p g x")
+            engine.dma_start(out=dst[:].bitcast(I32), in_=by_partition[:, :, 2 * first : 2 * last].bitcast(I32))
+
+        def load_x(piece):
+            load_codes(nc.sync, x_codes[piece], sym_words, *x_loads[piece])
+
+        def load_d(engine, s):
+            load_codes(engine, d_raw[s], dig_words, CHAINS * s, CHAINS * (s + 1))
 
         def load_scales(engine, dst, src, r):
             engine.dma_start(
@@ -97,22 +116,23 @@ def tile_hybrid_beamforming_precoder_s4_kernel(
                 in_=gain.rearrange("(s j n) -> j s n", s=PHASES, j=4),
             )
 
-        def load_w(k, nh, engine=nc.sync):
+        def load_w(k, nh):
             w = (cosw if k == "c" else sinw).rearrange("(q t r) n -> t q r n", t=SLOTS, r=RUN)
             for t in range(SLOTS):
-                engine.dma_start(out=w_raw[k, nh][:, t, :], in_=w[t][:, :, HALF * nh : HALF * (nh + 1)])
+                nc.sync.dma_start(out=w_raw[k, nh][:, t, :], in_=w[t][:, :, HALF * nh : HALF * (nh + 1)])
 
-        load_codes(nc.sync, d_raw, dig_words, U)
-        load_codes(nc.gpsimd, x_codes, sym_words, 0)
-        for r in range(4):
-            load_scales(nc.scalar, d_scales_raw, dig_scales, r)
-        for r in range(4):
-            load_scales(nc.sync if r < 3 else nc.gpsimd, x_scales, sym_scales, r)
+        load_x(0)
+        load_d(nc.sync, U)
+        load_d(nc.gpsimd, V)
         load_gain(nc.gpsimd)
-        load_codes(nc.sync, d_raw, dig_words, V)
+        for r in range(4):
+            load_scales(nc.sync, d_scales_raw, dig_scales, r)
+        for r in range(4):
+            load_scales(nc.sync, x_scales, sym_scales, r)
+        load_x(1)
         load_w("c", 0)
         load_w("b", 0)
-        load_codes(nc.sync, x_codes, sym_words, 1)
+        load_x(2)
         load_w("c", 1)
         load_w("b", 1)
 
@@ -140,19 +160,20 @@ def tile_hybrid_beamforming_precoder_s4_kernel(
         def gather_gain():
             nc.vector.tensor_copy(out=gain_cols[:].rearrange("p s t -> p (s t)"), in_=gain_turned[:, 0 : PHASES * P : 32])
 
-        sums = {}
+        sums, numbers = {}, {}
 
         def first_matmul(s, q):
-            n = QUARTER * (q % 2)
+            piece = min(q, 2)
+            n = QUARTER * q - x_loads[piece][0]
             for pair in range(2):
-                sums[s, q, pair] = next_bank(BANKS)
+                numbers[s, q, pair], sums[s, q, pair] = take_bank()
                 for j in range(2):
                     for g in range(GROUPS):
                         nc.tensor.matmul_mx(
                             out=sums[s, q, pair][:, QUARTER * j : QUARTER * (j + 1)],
                             lhsT=d_codes[s][:, g, 2 * pair + j, :].bitcast(FP4X4),
                             lhsT_scale=d_scales[s][:, g, 2 * pair + j, :],
-                            rhs=x_codes[q // 2][:, g, 2 * n : 2 * (n + QUARTER)].bitcast(FP4X4),
+                            rhs=x_codes[piece][:, g, 2 * n : 2 * (n + QUARTER)].bitcast(FP4X4),
                             rhs_scale=x_scales[:, g, QUARTER * q : QUARTER * (q + 1)],
                             start=(g == 0),
                             stop=(g == GROUPS - 1),
@@ -164,6 +185,7 @@ def tile_hybrid_beamforming_precoder_s4_kernel(
                 in_=sums[s, q, pair][:].rearrange("p (j n) -> p n j", j=2),
                 func=TANH,
             )
+            line.append(numbers[s, q, pair])
 
         def chains(s, q):
             first_matmul(s, q)
@@ -217,24 +239,25 @@ def tile_hybrid_beamforming_precoder_s4_kernel(
                     stop=(s != U),
                 )
 
-        def product(result, m, part, nh, copy, banks):
-            bank = next_bank(banks)
+        def product(result, m, part, nh, copy):
+            number, bank = take_bank()
             passes(bank[:], m, part, nh, 0, HALF)
             copy(out=result, in_=bank[:])
+            line.append(number)
 
         def store(result, part, m, blocks, first, last):
             out = (out_0, out_1)[part][P * m : P * (m + blocks), first:last]
             nc.sync.dma_start(out=out.rearrange("(j p) n -> p j n", j=blocks), in_=result)
 
-        def half_rows(m, part, nh, copy=nc.scalar.copy, banks=BANKS):
+        def half_rows(m, part, nh, copy=nc.scalar.copy):
             result = results.tile([P, 1, HALF], F32, name="half%d%d%d" % (m, part, nh))
-            product(result[:, 0, :], m, part, nh, copy, banks)
+            product(result[:, 0, :], m, part, nh, copy)
             store(result[:], part, m, 1, HALF * nh, HALF * (nh + 1))
 
-        def full_rows(m, part, first_copy, banks=BANKS):
+        def full_rows(m, part, first_copy):
             result = results.tile([P, 1, ANTENNAS], F32, name="full%d%d" % (m, part))
-            product(result[:, 0, 0:HALF], m, part, 0, first_copy, banks)
-            product(result[:, 0, HALF:ANTENNAS], m, part, 1, nc.scalar.copy, banks)
+            product(result[:, 0, 0:HALF], m, part, 0, first_copy)
+            product(result[:, 0, HALF:ANTENNAS], m, part, 1, nc.scalar.copy)
             store(result[:], part, m, 1, 0, ANTENNAS)
 
         sort_d(U)
@@ -252,35 +275,40 @@ def tile_hybrid_beamforming_precoder_s4_kernel(
         quantise_w("b", 0)
         chains(U, 2)
         pack_w(nc.scalar.copy, "c", 1)
-        chains(V, 2)
+        first_matmul(V, 2)
         first_matmul(U, 3)
-        first_matmul(V, 3)
 
-        for m in range(EARLY):
-            block(m)
-            half_rows(m, IM, 0, nc.scalar.copy, 4)
-            half_rows(m, RE, 0, nc.scalar.copy, 4)
-        soft_limit(0, 3, 0)
-        soft_limit(0, 3, 1)
+        block(0)
+        half_rows(0, IM, 0)
+        half_rows(0, RE, 0)
+        soft_limit(V, 2, 0)
+        soft_limit(V, 2, 1)
+        block(1)
+        half_rows(1, IM, 0)
+        half_rows(1, RE, 0)
+        first_matmul(V, 3)
+        soft_limit(U, 3, 0)
 
         pack_w(nc.vector.tensor_copy, "b", 1)
         quantise_w("c", 1)
         quantise_w("b", 1)
-        for m in range(EARLY):
-            half_rows(m, IM, 1, nc.scalar.copy, 4)
-            half_rows(m, RE, 1, nc.scalar.copy, 4)
-        block(EARLY)
+        for m in (0, 1):
+            half_rows(m, IM, 1)
+            half_rows(m, RE, 1)
+        block(2)
 
-        for m in range(EARLY, BLOCKS):
+        waiting = {(2, IM): (U, 3, 1), (2, RE): (V, 3, 0), (3, RE): (V, 3, 1)}
+        last_rows = ((BLOCKS - 2, RE), (BLOCKS - 1, IM), (BLOCKS - 1, RE))
+        for m in range(2, BLOCKS):
             if m + 1 < BLOCKS:
                 block(m + 1)
             for part in (IM, RE):
-                late = 2 * (m - EARLY) + (part == RE) + 2
-                first_copy = nc.vector.tensor_copy if m >= 6 or late < 4 else nc.scalar.copy
-                if late < 4:
-                    soft_limit(late // 2, 3, late % 2)
-                if (m, part) == (BLOCKS - 1, RE):
+                if (m, part) in waiting:
+                    soft_limit(*waiting[m, part])
+                by_vector = (m, part) in waiting or (m, part) in last_rows
+                first_copy = nc.vector.tensor_copy if by_vector else nc.scalar.copy
+                if (m, part) == last_rows[-1]:
                     half_rows(m, part, 0, first_copy)
                     half_rows(m, part, 1)
                 else:
-                    full_rows(m, part, first_copy, 4 if late < 4 else BANKS)
+                    full_rows(m, part, first_copy)

@@ -129,8 +129,8 @@ def tile_hybrid_beamforming_precoder_s4_kernel(
             load_scales(nc.sync, d_scales_raw, dig_scales, r)
         for r in range(4):
             load_scales(nc.sync, x_scales, sym_scales, r)
-        load_x(1)
         load_w("c", 0)
+        load_x(1)
         load_w("b", 0)
         load_x(2)
         load_w("c", 1)
@@ -262,23 +262,29 @@ def tile_hybrid_beamforming_precoder_s4_kernel(
 
         sort_d(U)
         chains(U, 0)
-        chains(U, 1)
-        sort_gain()
         sort_d(V)
         chains(V, 0)
+        chains(U, 1)
         chains(V, 1)
+        sort_gain()
         turn_gain()
-        pack_w(nc.vector.tensor_copy, "c", 0)
+        pack_w(nc.vector.tensor_copy, "c", 0, 0, QUARTER)
         gather_gain()
-        pack_w(nc.vector.tensor_copy, "b", 0)
+        pack_w(nc.vector.tensor_copy, "c", 0, QUARTER, HALF)
+        times_gain(U, 0)
         quantise_w("c", 0)
+        times_gain(V, 0)
+        pack_w(nc.vector.tensor_copy, "b", 0)
+        negate_v(0)
+        quantise_uv(0, V)
+        quantise_uv(0, U)
         quantise_w("b", 0)
+        quantise_uv(0, MINUS_V)
         chains(U, 2)
         pack_w(nc.scalar.copy, "c", 1)
         first_matmul(V, 2)
         first_matmul(U, 3)
 
-        block(0)
         half_rows(0, IM, 0)
         half_rows(0, RE, 0)
         soft_limit(V, 2, 0)

@@ -26,7 +26,7 @@ U, V, MINUS_V = 0, 1, 2
 RE, IM = 0, 1
 BANKS = 8
 BLOCKS = SAMPLES // P
-WARM_UP = 7
+WARM_UP = 6
 
 
 def tile_hybrid_beamforming_precoder_s4_kernel(
@@ -94,24 +94,24 @@ def tile_hybrid_beamforming_precoder_s4_kernel(
                 stop=True,
             )
 
-        def load_codes(engine, dst, src, first, last):
+        def load_codes(dst, src, first, last):
             by_partition = src.rearrange("g p x -> p g x")
-            engine.dma_start(out=dst[:].bitcast(I32), in_=by_partition[:, :, 2 * first : 2 * last].bitcast(I32))
+            nc.sync.dma_start(out=dst[:].bitcast(I32), in_=by_partition[:, :, 2 * first : 2 * last].bitcast(I32))
 
         def load_x(piece):
-            load_codes(nc.sync, x_codes[piece], sym_words, *x_loads[piece])
+            load_codes(x_codes[piece], sym_words, *x_loads[piece])
 
-        def load_d(engine, s):
-            load_codes(engine, d_raw[s], dig_words, CHAINS * s, CHAINS * (s + 1))
+        def load_d(s):
+            load_codes(d_raw[s], dig_words, CHAINS * s, CHAINS * (s + 1))
 
-        def load_scales(engine, dst, src, r):
-            engine.dma_start(
+        def load_scales(dst, src, r):
+            nc.sync.dma_start(
                 out=dst[r:P:32, :, :].bitcast(I32),
                 in_=src[:, r:16:4, :].rearrange("g j n -> j g n").bitcast(I32),
             )
 
-        def load_gain(engine):
-            engine.dma_start(
+        def load_gain():
+            nc.sync.dma_start(
                 out=gain_rows[0:P:32, :].rearrange("j (s n) -> j s n", s=PHASES),
                 in_=gain.rearrange("(s j n) -> j s n", s=PHASES, j=4),
             )
@@ -122,13 +122,13 @@ def tile_hybrid_beamforming_precoder_s4_kernel(
                 nc.sync.dma_start(out=w_raw[k, nh][:, t, :], in_=w[t][:, :, HALF * nh : HALF * (nh + 1)])
 
         load_x(0)
-        load_d(nc.sync, U)
-        load_d(nc.gpsimd, V)
-        load_gain(nc.gpsimd)
         for r in range(4):
-            load_scales(nc.sync, d_scales_raw, dig_scales, r)
+            load_scales(d_scales_raw, dig_scales, r)
+        load_d(U)
         for r in range(4):
-            load_scales(nc.sync, x_scales, sym_scales, r)
+            load_scales(x_scales, sym_scales, r)
+        load_d(V)
+        load_gain()
         load_w("c", 0)
         load_x(1)
         load_w("b", 0)

@@ -41,13 +41,17 @@ def tile_hybrid_beamforming_precoder_s4_kernel(
         def tile(shape, dtype, name):
             return keep.tile(shape, dtype, name=name, align_bytes=256)
 
+        def shifted(rows, width, dtype, name, shift):
+            whole = tile([P, shift + rows * width], dtype, name)
+            return whole[:, shift:].rearrange("p (r n) -> p r n", r=rows)
+
         x_loads = ((0, QUARTER), (QUARTER, HALF), (HALF, SAMPLES))
-        x_codes = [tile([P, GROUPS, 2 * (last - first)], U8, "x_codes%d" % first) for first, last in x_loads]
-        x_scales = tile([P, GROUPS, SAMPLES], U8, "x_scales")
+        x_codes = [shifted(GROUPS, 2 * (last - first), U8, "x_codes%d" % first, 128) for first, last in x_loads]
+        x_scales = shifted(GROUPS, SAMPLES, U8, "x_scales", 192)
         d_raw = {s: tile([P, GROUPS, 2 * CHAINS], U8, "d_raw%d" % s) for s in (U, V)}
         d_scales_raw = tile([P, GROUPS, PHASES * CHAINS], U8, "d_scales_raw")
         d_codes = {s: tile([P, GROUPS, SLOTS, 2 * P], U8, "d_codes%d" % s) for s in (U, V)}
-        d_scales = {s: tile([P, GROUPS, SLOTS, P], U8, "d_scales%d" % s) for s in (U, V)}
+        d_scales = {s: shifted(GROUPS * SLOTS, P, U8, "d_scales%d" % s, 64) for s in (U, V)}
         gain_rows = tile([P, PHASES * P], BF16, "gain_rows")
         gain_sorted = tile([P, PHASES * P], BF16, "gain_sorted")
         gain_turned = tile([P, PHASES * P], BF16, "gain_turned")
@@ -56,13 +60,13 @@ def tile_hybrid_beamforming_precoder_s4_kernel(
         halves = [(k, nh) for k in ("c", "b") for nh in range(2)]
         w_raw = {(k, nh): tile([P, SLOTS, HALF], BF16, "raw_%s%d" % (k, nh)) for k, nh in halves}
         w_packed = {(k, nh): tile([P, SLOTS * HALF], BF16, "packed_%s%d" % (k, nh)) for k, nh in halves}
-        w_codes = {(k, nh): tile([P, HALF], U32, "codes_%s%d" % (k, nh)) for k, nh in halves}
-        w_scales = {(k, nh): tile([P, HALF], U8, "scales_%s%d" % (k, nh)) for k, nh in halves}
+        w_codes = {(k, nh): shifted(1, HALF, U32, "codes_%s%d" % (k, nh), 32)[:, 0, :] for k, nh in halves}
+        w_scales = {(k, nh): shifted(1, HALF, U8, "scales_%s%d" % (k, nh), 192)[:, 0, :] for k, nh in halves}
 
         tanh_h = {(s, q): tile([P, 2, 2 * QUARTER], F32, "tanh_%d%d" % (s, q)) for s in (U, V) for q in range(4)}
         uv_packed = {m: tile([P, 3, SLOTS * P], BF16, "uv_packed%d" % m) for m in range(BLOCKS)}
         uv_codes = {m: tile([P, 3, P], U32, "uv_codes%d" % m) for m in range(BLOCKS)}
-        uv_scales = {m: tile([P, 3, P], U8, "uv_scales%d" % m) for m in range(BLOCKS)}
+        uv_scales = {m: shifted(3, P, U8, "uv_scales%d" % m, 64) for m in range(BLOCKS)}
 
         ctx.enter_context(tc.manual_schedule())
 
@@ -138,7 +142,7 @@ def tile_hybrid_beamforming_precoder_s4_kernel(
 
         def sort_d(s):
             nc.vector.tensor_copy(
-                out=words(d_scales[s], "p g t n -> p (g t n)").rearrange("p (g t q w) -> p g t q w", g=GROUPS, t=SLOTS, w=2),
+                out=words(d_scales[s], "p x n -> p (x n)").rearrange("p (g t q w) -> p g t q w", g=GROUPS, t=SLOTS, w=2),
                 in_=words(d_scales_raw, "p g n -> p (g n)").rearrange(
                     "p (g s q t w) -> p s g t q w", g=GROUPS, s=PHASES, t=SLOTS, w=2
                 )[:, s],
@@ -172,7 +176,7 @@ def tile_hybrid_beamforming_precoder_s4_kernel(
                         nc.tensor.matmul_mx(
                             out=sums[s, q, pair][:, QUARTER * j : QUARTER * (j + 1)],
                             lhsT=d_codes[s][:, g, 2 * pair + j, :].bitcast(FP4X4),
-                            lhsT_scale=d_scales[s][:, g, 2 * pair + j, :],
+                            lhsT_scale=d_scales[s][:, SLOTS * g + 2 * pair + j, :],
                             rhs=x_codes[piece][:, g, 2 * n : 2 * (n + QUARTER)].bitcast(FP4X4),
                             rhs_scale=x_scales[:, g, QUARTER * q : QUARTER * (q + 1)],
                             start=(g == 0),

@@ -231,23 +231,22 @@ def tile_hybrid_beamforming_precoder_s4_kernel(
             for s in (V, U, MINUS_V):
                 quantise_uv(m, s)
 
-        def passes(out, m, part, nh, first, last):
-            for s, k in (((U, "c"), (MINUS_V, "b")), ((U, "b"), (V, "c")))[part]:
-                nc.tensor.matmul_mx(
-                    out=out,
-                    lhsT=uv_codes[m][:, s, :].bitcast(FP8X4),
-                    lhsT_scale=uv_scales[m][:, s, :],
-                    rhs=w_codes[k, nh][:, first:last].bitcast(FP8X4),
-                    rhs_scale=w_scales[k, nh][:, first:last],
-                    start=(s == U),
-                    stop=(s != U),
-                )
-
-        def product(result, m, part, nh, copy):
-            number, bank = take_bank()
-            passes(bank[:], m, part, nh, 0, HALF)
-            copy(out=result, in_=bank[:])
-            line.append(number)
+        def products(m, part, targets):
+            banks = [take_bank() for unused in targets]
+            for s, k in (((U, "c"), (MINUS_V, "b")), ((V, "c"), (U, "b")))[part]:
+                for (number, bank), (result, nh, copy) in zip(banks, targets):
+                    nc.tensor.matmul_mx(
+                        out=bank[:],
+                        lhsT=uv_codes[m][:, s, :].bitcast(FP8X4),
+                        lhsT_scale=uv_scales[m][:, s, :],
+                        rhs=w_codes[k, nh].bitcast(FP8X4),
+                        rhs_scale=w_scales[k, nh],
+                        start=(k == "c"),
+                        stop=(k == "b"),
+                    )
+            for (number, bank), (result, nh, copy) in zip(banks, targets):
+                copy(out=result, in_=bank[:])
+                line.append(number)
 
         def store(result, part, m, blocks, first, last):
             out = (out_0, out_1)[part][P * m : P * (m + blocks), first:last]
@@ -255,13 +254,12 @@ def tile_hybrid_beamforming_precoder_s4_kernel(
 
         def half_rows(m, part, nh, copy=nc.scalar.copy):
             result = results.tile([P, 1, HALF], F32, name="half%d%d%d" % (m, part, nh))
-            product(result[:, 0, :], m, part, nh, copy)
+            products(m, part, [(result[:, 0, :], nh, copy)])
             store(result[:], part, m, 1, HALF * nh, HALF * (nh + 1))
 
         def full_rows(m, part, first_copy):
             result = results.tile([P, 1, ANTENNAS], F32, name="full%d%d" % (m, part))
-            product(result[:, 0, 0:HALF], m, part, 0, first_copy)
-            product(result[:, 0, HALF:ANTENNAS], m, part, 1, nc.scalar.copy)
+            products(m, part, [(result[:, 0, 0:HALF], 0, first_copy), (result[:, 0, HALF:ANTENNAS], 1, nc.scalar.copy)])
             store(result[:], part, m, 1, 0, ANTENNAS)
 
         sort_d(U)

@@ -47,7 +47,7 @@ def tile_hybrid_beamforming_precoder_s4_kernel(
 
         x_loads = ((0, QUARTER), (QUARTER, HALF), (HALF, SAMPLES))
         x_codes = [shifted(GROUPS, 2 * (last - first), U8, "x_codes%d" % first, 128) for first, last in x_loads]
-        x_scales = shifted(GROUPS, SAMPLES, U8, "x_scales", 192)
+        x_scales = [shifted(GROUPS, HALF, U8, "x_scales%d" % half, 192) for half in range(2)]
         d_raw = {s: tile([P, GROUPS, 2 * CHAINS], U8, "d_raw%d" % s) for s in (U, V)}
         d_scales_raw = tile([P, GROUPS, PHASES * CHAINS], U8, "d_scales_raw")
         d_codes = {s: tile([P, GROUPS, SLOTS, 2 * P], U8, "d_codes%d" % s) for s in (U, V)}
@@ -64,9 +64,12 @@ def tile_hybrid_beamforming_precoder_s4_kernel(
         w_scales = {(k, nh): shifted(1, HALF, U8, "scales_%s%d" % (k, nh), 192)[:, 0, :] for k, nh in halves}
 
         tanh_h = {(s, q): tile([P, 2, 2 * QUARTER], F32, "tanh_%d%d" % (s, q)) for s in (U, V) for q in range(4)}
-        uv_packed = {m: tile([P, 3, SLOTS * P], BF16, "uv_packed%d" % m) for m in range(BLOCKS)}
-        uv_codes = {m: tile([P, 3, P], U32, "uv_codes%d" % m) for m in range(BLOCKS)}
-        uv_scales = {m: shifted(3, P, U8, "uv_scales%d" % m, 64) for m in range(BLOCKS)}
+        batches = [(0, 2)] + [(m, 1) for m in range(2, BLOCKS)]
+        uv_packed = {m: tile([P, 3, blocks * SLOTS * P], BF16, "uv_packed%d" % m) for m, blocks in batches}
+        batch_codes = {m: tile([P, 3, blocks * P], U32, "uv_codes%d" % m) for m, blocks in batches}
+        batch_scales = {m: shifted(3, blocks * P, U8, "uv_scales%d" % m, 64) for m, blocks in batches}
+        uv_codes = {m + i: batch_codes[m][:, :, P * i : P * (i + 1)] for m, blocks in batches for i in range(blocks)}
+        uv_scales = {m + i: batch_scales[m][:, :, P * i : P * (i + 1)] for m, blocks in batches for i in range(blocks)}
 
         ctx.enter_context(tc.manual_schedule())
 
@@ -77,26 +80,29 @@ def tile_hybrid_beamforming_precoder_s4_kernel(
             line.remove(number)
             return number, psum.tile([P, HALF], F32, name="bank%d" % number)
 
-        def words(t, pattern):
-            return t[:].rearrange(pattern).bitcast(I32)
+        def flat(t, dtype):
+            pattern = "p a n -> p (a n)" if len(t.shape) == 3 else "p a b n -> p (a b n)"
+            return t[:].rearrange(pattern).bitcast(dtype)
 
-        nc.vector.memset(words(d_scales_raw, "p g n -> p (g n)"), 0)
-        nc.vector.memset(words(x_scales, "p g n -> p (g n)"), 0)
+        nc.vector.memset(flat(d_scales_raw, I32), 0)
+        nc.vector.memset(flat(x_scales[0], I32), 0)
         nc.vector.memset(gain_rows[:], 0.0)
 
-        nc.vector.memset(x_codes[2][:, 0, :].bitcast(I32), 0)
+        nc.vector.memset(x_codes[-1][:, 0, :].bitcast(I32), 0)
         nc.vector.memset(w_scales["b", 1][:].bitcast(I32), 0)
         warm_bank = psum.tile([P, HALF], F32, name="bank7")
         for unused in range(WARM_UP):
             nc.tensor.matmul_mx(
                 out=warm_bank[:],
-                lhsT=x_codes[2][:, 0, 0 : 2 * P].bitcast(FP4X4),
+                lhsT=x_codes[-1][:, 0, 0 : 2 * P].bitcast(FP4X4),
                 lhsT_scale=w_scales["b", 1][:, 0:P],
-                rhs=x_codes[2][:, 0, :].bitcast(FP4X4),
+                rhs=x_codes[-1][:, 0, :].bitcast(FP4X4),
                 rhs_scale=w_scales["b", 1][:],
                 start=True,
                 stop=True,
             )
+
+        nc.vector.memset(flat(x_scales[1], I32), 0)
 
         def load_codes(dst, src, first, last):
             by_partition = src.rearrange("g p x -> p g x")
@@ -108,11 +114,12 @@ def tile_hybrid_beamforming_precoder_s4_kernel(
         def load_d(s):
             load_codes(d_raw[s], dig_words, CHAINS * s, CHAINS * (s + 1))
 
-        def load_scales(dst, src, r):
-            nc.sync.dma_start(
-                out=dst[r:P:32, :, :].bitcast(I32),
-                in_=src[:, r:16:4, :].rearrange("g j n -> j g n").bitcast(I32),
-            )
+        def load_scales(dst, src, first, last):
+            for r in range(4):
+                nc.sync.dma_start(
+                    out=dst[r:P:32, :, :].bitcast(I32),
+                    in_=src[:, r:16:4, first:last].rearrange("g j n -> j g n").bitcast(I32),
+                )
 
         def load_gain():
             nc.sync.dma_start(
@@ -126,30 +133,29 @@ def tile_hybrid_beamforming_precoder_s4_kernel(
                 nc.sync.dma_start(out=w_raw[k, nh][:, t, :], in_=w[t][:, :, HALF * nh : HALF * (nh + 1)])
 
         load_x(0)
-        for r in range(4):
-            load_scales(d_scales_raw, dig_scales, r)
+        load_scales(d_scales_raw, dig_scales, 0, PHASES * CHAINS)
         load_d(U)
-        for r in range(4):
-            load_scales(x_scales, sym_scales, r)
+        load_scales(x_scales[0], sym_scales, 0, HALF)
         load_d(V)
         load_gain()
         load_w("c", 0)
         load_x(1)
-        load_w("b", 0)
+        load_scales(x_scales[1], sym_scales, HALF, SAMPLES)
         load_x(2)
+        load_w("b", 0)
         load_w("c", 1)
         load_w("b", 1)
 
-        def sort_d(s):
+        def deal_scales(s):
             nc.vector.tensor_copy(
-                out=words(d_scales[s], "p x n -> p (x n)").rearrange("p (g t q w) -> p g t q w", g=GROUPS, t=SLOTS, w=2),
-                in_=words(d_scales_raw, "p g n -> p (g n)").rearrange(
-                    "p (g s q t w) -> p s g t q w", g=GROUPS, s=PHASES, t=SLOTS, w=2
-                )[:, s],
+                out=flat(d_scales[s], I32).rearrange("p (g t q w) -> p g t q w", g=GROUPS, t=SLOTS, w=2),
+                in_=flat(d_scales_raw, I32).rearrange("p (g s q t w) -> p s g t q w", g=GROUPS, s=PHASES, t=SLOTS, w=2)[:, s],
             )
+
+        def deal_codes(s):
             nc.vector.tensor_copy(
-                out=words(d_codes[s], "p g t n -> p (g t n)").rearrange("p (g t q w) -> p g t q w", g=GROUPS, t=SLOTS, w=4),
-                in_=words(d_raw[s], "p g x -> p (g x)").rearrange("p (g q t w) -> p g t q w", g=GROUPS, t=SLOTS, w=4),
+                out=flat(d_codes[s], I32).rearrange("p (g t q w) -> p g t q w", g=GROUPS, t=SLOTS, w=4),
+                in_=flat(d_raw[s], I32).rearrange("p (g q t w) -> p g t q w", g=GROUPS, t=SLOTS, w=4),
             )
 
         def sort_gain():
@@ -164,32 +170,33 @@ def tile_hybrid_beamforming_precoder_s4_kernel(
         def gather_gain():
             nc.vector.tensor_copy(out=gain_cols[:].rearrange("p s t -> p (s t)"), in_=gain_turned[:, 0 : PHASES * P : 32])
 
-        sums, numbers = {}, {}
+        sums = {}
 
         def first_matmul(s, q):
-            piece = min(q, 2)
+            piece = [first <= QUARTER * q < last for first, last in x_loads].index(True)
             n = QUARTER * q - x_loads[piece][0]
             for pair in range(2):
-                numbers[s, q, pair], sums[s, q, pair] = take_bank()
+                sums[s, q, pair] = take_bank()
                 for j in range(2):
                     for g in range(GROUPS):
                         nc.tensor.matmul_mx(
-                            out=sums[s, q, pair][:, QUARTER * j : QUARTER * (j + 1)],
+                            out=sums[s, q, pair][1][:, QUARTER * j : QUARTER * (j + 1)],
                             lhsT=d_codes[s][:, g, 2 * pair + j, :].bitcast(FP4X4),
                             lhsT_scale=d_scales[s][:, SLOTS * g + 2 * pair + j, :],
                             rhs=x_codes[piece][:, g, 2 * n : 2 * (n + QUARTER)].bitcast(FP4X4),
-                            rhs_scale=x_scales[:, g, QUARTER * q : QUARTER * (q + 1)],
+                            rhs_scale=x_scales[q // 2][:, g, QUARTER * (q % 2) : QUARTER * (q % 2 + 1)],
                             start=(g == 0),
                             stop=(g == GROUPS - 1),
                         )
 
         def soft_limit(s, q, pair):
+            number, bank = sums[s, q, pair]
             nc.scalar.activation(
                 out=tanh_h[s, q][:, pair, :].rearrange("p (n j) -> p n j", j=2),
-                in_=sums[s, q, pair][:].rearrange("p (j n) -> p n j", j=2),
+                in_=bank[:].rearrange("p (j n) -> p n j", j=2),
                 func=TANH,
             )
-            line.append(numbers[s, q, pair])
+            line.append(number)
 
         def chains(s, q):
             first_matmul(s, q)
@@ -202,9 +209,6 @@ def tile_hybrid_beamforming_precoder_s4_kernel(
                 in_=w_raw[k, nh][:, :, first:last].rearrange("p t (c i) -> p c t i", i=4),
             )
 
-        def negate_v(m):
-            nc.vector.tensor_scalar(out=uv_packed[m][:, MINUS_V, :], in0=uv_packed[m][:, V, :], scalar1=-1.0, scalar2=None, op0=MULT)
-
         def quantise_w(k, nh, first=0, last=HALF):
             nc.vector.quantize_mx(
                 out=w_codes[k, nh][:, first:last].bitcast(FP8X4),
@@ -214,15 +218,19 @@ def tile_hybrid_beamforming_precoder_s4_kernel(
 
         def times_gain(s, m):
             n = P * (m % 2)
+            samples = P * dict(batches)[m]
             nc.vector.tensor_tensor(
                 out=uv_packed[m][:, s, :].rearrange("p (n u j) -> p n u j", u=2, j=2),
-                in0=tanh_h[s, m // 2][:].rearrange("p u (n j) -> p n u j", j=2)[:, n : n + P],
-                in1=gain_cols[:, s, :].rearrange("p (u j) -> p u j", j=2).unsqueeze(1).to_broadcast([P, P, 2, 2]),
+                in0=tanh_h[s, m // 2][:].rearrange("p u (n j) -> p n u j", j=2)[:, n : n + samples],
+                in1=gain_cols[:, s, :].rearrange("p (u j) -> p u j", j=2).unsqueeze(1).to_broadcast([P, samples, 2, 2]),
                 op=MULT,
             )
 
+        def negate_v(m):
+            nc.vector.tensor_scalar(out=uv_packed[m][:, MINUS_V, :], in0=uv_packed[m][:, V, :], scalar1=-1.0, scalar2=None, op0=MULT)
+
         def quantise_uv(m, s):
-            nc.vector.quantize_mx(out=uv_codes[m][:, s, :].bitcast(FP8X4), scales=uv_scales[m][:, s, :], in_=uv_packed[m][:, s, :])
+            nc.vector.quantize_mx(out=batch_codes[m][:, s, :].bitcast(FP8X4), scales=batch_scales[m][:, s, :], in_=uv_packed[m][:, s, :])
 
         def block(m):
             times_gain(V, m)
@@ -231,92 +239,111 @@ def tile_hybrid_beamforming_precoder_s4_kernel(
             for s in (V, U, MINUS_V):
                 quantise_uv(m, s)
 
-        def products(m, part, targets):
-            banks = [take_bank() for unused in targets]
-            for s, k in (((U, "c"), (MINUS_V, "b")), ((V, "c"), (U, "b")))[part]:
-                for (number, bank), (result, nh, copy) in zip(banks, targets):
-                    nc.tensor.matmul_mx(
-                        out=bank[:],
-                        lhsT=uv_codes[m][:, s, :].bitcast(FP8X4),
-                        lhsT_scale=uv_scales[m][:, s, :],
-                        rhs=w_codes[k, nh].bitcast(FP8X4),
-                        rhs_scale=w_scales[k, nh],
-                        start=(k == "c"),
-                        stop=(k == "b"),
-                    )
-            for (number, bank), (result, nh, copy) in zip(banks, targets):
-                copy(out=result, in_=bank[:])
-                line.append(number)
+        def passes(out, m, part, nh, first, last, turned):
+            pairs = (((U, "c"), (MINUS_V, "b")), ((U, "b"), (V, "c")))[part]
+            for opens, (s, k) in zip((True, False), pairs[::-1] if turned else pairs):
+                nc.tensor.matmul_mx(
+                    out=out,
+                    lhsT=uv_codes[m][:, s, :].bitcast(FP8X4),
+                    lhsT_scale=uv_scales[m][:, s, :],
+                    rhs=w_codes[k, nh][:, first:last].bitcast(FP8X4),
+                    rhs_scale=w_scales[k, nh][:, first:last],
+                    start=opens,
+                    stop=not opens,
+                )
 
-        def store(result, part, m, blocks, first, last):
-            out = (out_0, out_1)[part][P * m : P * (m + blocks), first:last]
-            nc.sync.dma_start(out=out.rearrange("(j p) n -> p j n", j=blocks), in_=result)
+        def product(result, m, part, nh, copy):
+            number, bank = take_bank()
+            passes(bank[:], m, part, nh, 0, HALF, nh == 1)
+            copy(out=result, in_=bank[:])
+            line.append(number)
 
-        def half_rows(m, part, nh, copy=nc.scalar.copy):
-            result = results.tile([P, 1, HALF], F32, name="half%d%d%d" % (m, part, nh))
-            products(m, part, [(result[:, 0, :], nh, copy)])
-            store(result[:], part, m, 1, HALF * nh, HALF * (nh + 1))
+        def quarter_rows(m, first, copy):
+            result = results.tile([P, 2, QUARTER], F32, name="quarter%d_%d" % (m, first))
+            number, bank = take_bank()
+            for part in (IM, RE):
+                passes(bank[:, QUARTER * part : QUARTER * (part + 1)], m, part, 1, first, first + QUARTER, part == IM)
+            copy(out=result[:].rearrange("p part n -> p (part n)"), in_=bank[:])
+            line.append(number)
+            for part in (IM, RE):
+                store(result[:, part, :], part, m, HALF + first, HALF + first + QUARTER)
 
-        def full_rows(m, part, first_copy):
-            result = results.tile([P, 1, ANTENNAS], F32, name="full%d%d" % (m, part))
-            products(m, part, [(result[:, 0, 0:HALF], 0, first_copy), (result[:, 0, HALF:ANTENNAS], 1, nc.scalar.copy)])
-            store(result[:], part, m, 1, 0, ANTENNAS)
+        def store(result, part, m, first, last):
+            nc.sync.dma_start(out=(out_0, out_1)[part][P * m : P * (m + 1), first:last], in_=result)
 
-        sort_d(U)
+        def half_row(m, part, nh, copy=nc.scalar.copy):
+            result = results.tile([P, HALF], F32, name="half%d%d%d" % (m, part, nh))
+            product(result[:], m, part, nh, copy)
+            store(result[:], part, m, HALF * nh, HALF * (nh + 1))
+
+        def full_row(m, part, first_copy, second_copy):
+            result = results.tile([P, ANTENNAS], F32, name="full%d%d" % (m, part))
+            product(result[:, 0:HALF], m, part, 0, first_copy)
+            product(result[:, HALF:ANTENNAS], m, part, 1, second_copy)
+            store(result[:], part, m, 0, ANTENNAS)
+
+        on_scalar, on_vector = nc.scalar.copy, nc.vector.tensor_copy
+
+        deal_scales(U)
+        deal_codes(U)
         chains(U, 0)
-        sort_d(V)
+        deal_scales(V)
+        deal_codes(V)
         chains(V, 0)
         chains(U, 1)
         chains(V, 1)
         sort_gain()
         turn_gain()
-        pack_w(nc.vector.tensor_copy, "c", 0, 0, QUARTER)
+        pack_w(on_vector, "c", 0, 0, 256)
         gather_gain()
-        pack_w(nc.vector.tensor_copy, "c", 0, QUARTER, HALF)
+        pack_w(on_vector, "c", 0, 256, 512)
         times_gain(U, 0)
         quantise_w("c", 0)
         times_gain(V, 0)
-        pack_w(nc.vector.tensor_copy, "b", 0)
+        pack_w(on_vector, "b", 0)
         negate_v(0)
         quantise_uv(0, V)
         quantise_uv(0, U)
         quantise_w("b", 0)
         quantise_uv(0, MINUS_V)
         chains(U, 2)
-        pack_w(nc.scalar.copy, "c", 1)
+        pack_w(on_scalar, "c", 1)
         first_matmul(V, 2)
         first_matmul(U, 3)
-
-        half_rows(0, IM, 0)
-        half_rows(0, RE, 0)
         soft_limit(V, 2, 0)
         soft_limit(V, 2, 1)
-        block(1)
-        half_rows(1, IM, 0)
-        half_rows(1, RE, 0)
         first_matmul(V, 3)
+        half_row(0, IM, 0, on_scalar)
+        half_row(0, RE, 0, on_scalar)
+        half_row(1, IM, 0, on_scalar)
+        half_row(1, RE, 0, on_scalar)
         soft_limit(U, 3, 0)
-
-        pack_w(nc.vector.tensor_copy, "b", 1)
+        pack_w(on_vector, "b", 1)
         quantise_w("c", 1)
         quantise_w("b", 1)
-        for m in (0, 1):
-            half_rows(m, IM, 1)
-            half_rows(m, RE, 1)
+        half_row(0, IM, 1, on_scalar)
+        half_row(0, RE, 1, on_scalar)
+        half_row(1, IM, 1, on_scalar)
+        half_row(1, RE, 1, on_scalar)
         block(2)
-
-        waiting = {(2, IM): (U, 3, 1), (2, RE): (V, 3, 0), (3, RE): (V, 3, 1)}
-        last_rows = ((BLOCKS - 2, RE), (BLOCKS - 1, IM), (BLOCKS - 1, RE))
-        for m in range(2, BLOCKS):
-            if m + 1 < BLOCKS:
-                block(m + 1)
-            for part in (IM, RE):
-                if (m, part) in waiting:
-                    soft_limit(*waiting[m, part])
-                by_vector = (m, part) in waiting or (m, part) in last_rows
-                first_copy = nc.vector.tensor_copy if by_vector else nc.scalar.copy
-                if (m, part) == last_rows[-1]:
-                    half_rows(m, part, 0, first_copy)
-                    half_rows(m, part, 1)
-                else:
-                    full_rows(m, part, first_copy)
+        block(3)
+        soft_limit(U, 3, 1)
+        full_row(2, IM, on_vector, on_scalar)
+        soft_limit(V, 3, 0)
+        full_row(2, RE, on_vector, on_scalar)
+        block(4)
+        full_row(3, IM, on_scalar, on_scalar)
+        soft_limit(V, 3, 1)
+        full_row(3, RE, on_vector, on_scalar)
+        block(5)
+        full_row(4, IM, on_scalar, on_scalar)
+        full_row(4, RE, on_scalar, on_scalar)
+        block(6)
+        full_row(5, IM, on_scalar, on_scalar)
+        full_row(5, RE, on_scalar, on_scalar)
+        block(7)
+        full_row(6, IM, on_scalar, on_scalar)
+        full_row(6, RE, on_vector, on_scalar)
+        full_row(7, IM, on_vector, on_scalar)
+        half_row(7, RE, 0, on_vector)
+        half_row(7, RE, 1, on_scalar)

@@ -1,6 +1,7 @@
 from contextlib import ExitStack
 
 import concourse.mybir as mybir
+from concourse.masks import make_identity
 
 SAMPLES, STREAMS, CHAINS, ANTENNAS = 1024, 1024, 512, 1024
 FLOPS = 2 * SAMPLES * STREAMS * 2 * CHAINS + 4 * 2 * SAMPLES * CHAINS * ANTENNAS
@@ -14,6 +15,7 @@ FP4X4 = mybir.dt.float4_e2m1fn_x4
 FP8X4 = mybir.dt.float8_e4m3fn_x4
 TANH = mybir.ActivationFunctionType.Tanh
 MULT = mybir.AluOpType.mult
+ADD = mybir.AluOpType.add
 
 P = 128
 SLOTS = 4
@@ -26,7 +28,7 @@ U, V, MINUS_V = 0, 1, 2
 RE, IM = 0, 1
 BANKS = 8
 BLOCKS = SAMPLES // P
-WARM_UP = 6
+WARM_UP = 5
 
 
 def tile_hybrid_beamforming_precoder_s4_kernel(
@@ -45,21 +47,22 @@ def tile_hybrid_beamforming_precoder_s4_kernel(
             whole = tile([P, shift + rows * width], dtype, name)
             return whole[:, shift:].rearrange("p (r n) -> p r n", r=rows)
 
-        x_loads = ((0, QUARTER), (QUARTER, HALF), (HALF, SAMPLES))
+        x_loads = tuple((QUARTER * q, QUARTER * (q + 1)) for q in range(4))
         x_codes = [shifted(GROUPS, 2 * (last - first), U8, "x_codes%d" % first, 128) for first, last in x_loads]
         x_scales = [shifted(GROUPS, HALF, U8, "x_scales%d" % half, 192) for half in range(2)]
         d_raw = {s: tile([P, GROUPS, 2 * CHAINS], U8, "d_raw%d" % s) for s in (U, V)}
         d_scales_raw = tile([P, GROUPS, PHASES * CHAINS], U8, "d_scales_raw")
         d_codes = {s: tile([P, GROUPS, SLOTS, 2 * P], U8, "d_codes%d" % s) for s in (U, V)}
         d_scales = {s: shifted(GROUPS * SLOTS, P, U8, "d_scales%d" % s, 64) for s in (U, V)}
-        gain_rows = tile([P, PHASES * P], BF16, "gain_rows")
-        gain_sorted = tile([P, PHASES * P], BF16, "gain_sorted")
-        gain_turned = tile([P, PHASES * P], BF16, "gain_turned")
+        gain_rows = tile([P, CHAINS], BF16, "gain_rows")
+        gain_sorted = tile([P, CHAINS], BF16, "gain_sorted")
+        identity = tile([P, P], BF16, "identity")
         gain_cols = tile([P, PHASES, SLOTS], F32, "gain_cols")
 
         halves = [(k, nh) for k in ("c", "b") for nh in range(2)]
         w_raw = {(k, nh): tile([P, SLOTS, HALF], BF16, "raw_%s%d" % (k, nh)) for k, nh in halves}
         w_packed = {(k, nh): tile([P, SLOTS * HALF], BF16, "packed_%s%d" % (k, nh)) for k, nh in halves}
+        w_packed["b", 0] = w_packed["c", 0]
         w_codes = {(k, nh): shifted(1, HALF, U32, "codes_%s%d" % (k, nh), 32)[:, 0, :] for k, nh in halves}
         w_scales = {(k, nh): shifted(1, HALF, U8, "scales_%s%d" % (k, nh), 192)[:, 0, :] for k, nh in halves}
 
@@ -85,10 +88,8 @@ def tile_hybrid_beamforming_precoder_s4_kernel(
             return t[:].rearrange(pattern).bitcast(dtype)
 
         nc.vector.memset(flat(d_scales_raw, I32), 0)
-        nc.vector.memset(flat(x_scales[0], I32), 0)
-        nc.vector.memset(gain_rows[:], 0.0)
 
-        nc.vector.memset(x_codes[-1][:, 0, :].bitcast(I32), 0)
+        nc.vector.memset(flat(x_codes[-1], I32), 0)
         nc.vector.memset(w_scales["b", 1][:].bitcast(I32), 0)
         warm_bank = psum.tile([P, HALF], F32, name="bank7")
         for unused in range(WARM_UP):
@@ -96,13 +97,17 @@ def tile_hybrid_beamforming_precoder_s4_kernel(
                 out=warm_bank[:],
                 lhsT=x_codes[-1][:, 0, 0 : 2 * P].bitcast(FP4X4),
                 lhsT_scale=w_scales["b", 1][:, 0:P],
-                rhs=x_codes[-1][:, 0, :].bitcast(FP4X4),
+                rhs=flat(x_codes[-1], U8).bitcast(FP4X4),
                 rhs_scale=w_scales["b", 1][:],
                 start=True,
                 stop=True,
             )
 
+        nc.vector.memset(gain_rows[:], 0.0)
+        nc.vector.memset(flat(x_scales[0], I32), 0)
         nc.vector.memset(flat(x_scales[1], I32), 0)
+        nc.vector.memset(identity[:], 0.0)
+        make_identity(nc, identity[:], nomemset=True)
 
         def load_codes(dst, src, first, last):
             by_partition = src.rearrange("g p x -> p g x")
@@ -122,10 +127,7 @@ def tile_hybrid_beamforming_precoder_s4_kernel(
                 )
 
         def load_gain():
-            nc.sync.dma_start(
-                out=gain_rows[0:P:32, :].rearrange("j (s n) -> j s n", s=PHASES),
-                in_=gain.rearrange("(s j n) -> j s n", s=PHASES, j=4),
-            )
+            nc.sync.dma_start(out=gain_rows[0:PHASES, :], in_=gain.rearrange("(s n) -> s n", s=PHASES))
 
         def load_w(k, nh):
             w = (cosw if k == "c" else sinw).rearrange("(q t r) n -> t q r n", t=SLOTS, r=RUN)
@@ -134,15 +136,16 @@ def tile_hybrid_beamforming_precoder_s4_kernel(
 
         load_x(0)
         load_scales(d_scales_raw, dig_scales, 0, PHASES * CHAINS)
+        load_gain()
         load_d(U)
         load_scales(x_scales[0], sym_scales, 0, HALF)
         load_d(V)
-        load_gain()
         load_w("c", 0)
         load_x(1)
+        load_w("b", 0)
         load_scales(x_scales[1], sym_scales, HALF, SAMPLES)
         load_x(2)
-        load_w("b", 0)
+        load_x(3)
         load_w("c", 1)
         load_w("b", 1)
 
@@ -158,17 +161,22 @@ def tile_hybrid_beamforming_precoder_s4_kernel(
                 in_=flat(d_raw[s], I32).rearrange("p (g q t w) -> p g t q w", g=GROUPS, t=SLOTS, w=4),
             )
 
+        gain_number, gain_bank = BANKS - 1, psum.tile([P, SLOTS * P], BF16, name="bank7")
+        line.remove(gain_number)
+        gain_in_bank = gain_bank[:].rearrange("p (t s) -> p s t", t=SLOTS)
+
         def sort_gain():
             nc.vector.tensor_copy(
-                out=gain_sorted[:].rearrange("p (s t q r) -> p s t q r", s=PHASES, t=SLOTS, r=RUN),
-                in_=gain_rows[:].rearrange("p (s q t r) -> p s t q r", s=PHASES, t=SLOTS, r=RUN),
+                out=gain_sorted[:].rearrange("p (t q r) -> p t q r", t=SLOTS, r=RUN),
+                in_=gain_rows[:].rearrange("p (q t r) -> p t q r", t=SLOTS, r=RUN),
             )
 
         def turn_gain():
-            nc.vector.transpose(out=gain_turned[:], in_=gain_sorted[:])
+            for t in range(SLOTS):
+                nc.tensor.transpose(gain_bank[:, P * t : P * (t + 1)], gain_sorted[:, P * t : P * (t + 1)], identity[:])
 
         def gather_gain():
-            nc.vector.tensor_copy(out=gain_cols[:].rearrange("p s t -> p (s t)"), in_=gain_turned[:, 0 : PHASES * P : 32])
+            nc.scalar.copy(out=gain_cols[:], in_=gain_in_bank[:, 0:PHASES, :])
 
         sums = {}
 
@@ -209,6 +217,16 @@ def tile_hybrid_beamforming_precoder_s4_kernel(
                 in_=w_raw[k, nh][:, :, first:last].rearrange("p t (c i) -> p c t i", i=4),
             )
 
+        def pack_on_gpsimd(k, nh, first, last):
+            nc.gpsimd.tensor_scalar(
+                out=w_packed[k, nh][:, SLOTS * first : SLOTS * last].rearrange("p (n t) -> p n t", t=SLOTS),
+                in0=w_raw[k, nh][:, :, first:last].rearrange("p t n -> p n t"),
+                scalar1=1.0,
+                scalar2=0.0,
+                op0=MULT,
+                op1=ADD,
+            )
+
         def quantise_w(k, nh, first=0, last=HALF):
             nc.vector.quantize_mx(
                 out=w_codes[k, nh][:, first:last].bitcast(FP8X4),
@@ -219,10 +237,11 @@ def tile_hybrid_beamforming_precoder_s4_kernel(
         def times_gain(s, m):
             n = P * (m % 2)
             samples = P * dict(batches)[m]
+            gains = gain_in_bank if m == 0 else gain_cols
             nc.vector.tensor_tensor(
                 out=uv_packed[m][:, s, :].rearrange("p (n u j) -> p n u j", u=2, j=2),
                 in0=tanh_h[s, m // 2][:].rearrange("p u (n j) -> p n u j", j=2)[:, n : n + samples],
-                in1=gain_cols[:, s, :].rearrange("p (u j) -> p u j", j=2).unsqueeze(1).to_broadcast([P, samples, 2, 2]),
+                in1=gains[:, s, :].rearrange("p (u j) -> p u j", j=2).unsqueeze(1).to_broadcast([P, samples, 2, 2]),
                 op=MULT,
             )
 
@@ -258,16 +277,6 @@ def tile_hybrid_beamforming_precoder_s4_kernel(
             copy(out=result, in_=bank[:])
             line.append(number)
 
-        def quarter_rows(m, first, copy):
-            result = results.tile([P, 2, QUARTER], F32, name="quarter%d_%d" % (m, first))
-            number, bank = take_bank()
-            for part in (IM, RE):
-                passes(bank[:, QUARTER * part : QUARTER * (part + 1)], m, part, 1, first, first + QUARTER, part == IM)
-            copy(out=result[:].rearrange("p part n -> p (part n)"), in_=bank[:])
-            line.append(number)
-            for part in (IM, RE):
-                store(result[:, part, :], part, m, HALF + first, HALF + first + QUARTER)
-
         def store(result, part, m, first, last):
             nc.sync.dma_start(out=(out_0, out_1)[part][P * m : P * (m + 1), first:last], in_=result)
 
@@ -284,7 +293,10 @@ def tile_hybrid_beamforming_precoder_s4_kernel(
 
         on_scalar, on_vector = nc.scalar.copy, nc.vector.tensor_copy
 
+        sort_gain()
         deal_scales(U)
+        turn_gain()
+        gather_gain()
         deal_codes(U)
         chains(U, 0)
         deal_scales(V)
@@ -292,32 +304,29 @@ def tile_hybrid_beamforming_precoder_s4_kernel(
         chains(V, 0)
         chains(U, 1)
         chains(V, 1)
-        sort_gain()
-        turn_gain()
-        pack_w(on_vector, "c", 0, 0, 256)
-        gather_gain()
-        pack_w(on_vector, "c", 0, 256, 512)
+        pack_w(on_vector, "c", 0, 0, 384)
+        pack_w(on_vector, "c", 0, 384, 512)
+        quantise_w("c", 0, 0, 384)
+        quantise_w("c", 0, 384, 512)
+        pack_on_gpsimd("b", 0, 0, 384)
         times_gain(U, 0)
-        quantise_w("c", 0)
         times_gain(V, 0)
-        pack_w(on_vector, "b", 0)
+        pack_w(on_vector, "b", 0, 384, 512)
+        line.append(gain_number)
         negate_v(0)
         quantise_uv(0, V)
         quantise_uv(0, U)
         quantise_w("b", 0)
         quantise_uv(0, MINUS_V)
         chains(U, 2)
-        pack_w(on_scalar, "c", 1)
-        first_matmul(V, 2)
-        first_matmul(U, 3)
-        soft_limit(V, 2, 0)
-        soft_limit(V, 2, 1)
-        first_matmul(V, 3)
+        chains(V, 2)
+        chains(U, 3)
+        chains(V, 3)
         half_row(0, IM, 0, on_scalar)
         half_row(0, RE, 0, on_scalar)
         half_row(1, IM, 0, on_scalar)
         half_row(1, RE, 0, on_scalar)
-        soft_limit(U, 3, 0)
+        pack_w(on_vector, "c", 1, 0, 512)
         pack_w(on_vector, "b", 1)
         quantise_w("c", 1)
         quantise_w("b", 1)
@@ -327,14 +336,11 @@ def tile_hybrid_beamforming_precoder_s4_kernel(
         half_row(1, RE, 1, on_scalar)
         block(2)
         block(3)
-        soft_limit(U, 3, 1)
-        full_row(2, IM, on_vector, on_scalar)
-        soft_limit(V, 3, 0)
-        full_row(2, RE, on_vector, on_scalar)
+        full_row(2, IM, on_scalar, on_scalar)
+        full_row(2, RE, on_scalar, on_scalar)
         block(4)
         full_row(3, IM, on_scalar, on_scalar)
-        soft_limit(V, 3, 1)
-        full_row(3, RE, on_vector, on_scalar)
+        full_row(3, RE, on_scalar, on_scalar)
         block(5)
         full_row(4, IM, on_scalar, on_scalar)
         full_row(4, RE, on_scalar, on_scalar)
@@ -345,5 +351,4 @@ def tile_hybrid_beamforming_precoder_s4_kernel(
         full_row(6, IM, on_scalar, on_scalar)
         full_row(6, RE, on_vector, on_scalar)
         full_row(7, IM, on_vector, on_scalar)
-        half_row(7, RE, 0, on_vector)
-        half_row(7, RE, 1, on_scalar)
+        full_row(7, RE, on_vector, on_scalar)

@@ -52,9 +52,9 @@ def tile_hybrid_beamforming_precoder_s4_kernel(
         x_scales = [shifted(GROUPS, HALF, U8, "x_scales%d" % half, 192) for half in range(2)]
         d_raw = {s: tile([P, GROUPS, 2 * CHAINS], U8, "d_raw%d" % s) for s in (U, V)}
         d_scales_raw = tile([P, GROUPS, PHASES * CHAINS], U8, "d_scales_raw")
-        d_codes = {s: tile([P, GROUPS, SLOTS, 2 * P], U8, "d_codes%d" % s) for s in (U, V)}
+        d_codes = {s: [tile([P, 2, GROUPS, 2 * P], U8, "d_codes%d%d" % (s, pair)) for pair in range(2)] for s in (U, V)}
         d_scales = {s: shifted(GROUPS * SLOTS, P, U8, "d_scales%d" % s, 64) for s in (U, V)}
-        gain_rows = tile([P, CHAINS], BF16, "gain_rows")
+        gain_rows = tile([PHASES, CHAINS], BF16, "gain_rows")
         gain_sorted = tile([P, CHAINS], BF16, "gain_sorted")
         identity = tile([P, P], BF16, "identity")
         gain_cols = tile([P, PHASES, SLOTS], F32, "gain_cols")
@@ -103,9 +103,9 @@ def tile_hybrid_beamforming_precoder_s4_kernel(
                 stop=True,
             )
 
-        nc.vector.memset(gain_rows[:], 0.0)
         nc.vector.memset(flat(x_scales[0], I32), 0)
         nc.vector.memset(flat(x_scales[1], I32), 0)
+        nc.vector.memset(gain_sorted[:], 0.0)
         nc.vector.memset(identity[:], 0.0)
         make_identity(nc, identity[:], nomemset=True)
 
@@ -127,7 +127,7 @@ def tile_hybrid_beamforming_precoder_s4_kernel(
                 )
 
         def load_gain():
-            nc.sync.dma_start(out=gain_rows[0:PHASES, :], in_=gain.rearrange("(s n) -> s n", s=PHASES))
+            nc.sync.dma_start(out=gain_rows[:], in_=gain.rearrange("(s n) -> s n", s=PHASES))
 
         def load_w(k, nh):
             w = (cosw if k == "c" else sinw).rearrange("(q t r) n -> t q r n", t=SLOTS, r=RUN)
@@ -135,8 +135,8 @@ def tile_hybrid_beamforming_precoder_s4_kernel(
                 nc.sync.dma_start(out=w_raw[k, nh][:, t, :], in_=w[t][:, :, HALF * nh : HALF * (nh + 1)])
 
         load_x(0)
-        load_scales(d_scales_raw, dig_scales, 0, PHASES * CHAINS)
         load_gain()
+        load_scales(d_scales_raw, dig_scales, 0, PHASES * CHAINS)
         load_d(U)
         load_scales(x_scales[0], sym_scales, 0, HALF)
         load_d(V)
@@ -156,10 +156,11 @@ def tile_hybrid_beamforming_precoder_s4_kernel(
             )
 
         def deal_codes(s):
-            nc.vector.tensor_copy(
-                out=flat(d_codes[s], I32).rearrange("p (g t q w) -> p g t q w", g=GROUPS, t=SLOTS, w=4),
-                in_=flat(d_raw[s], I32).rearrange("p (g q t w) -> p g t q w", g=GROUPS, t=SLOTS, w=4),
-            )
+            for pair in range(2):
+                nc.vector.tensor_copy(
+                    out=flat(d_codes[s][pair], I32).rearrange("p (j g q w) -> p j g q w", j=2, g=GROUPS, w=4),
+                    in_=flat(d_raw[s], I32).rearrange("p (g q u j w) -> p u j g q w", g=GROUPS, u=2, j=2, w=4)[:, pair],
+                )
 
         gain_number, gain_bank = BANKS - 1, psum.tile([P, SLOTS * P], BF16, name="bank7")
         line.remove(gain_number)
@@ -167,7 +168,7 @@ def tile_hybrid_beamforming_precoder_s4_kernel(
 
         def sort_gain():
             nc.vector.tensor_copy(
-                out=gain_sorted[:].rearrange("p (t q r) -> p t q r", t=SLOTS, r=RUN),
+                out=gain_sorted[0:PHASES, :].rearrange("p (t q r) -> p t q r", t=SLOTS, r=RUN),
                 in_=gain_rows[:].rearrange("p (q t r) -> p t q r", t=SLOTS, r=RUN),
             )
 
@@ -189,7 +190,7 @@ def tile_hybrid_beamforming_precoder_s4_kernel(
                     for g in range(GROUPS):
                         nc.tensor.matmul_mx(
                             out=sums[s, q, pair][1][:, QUARTER * j : QUARTER * (j + 1)],
-                            lhsT=d_codes[s][:, g, 2 * pair + j, :].bitcast(FP4X4),
+                            lhsT=d_codes[s][pair][:, j, g, :].bitcast(FP4X4),
                             lhsT_scale=d_scales[s][:, SLOTS * g + 2 * pair + j, :],
                             rhs=x_codes[piece][:, g, 2 * n : 2 * (n + QUARTER)].bitcast(FP4X4),
                             rhs_scale=x_scales[q // 2][:, g, QUARTER * (q % 2) : QUARTER * (q % 2 + 1)],
@@ -309,9 +310,9 @@ def tile_hybrid_beamforming_precoder_s4_kernel(
         quantise_w("c", 0, 0, 384)
         quantise_w("c", 0, 384, 512)
         pack_on_gpsimd("b", 0, 0, 384)
-        times_gain(U, 0)
+        pack_w(on_scalar, "b", 0, 384, 512)
         times_gain(V, 0)
-        pack_w(on_vector, "b", 0, 384, 512)
+        times_gain(U, 0)
         line.append(gain_number)
         negate_v(0)
         quantise_uv(0, V)

@@ -10,6 +10,7 @@ F32 = mybir.dt.float32
 BF16 = mybir.dt.bfloat16
 I32 = mybir.dt.int32
 U32 = mybir.dt.uint32
+U16 = mybir.dt.uint16
 U8 = mybir.dt.uint8
 FP4X4 = mybir.dt.float4_e2m1fn_x4
 FP8X4 = mybir.dt.float8_e4m3fn_x4
@@ -19,7 +20,6 @@ ADD = mybir.AluOpType.add
 
 P = 128
 SLOTS = 4
-RUN = 8
 GROUPS = STREAMS // 512
 HALF = 512
 QUARTER = 256
@@ -28,7 +28,9 @@ U, V, MINUS_V = 0, 1, 2
 RE, IM = 0, 1
 BANKS = 8
 BLOCKS = SAMPLES // P
-WARM_UP = 5
+EARLY = 2
+SHARE = 384
+WARM_UP = 6
 
 
 def tile_hybrid_beamforming_precoder_s4_kernel(
@@ -47,13 +49,12 @@ def tile_hybrid_beamforming_precoder_s4_kernel(
             whole = tile([P, shift + rows * width], dtype, name)
             return whole[:, shift:].rearrange("p (r n) -> p r n", r=rows)
 
-        x_loads = tuple((QUARTER * q, QUARTER * (q + 1)) for q in range(4))
-        x_codes = [shifted(GROUPS, 2 * (last - first), U8, "x_codes%d" % first, 128) for first, last in x_loads]
+        x_codes = [shifted(GROUPS, 2 * QUARTER, U8, "x_codes%d" % q, 128) for q in range(4)]
         x_scales = [shifted(GROUPS, HALF, U8, "x_scales%d" % half, 192) for half in range(2)]
         d_raw = {s: tile([P, GROUPS, 2 * CHAINS], U8, "d_raw%d" % s) for s in (U, V)}
         d_scales_raw = tile([P, GROUPS, PHASES * CHAINS], U8, "d_scales_raw")
         d_codes = {s: [tile([P, 2, GROUPS, 2 * P], U8, "d_codes%d%d" % (s, pair)) for pair in range(2)] for s in (U, V)}
-        d_scales = {s: shifted(GROUPS * SLOTS, P, U8, "d_scales%d" % s, 64) for s in (U, V)}
+        d_scales = {s: [shifted(2 * GROUPS, P, U8, "d_scales%d%d" % (s, pair), 64) for pair in range(2)] for s in (U, V)}
         gain_rows = tile([PHASES, CHAINS], BF16, "gain_rows")
         gain_sorted = tile([P, CHAINS], BF16, "gain_sorted")
         identity = tile([P, P], BF16, "identity")
@@ -61,18 +62,19 @@ def tile_hybrid_beamforming_precoder_s4_kernel(
 
         halves = [(k, nh) for k in ("c", "b") for nh in range(2)]
         w_raw = {(k, nh): tile([P, SLOTS, HALF], BF16, "raw_%s%d" % (k, nh)) for k, nh in halves}
-        w_packed = {(k, nh): tile([P, SLOTS * HALF], BF16, "packed_%s%d" % (k, nh)) for k, nh in halves}
-        w_packed["b", 0] = w_packed["c", 0]
+        packed_first = tile([P, SLOTS * HALF], BF16, "packed_first")
+        w_packed = {(k, nh): tile([P, SLOTS * HALF], BF16, "packed_%s" % k) if nh else packed_first for k, nh in halves}
         w_codes = {(k, nh): shifted(1, HALF, U32, "codes_%s%d" % (k, nh), 32)[:, 0, :] for k, nh in halves}
         w_scales = {(k, nh): shifted(1, HALF, U8, "scales_%s%d" % (k, nh), 192)[:, 0, :] for k, nh in halves}
 
         tanh_h = {(s, q): tile([P, 2, 2 * QUARTER], F32, "tanh_%d%d" % (s, q)) for s in (U, V) for q in range(4)}
-        batches = [(0, 2)] + [(m, 1) for m in range(2, BLOCKS)]
-        uv_packed = {m: tile([P, 3, blocks * SLOTS * P], BF16, "uv_packed%d" % m) for m, blocks in batches}
-        batch_codes = {m: tile([P, 3, blocks * P], U32, "uv_codes%d" % m) for m, blocks in batches}
-        batch_scales = {m: shifted(3, blocks * P, U8, "uv_scales%d" % m, 64) for m, blocks in batches}
-        uv_codes = {m + i: batch_codes[m][:, :, P * i : P * (i + 1)] for m, blocks in batches for i in range(blocks)}
-        uv_scales = {m + i: batch_scales[m][:, :, P * i : P * (i + 1)] for m, blocks in batches for i in range(blocks)}
+        batches = dict([(0, EARLY)] + [(m, 1) for m in range(EARLY, BLOCKS)])
+        uv_packed = {m: tile([P, 3, blocks * SLOTS * P], BF16, "uv_packed%d" % m) for m, blocks in batches.items()}
+        batch_codes = {m: tile([P, 3, blocks * P], U32, "uv_codes%d" % m) for m, blocks in batches.items()}
+        batch_scales = {m: shifted(3, blocks * P, U8, "uv_scales%d" % m, 64) for m, blocks in batches.items()}
+        places = [(m, i) for m, blocks in batches.items() for i in range(blocks)]
+        uv_codes = {m + i: batch_codes[m][:, :, P * i : P * (i + 1)] for m, i in places}
+        uv_scales = {m + i: batch_scales[m][:, :, P * i : P * (i + 1)] for m, i in places}
 
         ctx.enter_context(tc.manual_schedule())
 
@@ -113,8 +115,8 @@ def tile_hybrid_beamforming_precoder_s4_kernel(
             by_partition = src.rearrange("g p x -> p g x")
             nc.sync.dma_start(out=dst[:].bitcast(I32), in_=by_partition[:, :, 2 * first : 2 * last].bitcast(I32))
 
-        def load_x(piece):
-            load_codes(x_codes[piece], sym_words, *x_loads[piece])
+        def load_x(q):
+            load_codes(x_codes[q], sym_words, QUARTER * q, QUARTER * (q + 1))
 
         def load_d(s):
             load_codes(d_raw[s], dig_words, CHAINS * s, CHAINS * (s + 1))
@@ -130,9 +132,8 @@ def tile_hybrid_beamforming_precoder_s4_kernel(
             nc.sync.dma_start(out=gain_rows[:], in_=gain.rearrange("(s n) -> s n", s=PHASES))
 
         def load_w(k, nh):
-            w = (cosw if k == "c" else sinw).rearrange("(q t r) n -> t q r n", t=SLOTS, r=RUN)
-            for t in range(SLOTS):
-                nc.sync.dma_start(out=w_raw[k, nh][:, t, :], in_=w[t][:, :, HALF * nh : HALF * (nh + 1)])
+            w = (cosw if k == "c" else sinw).rearrange("(p t) n -> p t n", t=SLOTS)
+            nc.sync.dma_start(out=w_raw[k, nh][:], in_=w[:, :, HALF * nh : HALF * (nh + 1)])
 
         load_x(0)
         load_gain()
@@ -149,18 +150,17 @@ def tile_hybrid_beamforming_precoder_s4_kernel(
         load_w("c", 1)
         load_w("b", 1)
 
-        def deal_scales(s):
+        def deal_scales(s, pair):
             nc.vector.tensor_copy(
-                out=flat(d_scales[s], I32).rearrange("p (g t q w) -> p g t q w", g=GROUPS, t=SLOTS, w=2),
-                in_=flat(d_scales_raw, I32).rearrange("p (g s q t w) -> p s g t q w", g=GROUPS, s=PHASES, t=SLOTS, w=2)[:, s],
+                out=d_scales[s][pair].rearrange("p (j g) m -> p j g m", j=2),
+                in_=d_scales_raw[:].rearrange("p g (s m u j) -> p s u j g m", s=PHASES, u=2, j=2)[:, s, pair],
             )
 
-        def deal_codes(s):
-            for pair in range(2):
-                nc.vector.tensor_copy(
-                    out=flat(d_codes[s][pair], I32).rearrange("p (j g q w) -> p j g q w", j=2, g=GROUPS, w=4),
-                    in_=flat(d_raw[s], I32).rearrange("p (g q u j w) -> p u j g q w", g=GROUPS, u=2, j=2, w=4)[:, pair],
-                )
+        def deal_codes(copy, s, pair):
+            copy(
+                out=flat(d_codes[s][pair], U16).rearrange("p (j g m) -> p j g m", j=2, g=GROUPS),
+                in_=flat(d_raw[s], U16).rearrange("p (g m u j) -> p u j g m", g=GROUPS, u=2, j=2)[:, pair],
+            )
 
         gain_number, gain_bank = BANKS - 1, psum.tile([P, SLOTS * P], BF16, name="bank7")
         line.remove(gain_number)
@@ -168,8 +168,8 @@ def tile_hybrid_beamforming_precoder_s4_kernel(
 
         def sort_gain():
             nc.vector.tensor_copy(
-                out=gain_sorted[0:PHASES, :].rearrange("p (t q r) -> p t q r", t=SLOTS, r=RUN),
-                in_=gain_rows[:].rearrange("p (q t r) -> p t q r", t=SLOTS, r=RUN),
+                out=gain_sorted[0:PHASES, :].rearrange("p (t m) -> p t m", t=SLOTS),
+                in_=gain_rows[:].rearrange("p (m t) -> p t m", t=SLOTS),
             )
 
         def turn_gain():
@@ -179,38 +179,28 @@ def tile_hybrid_beamforming_precoder_s4_kernel(
         def gather_gain():
             nc.scalar.copy(out=gain_cols[:], in_=gain_in_bank[:, 0:PHASES, :])
 
-        sums = {}
-
-        def first_matmul(s, q):
-            piece = [first <= QUARTER * q < last for first, last in x_loads].index(True)
-            n = QUARTER * q - x_loads[piece][0]
+        def chains(s, q):
+            banks = []
             for pair in range(2):
-                sums[s, q, pair] = take_bank()
+                banks.append(take_bank())
                 for j in range(2):
                     for g in range(GROUPS):
                         nc.tensor.matmul_mx(
-                            out=sums[s, q, pair][1][:, QUARTER * j : QUARTER * (j + 1)],
+                            out=banks[pair][1][:, QUARTER * j : QUARTER * (j + 1)],
                             lhsT=d_codes[s][pair][:, j, g, :].bitcast(FP4X4),
-                            lhsT_scale=d_scales[s][:, SLOTS * g + 2 * pair + j, :],
-                            rhs=x_codes[piece][:, g, 2 * n : 2 * (n + QUARTER)].bitcast(FP4X4),
+                            lhsT_scale=d_scales[s][pair][:, GROUPS * j + g, :],
+                            rhs=x_codes[q][:, g, :].bitcast(FP4X4),
                             rhs_scale=x_scales[q // 2][:, g, QUARTER * (q % 2) : QUARTER * (q % 2 + 1)],
                             start=(g == 0),
                             stop=(g == GROUPS - 1),
                         )
-
-        def soft_limit(s, q, pair):
-            number, bank = sums[s, q, pair]
-            nc.scalar.activation(
-                out=tanh_h[s, q][:, pair, :].rearrange("p (n j) -> p n j", j=2),
-                in_=bank[:].rearrange("p (j n) -> p n j", j=2),
-                func=TANH,
-            )
-            line.append(number)
-
-        def chains(s, q):
-            first_matmul(s, q)
-            for pair in range(2):
-                soft_limit(s, q, pair)
+            for pair, (number, bank) in enumerate(banks):
+                nc.scalar.activation(
+                    out=tanh_h[s, q][:, pair, :].rearrange("p (n j) -> p n j", j=2),
+                    in_=bank[:].rearrange("p (j n) -> p n j", j=2),
+                    func=TANH,
+                )
+                line.append(number)
 
         def pack_w(copy, k, nh, first=0, last=HALF):
             copy(
@@ -237,7 +227,7 @@ def tile_hybrid_beamforming_precoder_s4_kernel(
 
         def times_gain(s, m):
             n = P * (m % 2)
-            samples = P * dict(batches)[m]
+            samples = P * batches[m]
             gains = gain_in_bank if m == 0 else gain_cols
             nc.vector.tensor_tensor(
                 out=uv_packed[m][:, s, :].rearrange("p (n u j) -> p n u j", u=2, j=2),
@@ -259,58 +249,62 @@ def tile_hybrid_beamforming_precoder_s4_kernel(
             for s in (V, U, MINUS_V):
                 quantise_uv(m, s)
 
-        def passes(out, m, part, nh, first, last, turned):
-            pairs = (((U, "c"), (MINUS_V, "b")), ((U, "b"), (V, "c")))[part]
-            for opens, (s, k) in zip((True, False), pairs[::-1] if turned else pairs):
+        def product(result, m, part, nh, copy):
+            number, bank = take_bank()
+            passes = (((U, "c"), (MINUS_V, "b")), ((U, "b"), (V, "c")))[part]
+            for opens, (s, k) in zip((True, False), passes[::-1] if nh else passes):
                 nc.tensor.matmul_mx(
-                    out=out,
+                    out=bank[:],
                     lhsT=uv_codes[m][:, s, :].bitcast(FP8X4),
                     lhsT_scale=uv_scales[m][:, s, :],
-                    rhs=w_codes[k, nh][:, first:last].bitcast(FP8X4),
-                    rhs_scale=w_scales[k, nh][:, first:last],
+                    rhs=w_codes[k, nh].bitcast(FP8X4),
+                    rhs_scale=w_scales[k, nh],
                     start=opens,
                     stop=not opens,
                 )
-
-        def product(result, m, part, nh, copy):
-            number, bank = take_bank()
-            passes(bank[:], m, part, nh, 0, HALF, nh == 1)
             copy(out=result, in_=bank[:])
             line.append(number)
 
         def store(result, part, m, first, last):
             nc.sync.dma_start(out=(out_0, out_1)[part][P * m : P * (m + 1), first:last], in_=result)
 
-        def half_row(m, part, nh, copy=nc.scalar.copy):
-            result = results.tile([P, HALF], F32, name="half%d%d%d" % (m, part, nh))
-            product(result[:], m, part, nh, copy)
-            store(result[:], part, m, HALF * nh, HALF * (nh + 1))
-
-        def full_row(m, part, first_copy, second_copy):
-            result = results.tile([P, ANTENNAS], F32, name="full%d%d" % (m, part))
-            product(result[:, 0:HALF], m, part, 0, first_copy)
-            product(result[:, HALF:ANTENNAS], m, part, 1, second_copy)
-            store(result[:], part, m, 0, ANTENNAS)
-
         on_scalar, on_vector = nc.scalar.copy, nc.vector.tensor_copy
 
+        def half_rows(nh):
+            for m in range(EARLY):
+                for part in (IM, RE):
+                    result = results.tile([P, HALF], F32, name="half%d%d%d" % (m, part, nh))
+                    product(result[:], m, part, nh, on_scalar)
+                    store(result[:], part, m, HALF * nh, HALF * (nh + 1))
+
+        def full_row(m, part, first_copy):
+            result = results.tile([P, ANTENNAS], F32, name="full%d%d" % (m, part))
+            product(result[:, 0:HALF], m, part, 0, first_copy)
+            product(result[:, HALF:ANTENNAS], m, part, 1, on_scalar)
+            store(result[:], part, m, 0, ANTENNAS)
+
         sort_gain()
-        deal_scales(U)
+        deal_scales(U, 0)
         turn_gain()
+        deal_scales(U, 1)
+        deal_codes(on_vector, U, 0)
+        deal_codes(on_scalar, U, 1)
         gather_gain()
-        deal_codes(U)
+        deal_scales(V, 0)
+        deal_scales(V, 1)
         chains(U, 0)
-        deal_scales(V)
-        deal_codes(V)
+        deal_codes(on_vector, V, 0)
+        deal_codes(on_vector, V, 1)
         chains(V, 0)
         chains(U, 1)
         chains(V, 1)
-        pack_w(on_vector, "c", 0, 0, 384)
-        pack_w(on_vector, "c", 0, 384, 512)
-        quantise_w("c", 0, 0, 384)
-        quantise_w("c", 0, 384, 512)
-        pack_on_gpsimd("b", 0, 0, 384)
-        pack_w(on_scalar, "b", 0, 384, 512)
+
+        for first, last in ((0, SHARE), (SHARE, HALF)):
+            pack_w(on_vector, "c", 0, first, last)
+        for first, last in ((0, SHARE), (SHARE, HALF)):
+            quantise_w("c", 0, first, last)
+        pack_on_gpsimd("b", 0, 0, SHARE)
+        pack_w(on_scalar, "b", 0, SHARE, HALF)
         times_gain(V, 0)
         times_gain(U, 0)
         line.append(gain_number)
@@ -319,37 +313,22 @@ def tile_hybrid_beamforming_precoder_s4_kernel(
         quantise_uv(0, U)
         quantise_w("b", 0)
         quantise_uv(0, MINUS_V)
+
         chains(U, 2)
         chains(V, 2)
         chains(U, 3)
+        half_rows(0)
         chains(V, 3)
-        half_row(0, IM, 0, on_scalar)
-        half_row(0, RE, 0, on_scalar)
-        half_row(1, IM, 0, on_scalar)
-        half_row(1, RE, 0, on_scalar)
-        pack_w(on_vector, "c", 1, 0, 512)
-        pack_w(on_vector, "b", 1)
-        quantise_w("c", 1)
-        quantise_w("b", 1)
-        half_row(0, IM, 1, on_scalar)
-        half_row(0, RE, 1, on_scalar)
-        half_row(1, IM, 1, on_scalar)
-        half_row(1, RE, 1, on_scalar)
-        block(2)
-        block(3)
-        full_row(2, IM, on_scalar, on_scalar)
-        full_row(2, RE, on_scalar, on_scalar)
-        block(4)
-        full_row(3, IM, on_scalar, on_scalar)
-        full_row(3, RE, on_scalar, on_scalar)
-        block(5)
-        full_row(4, IM, on_scalar, on_scalar)
-        full_row(4, RE, on_scalar, on_scalar)
-        block(6)
-        full_row(5, IM, on_scalar, on_scalar)
-        full_row(5, RE, on_scalar, on_scalar)
-        block(7)
-        full_row(6, IM, on_scalar, on_scalar)
-        full_row(6, RE, on_vector, on_scalar)
-        full_row(7, IM, on_vector, on_scalar)
-        full_row(7, RE, on_vector, on_scalar)
+        for k in ("c", "b"):
+            pack_w(on_vector, k, 1)
+        for k in ("c", "b"):
+            quantise_w(k, 1)
+        half_rows(1)
+
+        last_rows = ((BLOCKS - 2, RE), (BLOCKS - 1, IM), (BLOCKS - 1, RE))
+        block(EARLY)
+        for m in range(EARLY, BLOCKS):
+            if m + 1 < BLOCKS:
+                block(m + 1)
+            for part in (IM, RE):
+                full_row(m, part, on_vector if (m, part) in last_rows else on_scalar)

@@ -53,7 +53,7 @@ def tile_hybrid_beamforming_precoder_s4_kernel(
         x_scales = [shifted(GROUPS, HALF, U8, "x_scales%d" % half, 192) for half in range(2)]
         d_raw = {s: tile([P, GROUPS, 2 * CHAINS], U8, "d_raw%d" % s) for s in (U, V)}
         d_scales_raw = tile([P, GROUPS, PHASES * CHAINS], U8, "d_scales_raw")
-        d_codes = {s: [tile([P, 2, GROUPS, 2 * P], U8, "d_codes%d%d" % (s, pair)) for pair in range(2)] for s in (U, V)}
+        d_codes = {s: [tile([P, GROUPS, 2 * P], U8, "d_codes%d%d" % (s, t)) for t in range(SLOTS)] for s in (U, V)}
         d_scales = {s: [shifted(2 * GROUPS, P, U8, "d_scales%d%d" % (s, pair), 64) for pair in range(2)] for s in (U, V)}
         gain_rows = tile([PHASES, CHAINS], BF16, "gain_rows")
         gain_sorted = tile([P, CHAINS], BF16, "gain_sorted")
@@ -61,7 +61,14 @@ def tile_hybrid_beamforming_precoder_s4_kernel(
         gain_cols = tile([P, PHASES, SLOTS], F32, "gain_cols")
 
         halves = [(k, nh) for k in ("c", "b") for nh in range(2)]
-        w_raw = {(k, nh): tile([P, SLOTS, HALF], BF16, "raw_%s%d" % (k, nh)) for k, nh in halves}
+        parts = ((0, SHARE), (SHARE, HALF))
+        w_loads = [("c", 0, first, last) for first, last in parts] + [(k, nh, 0, HALF) for k, nh in halves[1:]]
+        w_raw = {(k, nh, first): tile([P, SLOTS, last - first], BF16, "raw_%s%d%d" % (k, nh, first)) for k, nh, first, last in w_loads}
+
+        def raw(k, nh, first, last):
+            loaded_from = first if (k, nh, first) in w_raw else 0
+            return w_raw[k, nh, loaded_from][:, :, first - loaded_from : last - loaded_from]
+
         packed_first = tile([P, SLOTS * HALF], BF16, "packed_first")
         w_packed = {(k, nh): tile([P, SLOTS * HALF], BF16, "packed_%s" % k) if nh else packed_first for k, nh in halves}
         w_codes = {(k, nh): shifted(1, HALF, U32, "codes_%s%d" % (k, nh), 32)[:, 0, :] for k, nh in halves}
@@ -131,9 +138,9 @@ def tile_hybrid_beamforming_precoder_s4_kernel(
         def load_gain():
             nc.sync.dma_start(out=gain_rows[:], in_=gain.rearrange("(s n) -> s n", s=PHASES))
 
-        def load_w(k, nh):
+        def load_w(k, nh, first=0, last=HALF):
             w = (cosw if k == "c" else sinw).rearrange("(p t) n -> p t n", t=SLOTS)
-            nc.sync.dma_start(out=w_raw[k, nh][:], in_=w[:, :, HALF * nh : HALF * (nh + 1)])
+            nc.sync.dma_start(out=w_raw[k, nh, first][:], in_=w[:, :, HALF * nh + first : HALF * nh + last])
 
         load_x(0)
         load_gain()
@@ -141,8 +148,9 @@ def tile_hybrid_beamforming_precoder_s4_kernel(
         load_d(U)
         load_scales(x_scales[0], sym_scales, 0, HALF)
         load_d(V)
-        load_w("c", 0)
+        load_w("c", 0, 0, SHARE)
         load_x(1)
+        load_w("c", 0, SHARE, HALF)
         load_w("b", 0)
         load_scales(x_scales[1], sym_scales, HALF, SAMPLES)
         load_x(2)
@@ -156,10 +164,10 @@ def tile_hybrid_beamforming_precoder_s4_kernel(
                 in_=d_scales_raw[:].rearrange("p g (s m u j) -> p s u j g m", s=PHASES, u=2, j=2)[:, s, pair],
             )
 
-        def deal_codes(copy, s, pair):
+        def deal_codes(copy, s, t):
             copy(
-                out=flat(d_codes[s][pair], U16).rearrange("p (j g m) -> p j g m", j=2, g=GROUPS),
-                in_=flat(d_raw[s], U16).rearrange("p (g m u j) -> p u j g m", g=GROUPS, u=2, j=2)[:, pair],
+                out=flat(d_codes[s][t], U16).rearrange("p (g m) -> p g m", g=GROUPS),
+                in_=flat(d_raw[s], U16).rearrange("p (g m t) -> p t g m", g=GROUPS, t=SLOTS)[:, t],
             )
 
         gain_number, gain_bank = BANKS - 1, psum.tile([P, SLOTS * P], BF16, name="bank7")
@@ -187,7 +195,7 @@ def tile_hybrid_beamforming_precoder_s4_kernel(
                     for g in range(GROUPS):
                         nc.tensor.matmul_mx(
                             out=banks[pair][1][:, QUARTER * j : QUARTER * (j + 1)],
-                            lhsT=d_codes[s][pair][:, j, g, :].bitcast(FP4X4),
+                            lhsT=d_codes[s][2 * pair + j][:, g, :].bitcast(FP4X4),
                             lhsT_scale=d_scales[s][pair][:, GROUPS * j + g, :],
                             rhs=x_codes[q][:, g, :].bitcast(FP4X4),
                             rhs_scale=x_scales[q // 2][:, g, QUARTER * (q % 2) : QUARTER * (q % 2 + 1)],
@@ -205,13 +213,13 @@ def tile_hybrid_beamforming_precoder_s4_kernel(
         def pack_w(copy, k, nh, first=0, last=HALF):
             copy(
                 out=w_packed[k, nh][:, SLOTS * first : SLOTS * last].rearrange("p (c i t) -> p c t i", t=SLOTS, i=4),
-                in_=w_raw[k, nh][:, :, first:last].rearrange("p t (c i) -> p c t i", i=4),
+                in_=raw(k, nh, first, last).rearrange("p t (c i) -> p c t i", i=4),
             )
 
         def pack_on_gpsimd(k, nh, first, last):
             nc.gpsimd.tensor_scalar(
                 out=w_packed[k, nh][:, SLOTS * first : SLOTS * last].rearrange("p (n t) -> p n t", t=SLOTS),
-                in0=w_raw[k, nh][:, :, first:last].rearrange("p t n -> p n t"),
+                in0=raw(k, nh, first, last).rearrange("p t n -> p n t"),
                 scalar1=1.0,
                 scalar2=0.0,
                 op0=MULT,
@@ -249,19 +257,23 @@ def tile_hybrid_beamforming_precoder_s4_kernel(
             for s in (V, U, MINUS_V):
                 quantise_uv(m, s)
 
+        def multiply(bank, m, s, k, nh, opens):
+            nc.tensor.matmul_mx(
+                out=bank[:],
+                lhsT=uv_codes[m][:, s, :].bitcast(FP8X4),
+                lhsT_scale=uv_scales[m][:, s, :],
+                rhs=w_codes[k, nh].bitcast(FP8X4),
+                rhs_scale=w_scales[k, nh],
+                start=opens,
+                stop=not opens,
+            )
+
+        passes = {RE: ((U, "c"), (MINUS_V, "b")), IM: ((V, "c"), (U, "b"))}
+
         def product(result, m, part, nh, copy):
             number, bank = take_bank()
-            passes = (((U, "c"), (MINUS_V, "b")), ((U, "b"), (V, "c")))[part]
-            for opens, (s, k) in zip((True, False), passes[::-1] if nh else passes):
-                nc.tensor.matmul_mx(
-                    out=bank[:],
-                    lhsT=uv_codes[m][:, s, :].bitcast(FP8X4),
-                    lhsT_scale=uv_scales[m][:, s, :],
-                    rhs=w_codes[k, nh].bitcast(FP8X4),
-                    rhs_scale=w_scales[k, nh],
-                    start=opens,
-                    stop=not opens,
-                )
+            for opens, (s, k) in zip((True, False), passes[part][::-1] if nh else passes[part]):
+                multiply(bank, m, s, k, nh, opens)
             copy(out=result, in_=bank[:])
             line.append(number)
 
@@ -271,10 +283,15 @@ def tile_hybrid_beamforming_precoder_s4_kernel(
         on_scalar, on_vector = nc.scalar.copy, nc.vector.tensor_copy
 
         def half_rows(nh):
-            for m in range(EARLY):
-                for part in (IM, RE):
+            for part in (IM, RE):
+                banks = [take_bank() for m in range(EARLY)]
+                for m, (number, bank) in enumerate(banks):
+                    multiply(bank, m, *passes[part][0], nh, True)
+                for m, (number, bank) in enumerate(banks):
+                    multiply(bank, m, *passes[part][1], nh, False)
                     result = results.tile([P, HALF], F32, name="half%d%d%d" % (m, part, nh))
-                    product(result[:], m, part, nh, on_scalar)
+                    on_scalar(out=result[:], in_=bank[:])
+                    line.append(number)
                     store(result[:], part, m, HALF * nh, HALF * (nh + 1))
 
         def full_row(m, part, first_copy):
@@ -288,20 +305,22 @@ def tile_hybrid_beamforming_precoder_s4_kernel(
         turn_gain()
         deal_scales(U, 1)
         deal_codes(on_vector, U, 0)
-        deal_codes(on_scalar, U, 1)
+        deal_codes(on_scalar, U, 2)
+        deal_codes(on_vector, U, 1)
+        deal_codes(on_scalar, U, 3)
         gather_gain()
         deal_scales(V, 0)
         deal_scales(V, 1)
         chains(U, 0)
-        deal_codes(on_vector, V, 0)
-        deal_codes(on_vector, V, 1)
+        for t in range(SLOTS):
+            deal_codes(on_vector, V, t)
         chains(V, 0)
         chains(U, 1)
         chains(V, 1)
 
-        for first, last in ((0, SHARE), (SHARE, HALF)):
+        for first, last in parts:
             pack_w(on_vector, "c", 0, first, last)
-        for first, last in ((0, SHARE), (SHARE, HALF)):
+        for first, last in parts:
             quantise_w("c", 0, first, last)
         pack_on_gpsimd("b", 0, 0, SHARE)
         pack_w(on_scalar, "b", 0, SHARE, HALF)

@@ -29,8 +29,11 @@ RE, IM = 0, 1
 BANKS = 8
 BLOCKS = SAMPLES // P
 EARLY = 2
-SHARE = 384
+SHARE = 320
 WARM_UP = 6
+FROM_BANK = (0,)
+W_LOADS = [("c", 0, 0, 384), ("c", 0, 384, HALF), ("b", 0, 0, 320), ("b", 0, 320, HALF), ("c", 1, 0, HALF), ("b", 1, 0, HALF)]
+LATE = 6
 
 
 def tile_hybrid_beamforming_precoder_s4_kernel(
@@ -39,7 +42,6 @@ def tile_hybrid_beamforming_precoder_s4_kernel(
     nc = tc.nc
     with ExitStack() as ctx:
         keep = ctx.enter_context(tc.tile_pool(name="keep", bufs=1))
-        results = ctx.enter_context(tc.tile_pool(name="results", bufs=1))
         psum = ctx.enter_context(tc.psum_pool(name="psum", bufs=1))
 
         def tile(shape, dtype, name):
@@ -48,6 +50,9 @@ def tile_hybrid_beamforming_precoder_s4_kernel(
         def shifted(rows, width, dtype, name, shift):
             whole = tile([P, shift + rows * width], dtype, name)
             return whole[:, shift:].rearrange("p (r n) -> p r n", r=rows)
+
+        def flat(t, dtype):
+            return t[:].rearrange("p a n -> p (a n)").bitcast(dtype)
 
         x_codes = [shifted(GROUPS, 2 * QUARTER, U8, "x_codes%d" % q, 128) for q in range(4)]
         x_scales = [shifted(GROUPS, HALF, U8, "x_scales%d" % half, 192) for half in range(2)]
@@ -61,12 +66,10 @@ def tile_hybrid_beamforming_precoder_s4_kernel(
         gain_cols = tile([P, PHASES, SLOTS], F32, "gain_cols")
 
         halves = [(k, nh) for k in ("c", "b") for nh in range(2)]
-        parts = ((0, SHARE), (SHARE, HALF))
-        w_loads = [("c", 0, first, last) for first, last in parts] + [(k, nh, 0, HALF) for k, nh in halves[1:]]
-        w_raw = {(k, nh, first): tile([P, SLOTS, last - first], BF16, "raw_%s%d%d" % (k, nh, first)) for k, nh, first, last in w_loads}
+        w_raw = {(k, nh, first): tile([P, SLOTS, last - first], BF16, "raw_%s%d%d" % (k, nh, first)) for k, nh, first, last in W_LOADS}
 
         def raw(k, nh, first, last):
-            loaded_from = first if (k, nh, first) in w_raw else 0
+            loaded_from = max(f for kk, hh, f in w_raw if (kk, hh) == (k, nh) and f <= first)
             return w_raw[k, nh, loaded_from][:, :, first - loaded_from : last - loaded_from]
 
         packed_first = tile([P, SLOTS * HALF], BF16, "packed_first")
@@ -82,6 +85,11 @@ def tile_hybrid_beamforming_precoder_s4_kernel(
         places = [(m, i) for m, blocks in batches.items() for i in range(blocks)]
         uv_codes = {m + i: batch_codes[m][:, :, P * i : P * (i + 1)] for m, i in places}
         uv_scales = {m + i: batch_scales[m][:, :, P * i : P * (i + 1)] for m, i in places}
+        results = {(m, part): [tile([P, HALF], F32, "y%d%d%d" % (m, part, nh)) for nh in range(2)] for m in range(EARLY) for part in (RE, IM)}
+        rows = {(m, part): tile([P, ANTENNAS], F32, "y%d%d" % (m, part)) for m in range(EARLY, BLOCKS) for part in (RE, IM)}
+
+        def result(m, part, nh):
+            return results[m, part][nh][:] if m < EARLY else rows[m, part][:, HALF * nh : HALF * (nh + 1)]
 
         ctx.enter_context(tc.manual_schedule())
 
@@ -92,12 +100,7 @@ def tile_hybrid_beamforming_precoder_s4_kernel(
             line.remove(number)
             return number, psum.tile([P, HALF], F32, name="bank%d" % number)
 
-        def flat(t, dtype):
-            pattern = "p a n -> p (a n)" if len(t.shape) == 3 else "p a b n -> p (a b n)"
-            return t[:].rearrange(pattern).bitcast(dtype)
-
         nc.vector.memset(flat(d_scales_raw, I32), 0)
-
         nc.vector.memset(flat(x_codes[-1], I32), 0)
         nc.vector.memset(w_scales["b", 1][:].bitcast(I32), 0)
         warm_bank = psum.tile([P, HALF], F32, name="bank7")
@@ -111,7 +114,6 @@ def tile_hybrid_beamforming_precoder_s4_kernel(
                 start=True,
                 stop=True,
             )
-
         nc.vector.memset(flat(x_scales[0], I32), 0)
         nc.vector.memset(flat(x_scales[1], I32), 0)
         nc.vector.memset(gain_sorted[:], 0.0)
@@ -138,25 +140,10 @@ def tile_hybrid_beamforming_precoder_s4_kernel(
         def load_gain():
             nc.sync.dma_start(out=gain_rows[:], in_=gain.rearrange("(s n) -> s n", s=PHASES))
 
-        def load_w(k, nh, first=0, last=HALF):
+        def load_w(number):
+            k, nh, first, last = W_LOADS[number]
             w = (cosw if k == "c" else sinw).rearrange("(p t) n -> p t n", t=SLOTS)
             nc.sync.dma_start(out=w_raw[k, nh, first][:], in_=w[:, :, HALF * nh + first : HALF * nh + last])
-
-        load_x(0)
-        load_gain()
-        load_scales(d_scales_raw, dig_scales, 0, PHASES * CHAINS)
-        load_d(U)
-        load_scales(x_scales[0], sym_scales, 0, HALF)
-        load_d(V)
-        load_w("c", 0, 0, SHARE)
-        load_x(1)
-        load_w("c", 0, SHARE, HALF)
-        load_w("b", 0)
-        load_scales(x_scales[1], sym_scales, HALF, SAMPLES)
-        load_x(2)
-        load_x(3)
-        load_w("c", 1)
-        load_w("b", 1)
 
         def deal_scales(s, pair):
             nc.vector.tensor_copy(
@@ -187,14 +174,15 @@ def tile_hybrid_beamforming_precoder_s4_kernel(
         def gather_gain():
             nc.scalar.copy(out=gain_cols[:], in_=gain_in_bank[:, 0:PHASES, :])
 
-        def chains(s, q):
-            banks = []
-            for pair in range(2):
-                banks.append(take_bank())
+        held = {}
+
+        def chains(s, q, pairs=(0, 1)):
+            for pair in pairs:
+                held[s, q, pair] = take_bank()
                 for j in range(2):
                     for g in range(GROUPS):
                         nc.tensor.matmul_mx(
-                            out=banks[pair][1][:, QUARTER * j : QUARTER * (j + 1)],
+                            out=held[s, q, pair][1][:, QUARTER * j : QUARTER * (j + 1)],
                             lhsT=d_codes[s][2 * pair + j][:, g, :].bitcast(FP4X4),
                             lhsT_scale=d_scales[s][pair][:, GROUPS * j + g, :],
                             rhs=x_codes[q][:, g, :].bitcast(FP4X4),
@@ -202,13 +190,20 @@ def tile_hybrid_beamforming_precoder_s4_kernel(
                             start=(g == 0),
                             stop=(g == GROUPS - 1),
                         )
-            for pair, (number, bank) in enumerate(banks):
+
+        def limit(s, q, pairs=(0, 1)):
+            for pair in pairs:
+                number, bank = held[s, q, pair]
                 nc.scalar.activation(
                     out=tanh_h[s, q][:, pair, :].rearrange("p (n j) -> p n j", j=2),
                     in_=bank[:].rearrange("p (j n) -> p n j", j=2),
                     func=TANH,
                 )
                 line.append(number)
+
+        def stage_one(s, q, pairs=(0, 1)):
+            chains(s, q, pairs)
+            limit(s, q, pairs)
 
         def pack_w(copy, k, nh, first=0, last=HALF):
             copy(
@@ -236,7 +231,7 @@ def tile_hybrid_beamforming_precoder_s4_kernel(
         def times_gain(s, m):
             n = P * (m % 2)
             samples = P * batches[m]
-            gains = gain_in_bank if m == 0 else gain_cols
+            gains = gain_in_bank if m in FROM_BANK else gain_cols
             nc.vector.tensor_tensor(
                 out=uv_packed[m][:, s, :].rearrange("p (n u j) -> p n u j", u=2, j=2),
                 in0=tanh_h[s, m // 2][:].rearrange("p u (n j) -> p n u j", j=2)[:, n : n + samples],
@@ -250,16 +245,29 @@ def tile_hybrid_beamforming_precoder_s4_kernel(
         def quantise_uv(m, s):
             nc.vector.quantize_mx(out=batch_codes[m][:, s, :].bitcast(FP8X4), scales=batch_scales[m][:, s, :], in_=uv_packed[m][:, s, :])
 
-        def block(m):
+        def gains(m):
             times_gain(V, m)
             times_gain(U, m)
+
+        def codes(m):
             negate_v(m)
             for s in (V, U, MINUS_V):
                 quantise_uv(m, s)
 
-        def multiply(bank, m, s, k, nh, opens):
+        def prepare(m):
+            gains(m)
+            codes(m)
+
+        passes = {(RE, "c"): U, (RE, "b"): MINUS_V, (IM, "c"): V, (IM, "b"): U}
+        sums = {}
+
+        def multiply(m, part, nh, k):
+            opens = (m, part, nh) not in sums
+            if opens:
+                sums[m, part, nh] = take_bank()
+            s = passes[part, k]
             nc.tensor.matmul_mx(
-                out=bank[:],
+                out=sums[m, part, nh][1][:],
                 lhsT=uv_codes[m][:, s, :].bitcast(FP8X4),
                 lhsT_scale=uv_scales[m][:, s, :],
                 rhs=w_codes[k, nh].bitcast(FP8X4),
@@ -268,38 +276,46 @@ def tile_hybrid_beamforming_precoder_s4_kernel(
                 stop=not opens,
             )
 
-        passes = {RE: ((U, "c"), (MINUS_V, "b")), IM: ((V, "c"), (U, "b"))}
-
-        def product(result, m, part, nh, copy):
-            number, bank = take_bank()
-            for opens, (s, k) in zip((True, False), passes[part][::-1] if nh else passes[part]):
-                multiply(bank, m, s, k, nh, opens)
-            copy(out=result, in_=bank[:])
-            line.append(number)
-
-        def store(result, part, m, first, last):
-            nc.sync.dma_start(out=(out_0, out_1)[part][P * m : P * (m + 1), first:last], in_=result)
-
         on_scalar, on_vector = nc.scalar.copy, nc.vector.tensor_copy
 
-        def half_rows(nh):
-            for part in (IM, RE):
-                banks = [take_bank() for m in range(EARLY)]
-                for m, (number, bank) in enumerate(banks):
-                    multiply(bank, m, *passes[part][0], nh, True)
-                for m, (number, bank) in enumerate(banks):
-                    multiply(bank, m, *passes[part][1], nh, False)
-                    result = results.tile([P, HALF], F32, name="half%d%d%d" % (m, part, nh))
-                    on_scalar(out=result[:], in_=bank[:])
-                    line.append(number)
-                    store(result[:], part, m, HALF * nh, HALF * (nh + 1))
+        def empty(copy, m, part, nh):
+            number, bank = sums[m, part, nh]
+            copy(out=result(m, part, nh), in_=bank[:])
+            line.append(number)
 
-        def full_row(m, part, first_copy):
-            result = results.tile([P, ANTENNAS], F32, name="full%d%d" % (m, part))
-            product(result[:, 0:HALF], m, part, 0, first_copy)
-            product(result[:, HALF:ANTENNAS], m, part, 1, on_scalar)
-            store(result[:], part, m, 0, ANTENNAS)
+        def store_half(m, part, nh):
+            nc.sync.dma_start(out=(out_0, out_1)[part][P * m : P * (m + 1), HALF * nh : HALF * (nh + 1)], in_=result(m, part, nh))
 
+        def store_row(m, part):
+            nc.sync.dma_start(out=(out_0, out_1)[part][P * m : P * (m + 1), :], in_=rows[m, part][:])
+
+        def product(m, part, nh):
+            for k in ("b", "c") if (nh == 0) == (part == IM and m >= LATE) else ("c", "b"):
+                multiply(m, part, nh, k)
+
+        def row(m, part, first_copy=on_scalar, second_copy=on_scalar):
+            product(m, part, 0)
+            empty(first_copy, m, part, 0)
+            product(m, part, 1)
+            empty(second_copy, m, part, 1)
+            store_row(m, part)
+
+        load_x(0)
+        load_gain()
+        load_scales(d_scales_raw, dig_scales, 0, PHASES * CHAINS)
+        load_d(U)
+        load_scales(x_scales[0], sym_scales, 0, HALF)
+        load_d(V)
+        load_w(0)
+        load_x(1)
+        load_w(1)
+        load_w(2)
+        load_w(3)
+        load_scales(x_scales[1], sym_scales, HALF, SAMPLES)
+        load_x(2)
+        load_w(4)
+        load_x(3)
+        load_w(5)
         sort_gain()
         deal_scales(U, 0)
         turn_gain()
@@ -311,43 +327,76 @@ def tile_hybrid_beamforming_precoder_s4_kernel(
         gather_gain()
         deal_scales(V, 0)
         deal_scales(V, 1)
-        chains(U, 0)
+        stage_one(U, 0)
         for t in range(SLOTS):
             deal_codes(on_vector, V, t)
-        chains(V, 0)
-        chains(U, 1)
-        chains(V, 1)
-
-        for first, last in parts:
+        stage_one(V, 0)
+        for first, last in ((0, 384), (384, HALF)):
             pack_w(on_vector, "c", 0, first, last)
-        for first, last in parts:
+        for first, last in ((0, 384), (384, HALF)):
             quantise_w("c", 0, first, last)
         pack_on_gpsimd("b", 0, 0, SHARE)
+        stage_one(U, 1)
         pack_w(on_scalar, "b", 0, SHARE, HALF)
-        times_gain(V, 0)
+        stage_one(V, 1)
         times_gain(U, 0)
+        times_gain(V, 0)
         line.append(gain_number)
+        quantise_uv(0, U)
         negate_v(0)
         quantise_uv(0, V)
-        quantise_uv(0, U)
         quantise_w("b", 0)
         quantise_uv(0, MINUS_V)
-
-        chains(U, 2)
-        chains(V, 2)
-        chains(U, 3)
-        half_rows(0)
-        chains(V, 3)
+        stage_one(U, 2)
+        stage_one(V, 2)
         for k in ("c", "b"):
-            pack_w(on_vector, k, 1)
+            for first in (0, 256):
+                pack_w(on_vector, k, 1, first, first + 256)
+            for first in (0, 256):
+                quantise_w(k, 1, first, first + 256)
+        for part in (IM, RE):
+            for k in ("c", "b"):
+                for m in range(EARLY):
+                    multiply(m, part, 0, k)
+            for m in range(EARLY):
+                empty(on_scalar, m, part, 0)
+                store_half(m, part, 0)
+        stage_one(U, 3)
         for k in ("c", "b"):
-            quantise_w(k, 1)
-        half_rows(1)
-
-        last_rows = ((BLOCKS - 2, RE), (BLOCKS - 1, IM), (BLOCKS - 1, RE))
-        block(EARLY)
-        for m in range(EARLY, BLOCKS):
-            if m + 1 < BLOCKS:
-                block(m + 1)
             for part in (IM, RE):
-                full_row(m, part, on_vector if (m, part) in last_rows else on_scalar)
+                for m in range(EARLY):
+                    multiply(m, part, 1, k)
+        prepare(2)
+        for part in (IM, RE):
+            for m in range(EARLY):
+                empty(on_scalar, m, part, 1)
+                store_half(m, part, 1)
+        prepare(3)
+        row(2, IM)
+        row(2, RE)
+        prepare(4)
+        row(3, IM)
+        gains(5)
+        row(3, RE, on_vector)
+        codes(5)
+        row(4, IM)
+        stage_one(V, 3)
+        for m in (6, 7):
+            times_gain(U, m)
+        quantise_uv(6, U)
+        row(4, RE, on_vector)
+        times_gain(V, 6)
+        quantise_uv(7, U)
+        quantise_uv(6, V)
+        times_gain(V, 7)
+        negate_v(6)
+        quantise_uv(7, V)
+        quantise_uv(6, MINUS_V)
+        negate_v(7)
+        row(5, IM)
+        row(5, RE)
+        row(6, IM, on_vector)
+        quantise_uv(7, MINUS_V)
+        row(6, RE, on_vector)
+        row(7, IM, on_vector)
+        row(7, RE, on_vector)

@@ -30,10 +30,11 @@ BANKS = 8
 BLOCKS = SAMPLES // P
 EARLY = 2
 SHARE = 320
+SLIP = 64
 WARM_UP = 6
 FROM_BANK = (0,)
-W_LOADS = [("c", 0, 0, 384), ("c", 0, 384, HALF), ("b", 0, 0, 320), ("b", 0, 320, HALF), ("c", 1, 0, HALF), ("b", 1, 0, HALF)]
 LATE = 6
+W_LOADS = [("c", 0, 0, 256), ("c", 0, 256, HALF), ("b", 0, 0, SHARE), ("b", 0, SHARE, HALF), ("c", 1, 0, HALF), ("b", 1, 0, HALF)]
 
 
 def tile_hybrid_beamforming_precoder_s4_kernel(
@@ -72,8 +73,10 @@ def tile_hybrid_beamforming_precoder_s4_kernel(
             loaded_from = max(f for kk, hh, f in w_raw if (kk, hh) == (k, nh) and f <= first)
             return w_raw[k, nh, loaded_from][:, :, first - loaded_from : last - loaded_from]
 
-        packed_first = tile([P, SLOTS * HALF], BF16, "packed_first")
-        w_packed = {(k, nh): tile([P, SLOTS * HALF], BF16, "packed_%s" % k) if nh else packed_first for k, nh in halves}
+        packed_first = tile([P, SLOTS * (HALF + SLIP)], BF16, "packed_first")
+        w_packed = {(k, 1): tile([P, SLOTS * HALF], BF16, "packed_%s" % k) for k in ("c", "b")}
+        w_packed["b", 0] = packed_first[:, 0 : SLOTS * HALF]
+        w_packed["c", 0] = packed_first[:, SLOTS * SLIP :]
         w_codes = {(k, nh): shifted(1, HALF, U32, "codes_%s%d" % (k, nh), 32)[:, 0, :] for k, nh in halves}
         w_scales = {(k, nh): shifted(1, HALF, U8, "scales_%s%d" % (k, nh), 192)[:, 0, :] for k, nh in halves}
 
@@ -245,6 +248,13 @@ def tile_hybrid_beamforming_precoder_s4_kernel(
         def quantise_uv(m, s):
             nc.vector.quantize_mx(out=batch_codes[m][:, s, :].bitcast(FP8X4), scales=batch_scales[m][:, s, :], in_=uv_packed[m][:, s, :])
 
+        def quantise_both(m):
+            nc.vector.quantize_mx(
+                out=batch_codes[m][:, 0:2, :].rearrange("p s n -> p (s n)").bitcast(FP8X4),
+                scales=batch_scales[m][:, 0:2, :].rearrange("p s n -> p (s n)"),
+                in_=uv_packed[m][:, 0:2, :].rearrange("p s n -> p (s n)"),
+            )
+
         def gains(m):
             times_gain(V, m)
             times_gain(U, m)
@@ -307,15 +317,15 @@ def tile_hybrid_beamforming_precoder_s4_kernel(
         load_scales(x_scales[0], sym_scales, 0, HALF)
         load_d(V)
         load_w(0)
-        load_x(1)
         load_w(1)
+        load_x(1)
         load_w(2)
-        load_w(3)
         load_scales(x_scales[1], sym_scales, HALF, SAMPLES)
         load_x(2)
+        load_w(3)
         load_w(4)
-        load_x(3)
         load_w(5)
+        load_x(3)
         sort_gain()
         deal_scales(U, 0)
         turn_gain()
@@ -331,14 +341,16 @@ def tile_hybrid_beamforming_precoder_s4_kernel(
         for t in range(SLOTS):
             deal_codes(on_vector, V, t)
         stage_one(V, 0)
-        for first, last in ((0, 384), (384, HALF)):
+        for first, last in ((0, 256), (256, HALF)):
             pack_w(on_vector, "c", 0, first, last)
-        for first, last in ((0, 384), (384, HALF)):
+        for first, last in ((0, 256), (256, HALF)):
             quantise_w("c", 0, first, last)
         pack_on_gpsimd("b", 0, 0, SHARE)
         stage_one(U, 1)
+        chains(V, 1)
+        limit(V, 1, (0,))
         pack_w(on_scalar, "b", 0, SHARE, HALF)
-        stage_one(V, 1)
+        limit(V, 1, (1,))
         times_gain(U, 0)
         times_gain(V, 0)
         line.append(gain_number)
@@ -349,11 +361,12 @@ def tile_hybrid_beamforming_precoder_s4_kernel(
         quantise_uv(0, MINUS_V)
         stage_one(U, 2)
         stage_one(V, 2)
-        for k in ("c", "b"):
-            for first in (0, 256):
-                pack_w(on_vector, k, 1, first, first + 256)
-            for first in (0, 256):
-                quantise_w(k, 1, first, first + 256)
+        pack_w(on_scalar, "b", 1, 448, HALF)
+        pack_w(on_vector, "c", 1, 0, 512)
+        pack_w(on_vector, "b", 1, 0, 256)
+        quantise_w("c", 1)
+        pack_w(on_vector, "b", 1, 256, 448)
+        quantise_w("b", 1)
         for part in (IM, RE):
             for k in ("c", "b"):
                 for m in range(EARLY):
@@ -366,11 +379,13 @@ def tile_hybrid_beamforming_precoder_s4_kernel(
             for part in (IM, RE):
                 for m in range(EARLY):
                     multiply(m, part, 1, k)
-        prepare(2)
+        gains(2)
+        codes(2)
         for part in (IM, RE):
             for m in range(EARLY):
                 empty(on_scalar, m, part, 1)
                 store_half(m, part, 1)
+        chains(V, 3, (0,))
         prepare(3)
         row(2, IM)
         row(2, RE)
@@ -380,7 +395,8 @@ def tile_hybrid_beamforming_precoder_s4_kernel(
         row(3, RE, on_vector)
         codes(5)
         row(4, IM)
-        stage_one(V, 3)
+        chains(V, 3, (1,))
+        limit(V, 3)
         for m in (6, 7):
             times_gain(U, m)
         quantise_uv(6, U)

@@ -32,6 +32,7 @@ EARLY = 2
 SHARE = 320
 SLIP = 64
 WARM_UP = 6
+LOWER = 4
 FROM_BANK = (0,)
 LATE = 6
 W_LOADS = [("c", 0, 0, 256), ("c", 0, 256, HALF), ("b", 0, 0, SHARE), ("b", 0, SHARE, HALF), ("c", 1, 0, HALF), ("b", 1, 0, HALF)]
@@ -96,7 +97,7 @@ def tile_hybrid_beamforming_precoder_s4_kernel(
 
         ctx.enter_context(tc.manual_schedule())
 
-        line = list(range(BANKS))
+        line = list(range(0, BANKS, 2)) + list(range(1, BANKS, 2))
 
         def take_bank():
             number = line[0]
@@ -246,7 +247,7 @@ def tile_hybrid_beamforming_precoder_s4_kernel(
             nc.vector.tensor_scalar(out=uv_packed[m][:, MINUS_V, :], in0=uv_packed[m][:, V, :], scalar1=-1.0, scalar2=None, op0=MULT)
 
         def quantise_uv(m, s):
-            nc.vector.quantize_mx(out=batch_codes[m][:, s, :].bitcast(FP8X4), scales=batch_scales[m][:, s, :], in_=uv_packed[m][:, s, :])
+            nc.vector.quantize_mx(out=batch_codes[m][:, s, :].bitcast(FP8X4), scales=batch_scales[m][LOWER:, s, :], in_=uv_packed[m][:, s, :])
 
         def quantise_both(m):
             nc.vector.quantize_mx(
@@ -279,7 +280,7 @@ def tile_hybrid_beamforming_precoder_s4_kernel(
             nc.tensor.matmul_mx(
                 out=sums[m, part, nh][1][:],
                 lhsT=uv_codes[m][:, s, :].bitcast(FP8X4),
-                lhsT_scale=uv_scales[m][:, s, :],
+                lhsT_scale=uv_scales[m][LOWER:, s, :],
                 rhs=w_codes[k, nh].bitcast(FP8X4),
                 rhs_scale=w_scales[k, nh],
                 start=opens,

@@ -31,11 +31,12 @@ BLOCKS = SAMPLES // P
 EARLY = 2
 SHARE = 320
 SLIP = 64
-WARM_UP = 6
+WARM_UP = 3
 LOWER = 4
 FROM_BANK = (0,)
 LATE = 6
 W_LOADS = [("c", 0, 0, 256), ("c", 0, 256, HALF), ("b", 0, 0, SHARE), ("b", 0, SHARE, HALF), ("c", 1, 0, HALF), ("b", 1, 0, HALF)]
+BATCHES = [(0, 2), (2, 1), (3, 1), (4, 1), (5, 1), (6, 1), (7, 1)]
 
 
 def tile_hybrid_beamforming_precoder_s4_kernel(
@@ -82,7 +83,7 @@ def tile_hybrid_beamforming_precoder_s4_kernel(
         w_scales = {(k, nh): shifted(1, HALF, U8, "scales_%s%d" % (k, nh), 192)[:, 0, :] for k, nh in halves}
 
         tanh_h = {(s, q): tile([P, 2, 2 * QUARTER], F32, "tanh_%d%d" % (s, q)) for s in (U, V) for q in range(4)}
-        batches = dict([(0, EARLY)] + [(m, 1) for m in range(EARLY, BLOCKS)])
+        batches = dict(BATCHES)
         uv_packed = {m: tile([P, 3, blocks * SLOTS * P], BF16, "uv_packed%d" % m) for m, blocks in batches.items()}
         batch_codes = {m: tile([P, 3, blocks * P], U32, "uv_codes%d" % m) for m, blocks in batches.items()}
         batch_scales = {m: shifted(3, blocks * P, U8, "uv_scales%d" % m, 64) for m, blocks in batches.items()}
@@ -104,21 +105,23 @@ def tile_hybrid_beamforming_precoder_s4_kernel(
             line.remove(number)
             return number, psum.tile([P, HALF], F32, name="bank%d" % number)
 
+        nc.vector.memset(flat(x_scales[0], I32), 0)
         nc.vector.memset(flat(d_scales_raw, I32), 0)
         nc.vector.memset(flat(x_codes[-1], I32), 0)
-        nc.vector.memset(w_scales["b", 1][:].bitcast(I32), 0)
-        warm_bank = psum.tile([P, HALF], F32, name="bank7")
-        for unused in range(WARM_UP):
-            nc.tensor.matmul_mx(
-                out=warm_bank[:],
-                lhsT=x_codes[-1][:, 0, 0 : 2 * P].bitcast(FP4X4),
-                lhsT_scale=w_scales["b", 1][:, 0:P],
-                rhs=flat(x_codes[-1], U8).bitcast(FP4X4),
-                rhs_scale=w_scales["b", 1][:],
-                start=True,
-                stop=True,
-            )
-        nc.vector.memset(flat(x_scales[0], I32), 0)
+        def warm_up(passes, number):
+            warm_bank = psum.tile([P, HALF], F32, name="bank%d" % number)
+            for unused in range(passes):
+                nc.tensor.matmul_mx(
+                    out=warm_bank[:],
+                    lhsT=x_codes[-1][:, 0, 0 : 2 * P].bitcast(FP4X4),
+                    lhsT_scale=x_codes[-1][:, 0, 0:P],
+                    rhs=flat(x_codes[-1], U8).bitcast(FP4X4),
+                    rhs_scale=x_codes[-1][:, 0, :],
+                    start=True,
+                    stop=True,
+                )
+
+        warm_up(WARM_UP, BANKS - 1)
         nc.vector.memset(flat(x_scales[1], I32), 0)
         nc.vector.memset(gain_sorted[:], 0.0)
         nc.vector.memset(identity[:], 0.0)
@@ -134,8 +137,8 @@ def tile_hybrid_beamforming_precoder_s4_kernel(
         def load_d(s):
             load_codes(d_raw[s], dig_words, CHAINS * s, CHAINS * (s + 1))
 
-        def load_scales(dst, src, first, last):
-            for r in range(4):
+        def load_scales(dst, src, first, last, rows=range(4)):
+            for r in rows:
                 nc.sync.dma_start(
                     out=dst[r:P:32, :, :].bitcast(I32),
                     in_=src[:, r:16:4, first:last].rearrange("g j n -> j g n").bitcast(I32),
@@ -272,26 +275,26 @@ def tile_hybrid_beamforming_precoder_s4_kernel(
         passes = {(RE, "c"): U, (RE, "b"): MINUS_V, (IM, "c"): V, (IM, "b"): U}
         sums = {}
 
-        def multiply(m, part, nh, k):
-            opens = (m, part, nh) not in sums
+        def multiply(m, part, nh, k, first=0, last=HALF):
+            opens = (m, part, nh, first) not in sums
             if opens:
-                sums[m, part, nh] = take_bank()
+                sums[m, part, nh, first] = take_bank()
             s = passes[part, k]
             nc.tensor.matmul_mx(
-                out=sums[m, part, nh][1][:],
+                out=sums[m, part, nh, first][1][:, 0 : last - first],
                 lhsT=uv_codes[m][:, s, :].bitcast(FP8X4),
                 lhsT_scale=uv_scales[m][LOWER:, s, :],
-                rhs=w_codes[k, nh].bitcast(FP8X4),
-                rhs_scale=w_scales[k, nh],
+                rhs=w_codes[k, nh][:, first:last].bitcast(FP8X4),
+                rhs_scale=w_scales[k, nh][:, first:last],
                 start=opens,
                 stop=not opens,
             )
 
         on_scalar, on_vector = nc.scalar.copy, nc.vector.tensor_copy
 
-        def empty(copy, m, part, nh):
-            number, bank = sums[m, part, nh]
-            copy(out=result(m, part, nh), in_=bank[:])
+        def empty(copy, m, part, nh, first=0, last=HALF):
+            number, bank = sums[m, part, nh, first]
+            copy(out=result(m, part, nh)[:, first:last], in_=bank[:, 0 : last - first])
             line.append(number)
 
         def store_half(m, part, nh):
@@ -300,9 +303,15 @@ def tile_hybrid_beamforming_precoder_s4_kernel(
         def store_row(m, part):
             nc.sync.dma_start(out=(out_0, out_1)[part][P * m : P * (m + 1), :], in_=rows[m, part][:])
 
-        def product(m, part, nh):
+        def product(m, part, nh, first=0, last=HALF):
             for k in ("b", "c") if (nh == 0) == (part == IM and m >= LATE) else ("c", "b"):
-                multiply(m, part, nh, k)
+                multiply(m, part, nh, k, first, last)
+
+        def split_row(m, part, copies):
+            for copy, piece in zip(copies, ((0, 0, HALF), (1, 0, QUARTER), (1, QUARTER, HALF))):
+                product(m, part, *piece)
+                empty(copy, m, part, *piece)
+            store_row(m, part)
 
         def row(m, part, first_copy=on_scalar, second_copy=on_scalar):
             product(m, part, 0)
@@ -313,9 +322,10 @@ def tile_hybrid_beamforming_precoder_s4_kernel(
 
         load_x(0)
         load_gain()
-        load_scales(d_scales_raw, dig_scales, 0, PHASES * CHAINS)
+        load_scales(x_scales[0], sym_scales, 0, HALF, (0,))
+        load_scales(d_scales_raw, dig_scales, 0, PHASES * CHAINS, (0, 1, 2, 3,))
         load_d(U)
-        load_scales(x_scales[0], sym_scales, 0, HALF)
+        load_scales(x_scales[0], sym_scales, 0, HALF, (1, 2, 3,))
         load_d(V)
         load_w(0)
         load_w(1)
@@ -326,10 +336,11 @@ def tile_hybrid_beamforming_precoder_s4_kernel(
         load_w(3)
         load_w(4)
         load_w(5)
-        load_x(3)
         sort_gain()
         deal_scales(U, 0)
         turn_gain()
+        warm_up(2, BANKS - 3)
+        load_x(3)
         deal_scales(U, 1)
         deal_codes(on_vector, U, 0)
         deal_codes(on_scalar, U, 2)
@@ -363,11 +374,12 @@ def tile_hybrid_beamforming_precoder_s4_kernel(
         stage_one(U, 2)
         stage_one(V, 2)
         pack_w(on_scalar, "b", 1, 448, HALF)
-        pack_w(on_vector, "c", 1, 0, 512)
+        pack_w(on_vector, "c", 1)
         pack_w(on_vector, "b", 1, 0, 256)
         quantise_w("c", 1)
         pack_w(on_vector, "b", 1, 256, 448)
-        quantise_w("b", 1)
+        quantise_w("b", 1, 0, 256)
+        quantise_w("b", 1, 256, 512)
         for part in (IM, RE):
             for k in ("c", "b"):
                 for m in range(EARLY):

@@ -29,9 +29,9 @@ RE, IM = 0, 1
 BANKS = 8
 BLOCKS = SAMPLES // P
 EARLY = 2
-SHARE = 320
-SLIP = 64
-WARM_UP = 3
+SHARE = 352
+SLIP = 96
+WARM_UP = 4
 LOWER = 4
 FROM_BANK = (0,)
 LATE = 6
@@ -105,7 +105,6 @@ def tile_hybrid_beamforming_precoder_s4_kernel(
             line.remove(number)
             return number, psum.tile([P, HALF], F32, name="bank%d" % number)
 
-        nc.vector.memset(flat(x_scales[0], I32), 0)
         nc.vector.memset(flat(d_scales_raw, I32), 0)
         nc.vector.memset(flat(x_codes[-1], I32), 0)
         def warm_up(passes, number):
@@ -122,6 +121,7 @@ def tile_hybrid_beamforming_precoder_s4_kernel(
                 )
 
         warm_up(WARM_UP, BANKS - 1)
+        nc.vector.memset(flat(x_scales[0], I32), 0)
         nc.vector.memset(flat(x_scales[1], I32), 0)
         nc.vector.memset(gain_sorted[:], 0.0)
         nc.vector.memset(identity[:], 0.0)
@@ -322,11 +322,10 @@ def tile_hybrid_beamforming_precoder_s4_kernel(
 
         load_x(0)
         load_gain()
-        load_scales(x_scales[0], sym_scales, 0, HALF, (0,))
         load_scales(d_scales_raw, dig_scales, 0, PHASES * CHAINS, (0, 1, 2, 3,))
         load_d(U)
-        load_scales(x_scales[0], sym_scales, 0, HALF, (1, 2, 3,))
         load_d(V)
+        load_scales(x_scales[0], sym_scales, 0, HALF, (0, 1, 2, 3,))
         load_w(0)
         load_w(1)
         load_x(1)
@@ -373,11 +372,11 @@ def tile_hybrid_beamforming_precoder_s4_kernel(
         quantise_uv(0, MINUS_V)
         stage_one(U, 2)
         stage_one(V, 2)
-        pack_w(on_scalar, "b", 1, 448, HALF)
+        pack_w(on_scalar, "b", 1, 480, HALF)
         pack_w(on_vector, "c", 1)
         pack_w(on_vector, "b", 1, 0, 256)
         quantise_w("c", 1)
-        pack_w(on_vector, "b", 1, 256, 448)
+        pack_w(on_vector, "b", 1, 256, 480)
         quantise_w("b", 1, 0, 256)
         quantise_w("b", 1, 256, 512)
         for part in (IM, RE):

@@ -62,7 +62,7 @@ def tile_hybrid_beamforming_precoder_s4_kernel(
         d_raw = {s: tile([P, GROUPS, 2 * CHAINS], U8, "d_raw%d" % s) for s in (U, V)}
         d_scales_raw = tile([P, GROUPS, PHASES * CHAINS], U8, "d_scales_raw")
         d_codes = {s: [tile([P, GROUPS, 2 * P], U8, "d_codes%d%d" % (s, t)) for t in range(SLOTS)] for s in (U, V)}
-        d_scales = {s: [shifted(2 * GROUPS, P, U8, "d_scales%d%d" % (s, pair), 64) for pair in range(2)] for s in (U, V)}
+        d_scales = {s: [shifted(2 * GROUPS, 2 * P, U8, "d_scales%d%d" % (s, pair), 64)[:, :, 0:P] for pair in range(2)] for s in (U, V)}
         gain_rows = tile([PHASES, CHAINS], BF16, "gain_rows")
         gain_sorted = tile([P, CHAINS], BF16, "gain_sorted")
         identity = tile([P, P], BF16, "identity")

from contextlib import ExitStack

import concourse.mybir as mybir
from concourse.masks import make_identity

SAMPLES, STREAMS, CHAINS, ANTENNAS = 1024, 1024, 512, 1024
FLOPS = 2 * SAMPLES * STREAMS * 2 * CHAINS + 4 * 2 * SAMPLES * CHAINS * ANTENNAS

F32 = mybir.dt.float32
BF16 = mybir.dt.bfloat16
I32 = mybir.dt.int32
U32 = mybir.dt.uint32
U16 = mybir.dt.uint16
U8 = mybir.dt.uint8
FP4X4 = mybir.dt.float4_e2m1fn_x4
FP8X4 = mybir.dt.float8_e4m3fn_x4
TANH = mybir.ActivationFunctionType.Tanh
MULT = mybir.AluOpType.mult
ADD = mybir.AluOpType.add

P = 128
SLOTS = 4
GROUPS = STREAMS // 512
HALF = 512
QUARTER = 256
PHASES = 2
U, V, MINUS_V = 0, 1, 2
RE, IM = 0, 1
BANKS = 8
BLOCKS = SAMPLES // P
EARLY = 2
SHARE = 352
SLIP = 96
WARM_UP = 4
LOWER = 4
FROM_BANK = (0,)
LATE = 6
W_LOADS = [("c", 0, 0, 256), ("c", 0, 256, HALF), ("b", 0, 0, SHARE), ("b", 0, SHARE, HALF), ("c", 1, 0, HALF), ("b", 1, 0, HALF)]
BATCHES = [(0, 2), (2, 1), (3, 1), (4, 1), (5, 1), (6, 1), (7, 1)]


def tile_hybrid_beamforming_precoder_s4_kernel(
    tc, sym_words, sym_scales, dig_words, dig_scales, gain, cosw, sinw, out_0, out_1
):
    nc = tc.nc
    with ExitStack() as ctx:
        keep = ctx.enter_context(tc.tile_pool(name="keep", bufs=1))
        psum = ctx.enter_context(tc.psum_pool(name="psum", bufs=1))

        def tile(shape, dtype, name):
            return keep.tile(shape, dtype, name=name, align_bytes=256)

        def shifted(rows, width, dtype, name, shift):
            whole = tile([P, shift + rows * width], dtype, name)
            return whole[:, shift:].rearrange("p (r n) -> p r n", r=rows)

        def flat(t, dtype):
            return t[:].rearrange("p a n -> p (a n)").bitcast(dtype)

        x_codes = [shifted(GROUPS, 2 * QUARTER, U8, "x_codes%d" % q, 128) for q in range(4)]
        x_scales = [shifted(GROUPS, HALF, U8, "x_scales%d" % half, 192) for half in range(2)]
        d_raw = {s: tile([P, GROUPS, 2 * CHAINS], U8, "d_raw%d" % s) for s in (U, V)}
        d_scales_raw = tile([P, GROUPS, PHASES * CHAINS], U8, "d_scales_raw")
        d_codes = {s: [tile([P, GROUPS, 2 * P], U8, "d_codes%d%d" % (s, t)) for t in range(SLOTS)] for s in (U, V)}
        d_scales = {s: [shifted(2 * GROUPS, 2 * P, U8, "d_scales%d%d" % (s, pair), 64)[:, :, 0:P] for pair in range(2)] for s in (U, V)}
        gain_rows = tile([PHASES, CHAINS], BF16, "gain_rows")
        gain_sorted = tile([P, CHAINS], BF16, "gain_sorted")
        identity = tile([P, P], BF16, "identity")
        gain_cols = tile([P, PHASES, SLOTS], F32, "gain_cols")

        halves = [(k, nh) for k in ("c", "b") for nh in range(2)]
        w_raw = {(k, nh, first): tile([P, SLOTS, last - first], BF16, "raw_%s%d%d" % (k, nh, first)) for k, nh, first, last in W_LOADS}

        def raw(k, nh, first, last):
            loaded_from = max(f for kk, hh, f in w_raw if (kk, hh) == (k, nh) and f <= first)
            return w_raw[k, nh, loaded_from][:, :, first - loaded_from : last - loaded_from]

        packed_first = tile([P, SLOTS * (HALF + SLIP)], BF16, "packed_first")
        w_packed = {(k, 1): tile([P, SLOTS * HALF], BF16, "packed_%s" % k) for k in ("c", "b")}
        w_packed["b", 0] = packed_first[:, 0 : SLOTS * HALF]
        w_packed["c", 0] = packed_first[:, SLOTS * SLIP :]
        w_codes = {(k, nh): shifted(1, HALF, U32, "codes_%s%d" % (k, nh), 32)[:, 0, :] for k, nh in halves}
        w_scales = {(k, nh): shifted(1, HALF, U8, "scales_%s%d" % (k, nh), 192)[:, 0, :] for k, nh in halves}

        tanh_h = {(s, q): tile([P, 2, 2 * QUARTER], F32, "tanh_%d%d" % (s, q)) for s in (U, V) for q in range(4)}
        batches = dict(BATCHES)
        uv_packed = {m: tile([P, 3, blocks * SLOTS * P], BF16, "uv_packed%d" % m) for m, blocks in batches.items()}
        batch_codes = {m: tile([P, 3, blocks * P], U32, "uv_codes%d" % m) for m, blocks in batches.items()}
        batch_scales = {m: shifted(3, blocks * P, U8, "uv_scales%d" % m, 64) for m, blocks in batches.items()}
        places = [(m, i) for m, blocks in batches.items() for i in range(blocks)]
        uv_codes = {m + i: batch_codes[m][:, :, P * i : P * (i + 1)] for m, i in places}
        uv_scales = {m + i: batch_scales[m][:, :, P * i : P * (i + 1)] for m, i in places}
        results = {(m, part): [tile([P, HALF], F32, "y%d%d%d" % (m, part, nh)) for nh in range(2)] for m in range(EARLY) for part in (RE, IM)}
        rows = {(m, part): tile([P, ANTENNAS], F32, "y%d%d" % (m, part)) for m in range(EARLY, BLOCKS) for part in (RE, IM)}

        def result(m, part, nh):
            return results[m, part][nh][:] if m < EARLY else rows[m, part][:, HALF * nh : HALF * (nh + 1)]

        ctx.enter_context(tc.manual_schedule())

        line = list(range(0, BANKS, 2)) + list(range(1, BANKS, 2))

        def take_bank():
            number = line[0]
            line.remove(number)
            return number, psum.tile([P, HALF], F32, name="bank%d" % number)

        nc.vector.memset(flat(d_scales_raw, I32), 0)
        nc.vector.memset(flat(x_codes[-1], I32), 0)
        def warm_up(passes, number):
            warm_bank = psum.tile([P, HALF], F32, name="bank%d" % number)
            for unused in range(passes):
                nc.tensor.matmul_mx(
                    out=warm_bank[:],
                    lhsT=x_codes[-1][:, 0, 0 : 2 * P].bitcast(FP4X4),
                    lhsT_scale=x_codes[-1][:, 0, 0:P],
                    rhs=flat(x_codes[-1], U8).bitcast(FP4X4),
                    rhs_scale=x_codes[-1][:, 0, :],
                    start=True,
                    stop=True,
                )

        warm_up(WARM_UP, BANKS - 1)
        nc.vector.memset(flat(x_scales[0], I32), 0)
        nc.vector.memset(flat(x_scales[1], I32), 0)
        nc.vector.memset(gain_sorted[:], 0.0)
        nc.vector.memset(identity[:], 0.0)
        make_identity(nc, identity[:], nomemset=True)

        def load_codes(dst, src, first, last):
            by_partition = src.rearrange("g p x -> p g x")
            nc.sync.dma_start(out=dst[:].bitcast(I32), in_=by_partition[:, :, 2 * first : 2 * last].bitcast(I32))

        def load_x(q):
            load_codes(x_codes[q], sym_words, QUARTER * q, QUARTER * (q + 1))

        def load_d(s):
            load_codes(d_raw[s], dig_words, CHAINS * s, CHAINS * (s + 1))

        def load_scales(dst, src, first, last, rows=range(4)):
            for r in rows:
                nc.sync.dma_start(
                    out=dst[r:P:32, :, :].bitcast(I32),
                    in_=src[:, r:16:4, first:last].rearrange("g j n -> j g n").bitcast(I32),
                )

        def load_gain():
            nc.sync.dma_start(out=gain_rows[:], in_=gain.rearrange("(s n) -> s n", s=PHASES))

        def load_w(number):
            k, nh, first, last = W_LOADS[number]
            w = (cosw if k == "c" else sinw).rearrange("(p t) n -> p t n", t=SLOTS)
            nc.sync.dma_start(out=w_raw[k, nh, first][:], in_=w[:, :, HALF * nh + first : HALF * nh + last])

        def deal_scales(s, pair):
            nc.vector.tensor_copy(
                out=d_scales[s][pair].rearrange("p (j g) m -> p j g m", j=2),
                in_=d_scales_raw[:].rearrange("p g (s m u j) -> p s u j g m", s=PHASES, u=2, j=2)[:, s, pair],
            )

        def deal_codes(copy, s, t):
            copy(
                out=flat(d_codes[s][t], U16).rearrange("p (g m) -> p g m", g=GROUPS),
                in_=flat(d_raw[s], U16).rearrange("p (g m t) -> p t g m", g=GROUPS, t=SLOTS)[:, t],
            )

        gain_number, gain_bank = BANKS - 1, psum.tile([P, SLOTS * P], BF16, name="bank7")
        line.remove(gain_number)
        gain_in_bank = gain_bank[:].rearrange("p (t s) -> p s t", t=SLOTS)

        def sort_gain():
            nc.vector.tensor_copy(
                out=gain_sorted[0:PHASES, :].rearrange("p (t m) -> p t m", t=SLOTS),
                in_=gain_rows[:].rearrange("p (m t) -> p t m", t=SLOTS),
            )

        def turn_gain():
            for t in range(SLOTS):
                nc.tensor.transpose(gain_bank[:, P * t : P * (t + 1)], gain_sorted[:, P * t : P * (t + 1)], identity[:])

        def gather_gain():
            nc.scalar.copy(out=gain_cols[:], in_=gain_in_bank[:, 0:PHASES, :])

        held = {}

        def chains(s, q, pairs=(0, 1)):
            for pair in pairs:
                held[s, q, pair] = take_bank()
                for j in range(2):
                    for g in range(GROUPS):
                        nc.tensor.matmul_mx(
                            out=held[s, q, pair][1][:, QUARTER * j : QUARTER * (j + 1)],
                            lhsT=d_codes[s][2 * pair + j][:, g, :].bitcast(FP4X4),
                            lhsT_scale=d_scales[s][pair][:, GROUPS * j + g, :],
                            rhs=x_codes[q][:, g, :].bitcast(FP4X4),
                            rhs_scale=x_scales[q // 2][:, g, QUARTER * (q % 2) : QUARTER * (q % 2 + 1)],
                            start=(g == 0),
                            stop=(g == GROUPS - 1),
                        )

        def limit(s, q, pairs=(0, 1)):
            for pair in pairs:
                number, bank = held[s, q, pair]
                nc.scalar.activation(
                    out=tanh_h[s, q][:, pair, :].rearrange("p (n j) -> p n j", j=2),
                    in_=bank[:].rearrange("p (j n) -> p n j", j=2),
                    func=TANH,
                )
                line.append(number)

        def stage_one(s, q, pairs=(0, 1)):
            chains(s, q, pairs)
            limit(s, q, pairs)

        def pack_w(copy, k, nh, first=0, last=HALF):
            copy(
                out=w_packed[k, nh][:, SLOTS * first : SLOTS * last].rearrange("p (c i t) -> p c t i", t=SLOTS, i=4),
                in_=raw(k, nh, first, last).rearrange("p t (c i) -> p c t i", i=4),
            )

        def pack_on_gpsimd(k, nh, first, last):
            nc.gpsimd.tensor_scalar(
                out=w_packed[k, nh][:, SLOTS * first : SLOTS * last].rearrange("p (n t) -> p n t", t=SLOTS),
                in0=raw(k, nh, first, last).rearrange("p t n -> p n t"),
                scalar1=1.0,
                scalar2=0.0,
                op0=MULT,
                op1=ADD,
            )

        def quantise_w(k, nh, first=0, last=HALF):
            nc.vector.quantize_mx(
                out=w_codes[k, nh][:, first:last].bitcast(FP8X4),
                scales=w_scales[k, nh][:, first:last],
                in_=w_packed[k, nh][:, SLOTS * first : SLOTS * last],
            )

        def times_gain(s, m):
            n = P * (m % 2)
            samples = P * batches[m]
            gains = gain_in_bank if m in FROM_BANK else gain_cols
            nc.vector.tensor_tensor(
                out=uv_packed[m][:, s, :].rearrange("p (n u j) -> p n u j", u=2, j=2),
                in0=tanh_h[s, m // 2][:].rearrange("p u (n j) -> p n u j", j=2)[:, n : n + samples],
                in1=gains[:, s, :].rearrange("p (u j) -> p u j", j=2).unsqueeze(1).to_broadcast([P, samples, 2, 2]),
                op=MULT,
            )

        def negate_v(m):
            nc.vector.tensor_scalar(out=uv_packed[m][:, MINUS_V, :], in0=uv_packed[m][:, V, :], scalar1=-1.0, scalar2=None, op0=MULT)

        def quantise_uv(m, s):
            nc.vector.quantize_mx(out=batch_codes[m][:, s, :].bitcast(FP8X4), scales=batch_scales[m][LOWER:, s, :], in_=uv_packed[m][:, s, :])

        def quantise_both(m):
            nc.vector.quantize_mx(
                out=batch_codes[m][:, 0:2, :].rearrange("p s n -> p (s n)").bitcast(FP8X4),
                scales=batch_scales[m][:, 0:2, :].rearrange("p s n -> p (s n)"),
                in_=uv_packed[m][:, 0:2, :].rearrange("p s n -> p (s n)"),
            )

        def gains(m):
            times_gain(V, m)
            times_gain(U, m)

        def codes(m):
            negate_v(m)
            for s in (V, U, MINUS_V):
                quantise_uv(m, s)

        def prepare(m):
            gains(m)
            codes(m)

        passes = {(RE, "c"): U, (RE, "b"): MINUS_V, (IM, "c"): V, (IM, "b"): U}
        sums = {}

        def multiply(m, part, nh, k, first=0, last=HALF):
            opens = (m, part, nh, first) not in sums
            if opens:
                sums[m, part, nh, first] = take_bank()
            s = passes[part, k]
            nc.tensor.matmul_mx(
                out=sums[m, part, nh, first][1][:, 0 : last - first],
                lhsT=uv_codes[m][:, s, :].bitcast(FP8X4),
                lhsT_scale=uv_scales[m][LOWER:, s, :],
                rhs=w_codes[k, nh][:, first:last].bitcast(FP8X4),
                rhs_scale=w_scales[k, nh][:, first:last],
                start=opens,
                stop=not opens,
            )

        on_scalar, on_vector = nc.scalar.copy, nc.vector.tensor_copy

        def empty(copy, m, part, nh, first=0, last=HALF):
            number, bank = sums[m, part, nh, first]
            copy(out=result(m, part, nh)[:, first:last], in_=bank[:, 0 : last - first])
            line.append(number)

        def store_half(m, part, nh):
            nc.sync.dma_start(out=(out_0, out_1)[part][P * m : P * (m + 1), HALF * nh : HALF * (nh + 1)], in_=result(m, part, nh))

        def store_row(m, part):
            nc.sync.dma_start(out=(out_0, out_1)[part][P * m : P * (m + 1), :], in_=rows[m, part][:])

        def product(m, part, nh, first=0, last=HALF):
            for k in ("b", "c") if (nh == 0) == (part == IM and m >= LATE) else ("c", "b"):
                multiply(m, part, nh, k, first, last)

        def split_row(m, part, copies):
            for copy, piece in zip(copies, ((0, 0, HALF), (1, 0, QUARTER), (1, QUARTER, HALF))):
                product(m, part, *piece)
                empty(copy, m, part, *piece)
            store_row(m, part)

        def row(m, part, first_copy=on_scalar, second_copy=on_scalar):
            product(m, part, 0)
            empty(first_copy, m, part, 0)
            product(m, part, 1)
            empty(second_copy, m, part, 1)
            store_row(m, part)

        load_x(0)
        load_gain()
        load_scales(d_scales_raw, dig_scales, 0, PHASES * CHAINS, (0, 1, 2, 3,))
        load_d(U)
        load_d(V)
        load_scales(x_scales[0], sym_scales, 0, HALF, (0, 1, 2, 3,))
        load_w(0)
        load_w(1)
        load_x(1)
        load_w(2)
        load_scales(x_scales[1], sym_scales, HALF, SAMPLES)
        load_x(2)
        load_w(3)
        load_w(4)
        load_w(5)
        sort_gain()
        deal_scales(U, 0)
        turn_gain()
        warm_up(2, BANKS - 3)
        load_x(3)
        deal_scales(U, 1)
        deal_codes(on_vector, U, 0)
        deal_codes(on_scalar, U, 2)
        deal_codes(on_vector, U, 1)
        deal_codes(on_scalar, U, 3)
        gather_gain()
        deal_scales(V, 0)
        deal_scales(V, 1)
        stage_one(U, 0)
        for t in range(SLOTS):
            deal_codes(on_vector, V, t)
        stage_one(V, 0)
        for first, last in ((0, 256), (256, HALF)):
            pack_w(on_vector, "c", 0, first, last)
        for first, last in ((0, 256), (256, HALF)):
            quantise_w("c", 0, first, last)
        pack_on_gpsimd("b", 0, 0, SHARE)
        stage_one(U, 1)
        chains(V, 1)
        limit(V, 1, (0,))
        pack_w(on_scalar, "b", 0, SHARE, HALF)
        limit(V, 1, (1,))
        times_gain(U, 0)
        times_gain(V, 0)
        line.append(gain_number)
        quantise_uv(0, U)
        negate_v(0)
        quantise_uv(0, V)
        quantise_w("b", 0)
        quantise_uv(0, MINUS_V)
        stage_one(U, 2)
        stage_one(V, 2)
        pack_w(on_scalar, "b", 1, 480, HALF)
        pack_w(on_vector, "c", 1)
        pack_w(on_vector, "b", 1, 0, 256)
        quantise_w("c", 1)
        pack_w(on_vector, "b", 1, 256, 480)
        quantise_w("b", 1, 0, 256)
        quantise_w("b", 1, 256, 512)
        for part in (IM, RE):
            for k in ("c", "b"):
                for m in range(EARLY):
                    multiply(m, part, 0, k)
            for m in range(EARLY):
                empty(on_scalar, m, part, 0)
                store_half(m, part, 0)
        stage_one(U, 3)
        for k in ("c", "b"):
            for part in (IM, RE):
                for m in range(EARLY):
                    multiply(m, part, 1, k)
        gains(2)
        codes(2)
        for part in (IM, RE):
            for m in range(EARLY):
                empty(on_scalar, m, part, 1)
                store_half(m, part, 1)
        chains(V, 3, (0,))
        prepare(3)
        row(2, IM)
        row(2, RE)
        prepare(4)
        row(3, IM)
        gains(5)
        row(3, RE, on_vector)
        codes(5)
        row(4, IM)
        chains(V, 3, (1,))
        limit(V, 3)
        for m in (6, 7):
            times_gain(U, m)
        quantise_uv(6, U)
        row(4, RE, on_vector)
        times_gain(V, 6)
        quantise_uv(7, U)
        quantise_uv(6, V)
        times_gain(V, 7)
        negate_v(6)
        quantise_uv(7, V)
        quantise_uv(6, MINUS_V)
        negate_v(7)
        row(5, IM)
        row(5, RE)
        row(6, IM, on_vector)
        quantise_uv(7, MINUS_V)
        row(6, RE, on_vector)
        row(7, IM, on_vector)
        row(7, RE, on_vector)
